import numpy as np
import ml_dtypes


def mxq(x, axis, fmt="e4m3"):
    dtype, down = {"e4m3": (ml_dtypes.float8_e4m3fn, 7), "e5m2": (ml_dtypes.float8_e5m2, 14)}[fmt]
    v = np.moveaxis(np.asarray(x, np.float32).astype(ml_dtypes.bfloat16).astype(np.float64), axis, -1)
    blocks = v.reshape(v.shape[:-1] + (-1, 32))
    amax = np.abs(blocks).max(-1, keepdims=True)
    byte = np.maximum(np.where(amax > 0, np.frexp(amax)[1] - 1 + 127, 0) - down, 1)
    scale = np.exp2(byte - 127.0)
    codes = (blocks / scale).astype(np.float32).astype(dtype).astype(np.float64)
    return np.moveaxis((codes * scale).reshape(v.shape), -1, axis)


WIDE = False


def mx_kscale(k):
    if not WIDE:
        return np.ones(k)
    levels = np.array([10, -10, 5, -5, 0])
    if k % 512:
        return np.exp2(np.random.permutation(np.resize(levels, k // 32))).repeat(32)
    a = np.empty((k // 512, 16))
    for p in range(k // 512):
        a[p, :8] = np.random.permutation(np.resize(levels, 8))
        for g in range(8):
            far = levels[np.abs(levels - a[p, g]) >= 10]
            a[p, g + 8] = far[np.random.randint(len(far))]
    return np.exp2(a.ravel()).repeat(32)


BF16 = ml_dtypes.bfloat16


def bf(x):
    return np.asarray(x, np.float32).astype(BF16)


def f64(x):
    return np.asarray(x).astype(np.float64)


E2M1 = np.array([0.0, 0.5, 1.0, 1.5, 2.0, 3.0, 4.0, 6.0, -0.0, -0.5, -1.0, -1.5, -2.0, -3.0, -4.0, -6.0])


def pack_weight(w, fmt):
    k, n = w.shape
    w = f64(bf(w)).reshape(k // 32, 32, n)
    amax = np.abs(w).max(1)
    if fmt == "e4m3":
        byte = np.frexp(amax)[1] - 1 + 127 - 7
    else:
        mant, ex = np.frexp(amax / 6.0)
        byte = np.where(mant > 0.5, ex, ex - 1) + 127
    byte = np.clip(np.where(amax > 0, byte, 1), 1, 254)
    scaled = (w * np.exp2(127.0 - byte)[:, None, :]).reshape(k, n).astype(np.float32)
    by_word = np.ascontiguousarray(scaled.reshape(k // 512, 128, 4, n).transpose(0, 1, 3, 2))
    if fmt == "e4m3":
        words = by_word.astype(ml_dtypes.float8_e4m3fn).view(np.uint8)
    else:
        c = by_word.astype(ml_dtypes.float4_e2m1fn).view(np.uint8) & 0xF
        words = c[..., 0::2] | (c[..., 1::2] << 4)
    return np.ascontiguousarray(words), np.ascontiguousarray(byte.astype(np.uint8).reshape(k // 512, 16, n))


def unpack_weight(words, scales, fmt):
    g, p, n, _ = words.shape
    if fmt == "e4m3":
        vals = np.ascontiguousarray(words).view(ml_dtypes.float8_e4m3fn).astype(np.float64)
    else:
        nib = np.empty((g, p, n, 4), np.uint8)
        nib[..., 0::2] = words & 0xF
        nib[..., 1::2] = words >> 4
        vals = E2M1[nib]
    vals = vals * np.repeat(np.exp2(scales.astype(np.float64) - 127.0), 8, axis=1)[..., None]
    return vals.transpose(0, 1, 3, 2).reshape(g * 512, n)
def pack4(w):
    words, scales = pack_weight(w, "e2m1")
    return words.reshape(words.shape[0], 128, -1), scales


def unpack4(words, scales):
    return unpack_weight(words.reshape(words.shape[0], 128, -1, 2), scales, "e2m1")


M, N, D = 2048, 1024, 1024

TEMPERATURE = 2.0
BIAS_MEAN = -1.0


def draw0():
    s = mx_kscale(D)
    t = mx_kscale(M)
    a = np.random.standard_normal((M, D))
    c = TEMPERATURE * np.random.standard_normal((N, D)) / np.sqrt(D)
    bank_words, bank_scales = pack4(a / np.sqrt(M) / t[:, None])
    return {"audio": bf(a * s),
            "captions": bf(c / s),
            "bias": bf(BIAS_MEAN + 0.5 * np.random.standard_normal(N)),
            "clip_weight": bf((1 + 0.1 * np.random.standard_normal(M)) * t),
            "bank_words": bank_words,
            "bank_scales": bank_scales}


def core(audio, captions, bias, clip_weight, bank_words, bank_scales):
    qa = mxq(f64(audio), 1, "e4m3")
    qc = mxq(f64(captions), 1, "e4m3")
    logits = (qa @ qc.T) + f64(bias)
    prob = 1.0 / (1.0 + np.exp(-logits))
    resid = prob * f64(clip_weight)[:, None]
    qr = mxq(resid, 0, "e4m3")
    bank = unpack4(bank_words, bank_scales)
    return qr.T @ bank


def e4m3fn_bytes(y):
    return np.clip(np.asarray(y, np.float64), -448.0, 448.0).astype(np.float32).astype(ml_dtypes.float8_e4m3fn).view(np.uint8)


def e4m3fn_values(b):
    return np.asarray(b, np.uint8).view(ml_dtypes.float8_e4m3fn).astype(np.float64)


def setup_inputs():
    d = draw0()
    x0 = np.asarray(d['audio']).astype(np.float64)
    s = (np.max(np.abs(x0), axis=(0,), keepdims=True) / 448.0).astype(np.float32)
    out = {}
    for k, v in d.items():
        if k == 'audio':
            out['audio_bytes'] = e4m3fn_bytes(x0 / s.astype(np.float64))
            out['audio_scale'] = s
        else:
            out[k] = v
    return out


def reference(audio_bytes, audio_scale, captions, bias, clip_weight, bank_words, bank_scales):
    return core(e4m3fn_values(audio_bytes) * audio_scale.astype(np.float64), captions, bias, clip_weight, bank_words, bank_scales)

@@ -1,0 +1,400 @@
+from contextlib import ExitStack
+
+import concourse.mybir as mybir
+from concourse.masks import make_identity
+
+F32 = mybir.dt.float32
+BF16 = mybir.dt.bfloat16
+U32 = mybir.dt.uint32
+I32 = mybir.dt.int32
+U8 = mybir.dt.uint8
+FP8 = mybir.dt.float8_e4m3fn
+FP8X4 = mybir.dt.float8_e4m3fn_x4
+FP4X4 = mybir.dt.float4_e2m1fn_x4
+MULT = mybir.AluOpType.mult
+SIGMOID = mybir.ActivationFunctionType.Sigmoid
+
+CLIPS, CAPS, FEATS = 2048, 1024, 1024
+P = 128
+CHUNK = 512
+CHUNKS = CLIPS // CHUNK
+PASSES = FEATS // CHUNK
+CAP_TILES = CAPS // P
+
+SORT = 3
+
+FLOPS = 2 * 2 * CLIPS * CAPS * FEATS
+
+
+def tile_siglip_negative_caption_gradient_s13_kernel(
+    tc, audio_bytes, audio_scale, captions, bias, clip_weight, bank_words, bank_scales, out
+):
+    nc = tc.nc
+    with ExitStack() as ctx:
+        keep = ctx.enter_context(tc.tile_pool(name="keep", bufs=1))
+        work = ctx.enter_context(tc.tile_pool(name="work", bufs=3))
+        psum = ctx.enter_context(tc.psum_pool(name="psum", bufs=2))
+
+        scale_all = keep.tile([P, FEATS], F32, name="scale_all")
+        raw = [keep.tile([P, 4 * FEATS], U8, name="raw%d" % g) for g in range(CHUNKS)]
+        cap = [keep.tile([P, FEATS], BF16, name="cap%d" % t) for t in range(CAP_TILES)]
+        scale_cols = keep.tile([P, PASSES, 4], F32, name="scale_cols")
+        weight_all = keep.tile([P, CLIPS], BF16, name="weight_all")
+        weight_ord = keep.tile([P, CLIPS], BF16, name="weight_ord")
+        bias_rows = keep.tile([P, P], BF16, name="bias_rows")
+        bias_cols = keep.tile([P, CAP_TILES], F32, name="bias_cols")
+        bank = keep.tile([P, CHUNKS, 2 * FEATS], U8, align_bytes=64, name="bank")
+        bank_sc = keep.tile([P, CHUNKS, FEATS], U8, align_bytes=64, name="bank_sc")
+        ident = keep.tile([P, P], F32, name="ident")
+        ident_b = keep.tile([P, P], BF16, name="ident_b")
+        dummy = keep.tile([P, 1], F32, name="dummy")
+        aud_codes = keep.tile([P, CHUNKS, PASSES, CHUNK], U32, align_bytes=64, name="aud_codes")
+        aud_planes = keep.tile([P, CHUNKS, PASSES, CHUNK], U8, align_bytes=64, name="aud_planes")
+        cap_codes = keep.tile([P, CAP_TILES, PASSES, P], U32, align_bytes=64, name="cap_codes")
+        cap_planes = keep.tile([P, CAP_TILES, PASSES, P], U8, align_bytes=64, name="cap_planes")
+        r_codes = keep.tile([P, CAP_TILES, CHUNKS, P], U32, align_bytes=64, name="r_codes")
+        r_planes = keep.tile([P, CAP_TILES, CHUNKS, P], U8, align_bytes=64, name="r_planes")
+
+        nc.vector.memset(dummy[:], 0.0)
+        nc.vector.memset(bias_rows[:], 0.0)
+        nc.scalar.activation(out=dummy[:], in_=dummy[:], func=SIGMOID)
+        make_identity(nc, ident[:])
+        make_identity(nc, ident_b[:])
+        nc.gpsimd.memset(bank_sc[:].rearrange("p g d -> p (g d)").bitcast(U32), 0)
+
+        aud_view = audio_bytes.rearrange("(g q s) d -> g q (s d)", q=P, s=4)
+        cap_view = captions.rearrange("(t p) d -> t p d", p=P)
+        half = 2 * FEATS
+        def load_cap(t):
+            nc.sync.dma_start(out=cap[t][:], in_=cap_view[t])
+
+        nc.sync.dma_start(out=scale_cols[:], in_=audio_scale.rearrange("o (h n m) -> n (o h) m", h=PASSES, m=4))
+        nc.sync.dma_start(out=raw[0][:, :half], in_=aud_view[0][:, :half])
+        load_cap(0)
+        nc.sync.dma_start(out=raw[0][:, half:], in_=aud_view[0][:, half:])
+        nc.sync.dma_start(out=bias_rows[0:CAP_TILES, :], in_=bias.rearrange("(t p) -> t p", p=P))
+        load_cap(1)
+        load_cap(2)
+        load_cap(3)
+        for t in range(4, CAP_TILES):
+            load_cap(t)
+        nc.sync.dma_start(out=raw[1][:], in_=aud_view[1])
+        nc.sync.dma_start(out=raw[2][:], in_=aud_view[2])
+        nc.sync.dma_start(out=raw[3][:], in_=aud_view[3])
+        nc.sync.dma_start(out=weight_all[:], in_=clip_weight.partition_broadcast(P))
+        for q in range(4):
+            nc.sync.dma_start(
+                out=bank_sc[32 * q : 32 * q + 4, :, :].bitcast(I32),
+                in_=bank_scales[:, 4 * q : 4 * q + 4, :].rearrange("g r n -> r g n").bitcast(I32),
+            )
+        nc.sync.dma_start(out=bank[:], in_=bank_words.rearrange("g p n -> p g n"))
+
+        def spread_scale(h):
+            xt = psum.tile([P, 4, P], F32, tag="sum", name="spread", bufs=4)
+            for m in range(4):
+                nc.tensor.transpose(xt[:, m, :], scale_cols[:, h, m : m + 1].to_broadcast([P, P]), ident[:])
+            nc.scalar.copy(
+                out=scale_all[:, CHUNK * h : CHUNK * (h + 1)].rearrange("p (n m) -> p n m", m=4),
+                in_=xt[:].rearrange("p m n -> p n m"),
+            )
+
+        def cap_turn(t):
+            xt = psum.tile([P, PASSES, 2, P], F32, tag="turn", name="xt", bufs=4)
+            words = cap[t][:].bitcast(F32)
+            for h in range(PASSES):
+                for u in range(2):
+                    nc.tensor.transpose(xt[:, h, u, :], words[:, 256 * h + u : 256 * (h + 1) : 2], ident[:])
+            grouped = work.tile([P, 1024], BF16, align_bytes=64, tag="grouped", name="cap_grouped", bufs=7)
+            nc.scalar.copy(
+                out=grouped[:].bitcast(F32).rearrange("p (h j u) -> p h j u", h=PASSES, u=2),
+                in_=xt[:].rearrange("p h u j -> p h j u"),
+            )
+            return grouped
+
+        def cap_quant(t, grouped):
+            nc.vector.quantize_mx(
+                out=cap_codes[:, t, :, :].rearrange("p h j -> p (h j)").bitcast(FP8X4),
+                scales=cap_planes[:, t, :, :].rearrange("p h j -> p (h j)"),
+                in_=grouped[:],
+            )
+
+        audio = {}
+
+        def widen(g, s, first=0, end=FEATS):
+            if first == 0:
+                audio[g, s] = work.tile([P, FEATS], BF16, align_bytes=64, tag="audio", name="audio", bufs=6)
+            nc.vector.tensor_tensor(
+                out=audio[g, s][:, first:end],
+                in0=raw[g][:, s * FEATS + first : s * FEATS + end].bitcast(FP8),
+                in1=scale_all[:, first:end],
+                op=MULT,
+            )
+
+        def sort(g, s):
+            if g < SORT:
+                return
+            flat = work.tile([P, FEATS], BF16, align_bytes=64, tag="sorted", name="flat", bufs=4)
+            nc.vector.tensor_copy(
+                out=flat[:].bitcast(F32).rearrange("p (h u w) -> p h u w", h=PASSES, u=2),
+                in_=audio[g, s][:].bitcast(F32).rearrange("p (h w u) -> p h u w", h=PASSES, u=2),
+            )
+            audio[g, s] = flat
+
+        def aud_turn(g, top, halves=range(PASSES)):
+            res = []
+            for h in halves:
+                xt = psum.tile([P, 2, 2, P], F32, tag="turn", name="xt", bufs=4)
+                for u in range(2):
+                    for e in range(2):
+                        words = audio[g, 2 * top + e][:].bitcast(F32)
+                        if g < SORT:
+                            words = words[:, 256 * h + u : 256 * (h + 1) : 2]
+                        else:
+                            words = words[:, 256 * h + P * u : 256 * h + P * (u + 1)]
+                        nc.tensor.transpose(xt[:, u, e, :], words, ident[:])
+                grouped = work.tile([P, 1024], BF16, align_bytes=64, tag="grouped", name="aud_grouped", bufs=7)
+                nc.scalar.copy(
+                    out=grouped[:].bitcast(F32).rearrange("p (q e u) -> p q e u", e=2, u=2),
+                    in_=xt[:].rearrange("p u e q -> p q e u"),
+                )
+                res.append(grouped)
+            return res
+
+        def aud_quant(g, top, res):
+            for h in range(PASSES):
+                cols = slice(256 * top, 256 * (top + 1))
+                nc.vector.quantize_mx(
+                    out=aud_codes[:, g, h, cols].bitcast(FP8X4), scales=aud_planes[:, g, h, cols], in_=res[h][:]
+                )
+
+        sigs = {}
+        resids = {}
+
+        def logits(t, g):
+            pair = g // 2
+            if g % 2 == 0:
+                sigs[t, pair] = work.tile([P, 2, CHUNK], F32, tag="sig", name="sig", bufs=16)
+            acc = psum.tile([P, CHUNK], F32, tag="sum", name="acc", bufs=4)
+            for h in range(PASSES):
+                nc.tensor.matmul_mx(
+                    out=acc[:],
+                    lhsT=cap_codes[:, t, h, :].bitcast(FP8X4),
+                    lhsT_scale=cap_planes[:, t, h, :],
+                    rhs=aud_codes[:, g, h, :].bitcast(FP8X4),
+                    rhs_scale=aud_planes[:, g, h, :],
+                    start=(h == 0),
+                    stop=(h == PASSES - 1),
+                )
+            nc.scalar.activation(out=sigs[t, pair][:, g % 2, :], in_=acc[:], func=SIGMOID, bias=bias_cols[:, t : t + 1])
+
+        def weigh(t, pair):
+            resids[t, pair] = work.tile([P, 2, CHUNK], BF16, align_bytes=64, tag="resid", name="resid", bufs=10)
+            nc.vector.tensor_tensor(
+                out=resids[t, pair][:],
+                in0=sigs[t, pair][:],
+                in1=weight_ord[:, 2 * CHUNK * pair : 2 * CHUNK * (pair + 1)].rearrange("p (a c) -> p a c", a=2),
+                op=MULT,
+            )
+
+        def pair_turn(t, pair):
+            xt = psum.tile([P, 2, 2, P], F32, tag="turn", name="xt", bufs=4)
+            for a in range(2):
+                words = resids[t, pair][:, a, :].bitcast(F32)
+                for top in range(2):
+                    nc.tensor.transpose(xt[:, a, top, :], words[:, P * top : P * (top + 1)], ident[:])
+            grouped = work.tile([P, 1024], BF16, align_bytes=64, tag="grouped", name="r_grouped", bufs=7)
+            nc.scalar.copy(
+                out=grouped[:].bitcast(F32).rearrange("p (a j u) -> p a j u", a=2, u=2),
+                in_=xt[:].rearrange("p a u j -> p a j u"),
+            )
+            return grouped
+
+        def pair_quant(t, pair, grouped):
+            two = slice(2 * pair, 2 * pair + 2)
+            nc.vector.quantize_mx(
+                out=r_codes[:, t, two, :].rearrange("p a j -> p (a j)").bitcast(FP8X4),
+                scales=r_planes[:, t, two, :].rearrange("p a j -> p (a j)"),
+                in_=grouped[:],
+            )
+
+        sums = {}
+
+        def grad(t):
+            for h in range(2):
+                sums[t, h] = psum.tile([P, 512], F32, tag="sum", name="gradsum", bufs=4)
+                for g in range(CHUNKS):
+                    nc.tensor.matmul_mx(
+                        out=sums[t, h][:],
+                        lhsT=r_codes[:, t, g, :].bitcast(FP8X4),
+                        lhsT_scale=r_planes[:, t, g, :],
+                        rhs=bank[:, g, 1024 * h : 1024 * (h + 1)].bitcast(FP4X4),
+                        rhs_scale=bank_sc[:, g, 512 * h : 512 * (h + 1)],
+                        start=(g == 0),
+                        stop=(g == CHUNKS - 1),
+                    )
+
+        def finish(t):
+            res = work.tile([P, FEATS], F32, tag="res", name="res")
+            rows = slice(t * P, (t + 1) * P)
+            last = t == CAP_TILES - 1
+            for h in range(2):
+                cols = slice(512 * h, 512 * (h + 1))
+                if last and h == 1:
+                    for x in range(2):
+                        part = slice(512 + 256 * x, 512 + 256 * (x + 1))
+                        nc.vector.tensor_copy(out=res[:, part], in_=sums[t, h][:, 256 * x : 256 * (x + 1)])
+                        nc.sync.dma_start(out=out[rows, part], in_=res[:, part])
+                else:
+                    nc.scalar.copy(out=res[:, cols], in_=sums[t, h][:])
+                    if last:
+                        nc.sync.dma_start(out=out[rows, cols], in_=res[:, cols])
+            if not last:
+                nc.sync.dma_start(out=out[rows, :], in_=res[:])
+
+        def order_weights():
+            nc.vector.tensor_copy(
+                out=weight_ord[:].bitcast(F32).rearrange("p (g u q) -> p g u q", g=CHUNKS, u=2),
+                in_=weight_all[:].bitcast(F32).rearrange("p (g q u) -> p g u q", g=CHUNKS, u=2),
+            )
+
+        ctx.enter_context(tc.manual_schedule())
+        for h in range(PASSES):
+            spread_scale(h)
+        c0 = cap_turn(0)
+        for h in range(PASSES):
+            for s in range(2):
+                widen(0, s, CHUNK * h, CHUNK * (h + 1))
+        a0 = aud_turn(0, 0, [0])
+        c1 = cap_turn(1)
+        a0 += aud_turn(0, 0, [1])
+        bias_ps = psum.tile([P, P], BF16, tag="turn", name="bias_ps", bufs=4)
+        nc.tensor.transpose(bias_ps[:], bias_rows[:], ident_b[:])
+        widen(0, 2)
+        c2 = cap_turn(2)
+        widen(0, 3)
+        c3 = cap_turn(3)
+        aud_quant(0, 0, a0)
+        cap_quant(0, c0)
+        cap_quant(1, c1)
+        a1 = aud_turn(0, 1)
+        c4 = cap_turn(4)
+        cap_quant(2, c2)
+        nc.vector.tensor_copy(out=bias_cols[:], in_=bias_ps[:, 0:CAP_TILES])
+        aud_quant(0, 1, a1)
+        cap_quant(3, c3)
+        widen(1, 0)
+        c5 = cap_turn(5)
+        cap_quant(4, c4)
+        widen(1, 1)
+
+        def turns(t):
+            return [pair_turn(t, 0), pair_turn(t, 1)]
+
+        def quants(t, r):
+            pair_quant(t, 0, r[0])
+            pair_quant(t, 1, r[1])
+
+        for t in range(3):
+            logits(t, 0)
+        widen(1, 2)
+        c6 = cap_turn(6)
+        n0 = aud_turn(1, 0)
+        cap_quant(5, c5)
+        widen(1, 3)
+        for t in range(3, 5):
+            logits(t, 0)
+        aud_quant(1, 0, n0)
+        cap_quant(6, c6)
+        c7 = cap_turn(7)
+        n1 = aud_turn(1, 1)
+        widen(2, 0)
+        cap_quant(7, c7)
+        for t in range(5, 8):
+            logits(t, 0)
+        aud_quant(1, 1, n1)
+        widen(2, 1)
+        sort(2, 0)
+        widen(2, 2)
+        sort(2, 1)
+        widen(2, 3)
+        sort(2, 2)
+        for g in range(1, CHUNKS):
+            more = g + 1 < CHUNKS
+            for t in range(4):
+                logits(t, g)
+            if g == 1:
+                widen(3, 0)
+                sort(2, 3)
+            if more:
+                n0 = aud_turn(g + 1, 0)
+                n1 = aud_turn(g + 1, 1)
+            if g == 1:
+                widen(3, 1)
+                sort(3, 0)
+            if more:
+                aud_quant(g + 1, 0, n0)
+            if g == 1:
+                sort(3, 1)
+            if more:
+                aud_quant(g + 1, 1, n1)
+                for t in range(4, 8):
+                    logits(t, g)
+            if g == 1:
+                widen(3, 2)
+                widen(3, 3)
+                sort(3, 2)
+                sort(3, 3)
+                order_weights()
+                weigh(0, 0)
+                weigh(1, 0)
+        weigh(2, 0)
+        weigh(0, 1)
+        logits(4, 3)
+        weigh(1, 1)
+        logits(5, 3)
+        weigh(2, 1)
+        r0 = turns(0)
+        r1 = turns(1)
+        quants(0, r0)
+        logits(6, 3)
+        logits(7, 3)
+        weigh(3, 0)
+        weigh(3, 1)
+        quants(1, r1)
+
+        grad(0)
+        finish(0)
+        r2 = turns(2)
+        r3 = turns(3)
+        weigh(4, 0)
+        quants(2, r2)
+        weigh(4, 1)
+        quants(3, r3)
+        grad(1)
+        finish(1)
+        weigh(5, 0)
+        weigh(5, 1)
+        grad(2)
+        finish(2)
+        r4 = turns(4)
+        r5 = turns(5)
+        weigh(6, 0)
+        quants(4, r4)
+        weigh(6, 1)
+        quants(5, r5)
+        weigh(7, 0)
+        weigh(7, 1)
+        grad(3)
+        finish(3)
+        grad(4)
+        finish(4)
+        r6 = turns(6)
+        r7 = turns(7)
+        quants(6, r6)
+        quants(7, r7)
+        grad(5)
+        finish(5)
+        grad(6)
+        finish(6)
+        grad(7)
+        finish(7)

@@ -17,11 +17,10 @@ SIGMOID = mybir.ActivationFunctionType.Sigmoid
 CLIPS, CAPS, FEATS = 2048, 1024, 1024
 P = 128
 CHUNK = 512
+HALF = CHUNK // 2
 CHUNKS = CLIPS // CHUNK
 PASSES = FEATS // CHUNK
-CAP_TILES = CAPS // P
-
-SORT = 3
+TILES = CAPS // P
 
 FLOPS = 2 * 2 * CLIPS * CAPS * FEATS
 
@@ -33,368 +32,362 @@ def tile_siglip_negative_caption_gradient_s13_kernel(
     with ExitStack() as ctx:
         keep = ctx.enter_context(tc.tile_pool(name="keep", bufs=1))
         work = ctx.enter_context(tc.tile_pool(name="work", bufs=3))
-        psum = ctx.enter_context(tc.psum_pool(name="psum", bufs=2))
+        psum = ctx.enter_context(tc.psum_pool(name="psum", bufs=4))
 
-        scale_all = keep.tile([P, FEATS], F32, name="scale_all")
-        raw = [keep.tile([P, 4 * FEATS], U8, name="raw%d" % g) for g in range(CHUNKS)]
-        cap = [keep.tile([P, FEATS], BF16, name="cap%d" % t) for t in range(CAP_TILES)]
         scale_cols = keep.tile([P, PASSES, 4], F32, name="scale_cols")
+        scale_all = keep.tile([P, FEATS], F32, name="scale_all")
+        raw_first = [keep.tile([P, 2 * FEATS], U8, name="raw_first%d" % a) for a in range(2)]
+        raw_later = [keep.tile([P, 4 * FEATS], U8, name="raw_later%d" % g) for g in range(1, CHUNKS)]
+        cap_one = [keep.tile([P, FEATS], BF16, name="cap_one%d" % t) for t in range(2)]
+        cap_two = [keep.tile([P, 2 * FEATS], BF16, name="cap_two%d" % i) for i in range(1, TILES // 2)]
         weight_all = keep.tile([P, CLIPS], BF16, name="weight_all")
-        weight_ord = keep.tile([P, CLIPS], BF16, name="weight_ord")
-        bias_rows = keep.tile([P, P], BF16, name="bias_rows")
-        bias_cols = keep.tile([P, CAP_TILES], F32, name="bias_cols")
+        bias_cols = keep.tile([P, TILES], BF16, name="bias_cols")
         bank = keep.tile([P, CHUNKS, 2 * FEATS], U8, align_bytes=64, name="bank")
         bank_sc = keep.tile([P, CHUNKS, FEATS], U8, align_bytes=64, name="bank_sc")
         ident = keep.tile([P, P], F32, name="ident")
-        ident_b = keep.tile([P, P], BF16, name="ident_b")
-        dummy = keep.tile([P, 1], F32, name="dummy")
-        aud_codes = keep.tile([P, CHUNKS, PASSES, CHUNK], U32, align_bytes=64, name="aud_codes")
-        aud_planes = keep.tile([P, CHUNKS, PASSES, CHUNK], U8, align_bytes=64, name="aud_planes")
-        cap_codes = keep.tile([P, CAP_TILES, PASSES, P], U32, align_bytes=64, name="cap_codes")
-        cap_planes = keep.tile([P, CAP_TILES, PASSES, P], U8, align_bytes=64, name="cap_planes")
-        r_codes = keep.tile([P, CAP_TILES, CHUNKS, P], U32, align_bytes=64, name="r_codes")
-        r_planes = keep.tile([P, CAP_TILES, CHUNKS, P], U8, align_bytes=64, name="r_planes")
+        aud_codes = [keep.tile([P, PASSES, CHUNK], U32, align_bytes=64, name="aud_codes%d" % g) for g in range(CHUNKS)]
+        aud_planes = [keep.tile([P, PASSES, CHUNK], U8, align_bytes=64, name="aud_planes%d" % g) for g in range(CHUNKS)]
+        cap_codes = [keep.tile([P, PASSES * P], U32, align_bytes=64, name="cap_codes%d" % t) for t in range(TILES)]
+        cap_planes = [keep.tile([P, PASSES * P], U8, align_bytes=64, name="cap_planes%d" % t) for t in range(TILES)]
+        r_codes = [keep.tile([P, CHUNKS * P], U32, align_bytes=64, name="r_codes%d" % t) for t in range(TILES)]
+        r_planes = [keep.tile([P, CHUNKS * P], U8, align_bytes=64, name="r_planes%d" % t) for t in range(TILES)]
 
-        nc.vector.memset(dummy[:], 0.0)
-        nc.vector.memset(bias_rows[:], 0.0)
-        nc.scalar.activation(out=dummy[:], in_=dummy[:], func=SIGMOID)
+        ctx.enter_context(tc.manual_schedule())
+
+        table = keep.tile([P, 1], F32, name="table")
+        nc.vector.memset(table[:], 0.0)
+        nc.scalar.activation(out=table[:], in_=table[:], func=SIGMOID)
+
         make_identity(nc, ident[:])
-        make_identity(nc, ident_b[:])
         nc.gpsimd.memset(bank_sc[:].rearrange("p g d -> p (g d)").bitcast(U32), 0)
 
         aud_view = audio_bytes.rearrange("(g q s) d -> g q (s d)", q=P, s=4)
-        cap_view = captions.rearrange("(t p) d -> t p d", p=P)
-        half = 2 * FEATS
-        def load_cap(t):
-            nc.sync.dma_start(out=cap[t][:], in_=cap_view[t])
+        cap_view = captions.rearrange("(p t) d -> p (t d)", t=TILES)
+        out_view = out.rearrange("(p t) d -> p t d", t=TILES)
+
+        def load_cap_one(t):
+            nc.sync.dma_start(out=cap_one[t][:], in_=cap_view[:, t * FEATS : (t + 1) * FEATS])
+
+        def load_cap_two(i):
+            nc.sync.dma_start(out=cap_two[i - 1][:], in_=cap_view[:, 2 * i * FEATS : 2 * (i + 1) * FEATS])
+
+        def load_raw_first(a):
+            nc.sync.dma_start(out=raw_first[a][:], in_=aud_view[0][:, 2 * a * FEATS : 2 * (a + 1) * FEATS])
 
         nc.sync.dma_start(out=scale_cols[:], in_=audio_scale.rearrange("o (h n m) -> n (o h) m", h=PASSES, m=4))
-        nc.sync.dma_start(out=raw[0][:, :half], in_=aud_view[0][:, :half])
-        load_cap(0)
-        nc.sync.dma_start(out=raw[0][:, half:], in_=aud_view[0][:, half:])
-        nc.sync.dma_start(out=bias_rows[0:CAP_TILES, :], in_=bias.rearrange("(t p) -> t p", p=P))
-        load_cap(1)
-        load_cap(2)
-        load_cap(3)
-        for t in range(4, CAP_TILES):
-            load_cap(t)
-        nc.sync.dma_start(out=raw[1][:], in_=aud_view[1])
-        nc.sync.dma_start(out=raw[2][:], in_=aud_view[2])
-        nc.sync.dma_start(out=raw[3][:], in_=aud_view[3])
+        load_raw_first(0)
+        load_cap_one(0)
+        load_cap_one(1)
+        load_cap_two(1)
+        load_raw_first(1)
+        nc.sync.dma_start(out=bias_cols[:], in_=bias.rearrange("(p t) -> p t", t=TILES))
+        load_cap_two(2)
+        nc.sync.dma_start(out=raw_later[0][:], in_=aud_view[1])
+        load_cap_two(3)
+        nc.sync.dma_start(out=raw_later[1][:], in_=aud_view[2])
+        nc.sync.dma_start(out=raw_later[2][:], in_=aud_view[3])
         nc.sync.dma_start(out=weight_all[:], in_=clip_weight.partition_broadcast(P))
+        nc.sync.dma_start(out=bank[:], in_=bank_words.rearrange("g p n -> p g n"))
         for q in range(4):
             nc.sync.dma_start(
                 out=bank_sc[32 * q : 32 * q + 4, :, :].bitcast(I32),
                 in_=bank_scales[:, 4 * q : 4 * q + 4, :].rearrange("g r n -> r g n").bitcast(I32),
             )
-        nc.sync.dma_start(out=bank[:], in_=bank_words.rearrange("g p n -> p g n"))
 
-        def spread_scale(h):
-            xt = psum.tile([P, 4, P], F32, tag="sum", name="spread", bufs=4)
+        def cap_words(t):
+            if t < 2:
+                return cap_one[t][:].bitcast(F32)
+            return cap_two[t // 2 - 1][:, (t % 2) * FEATS : (t % 2 + 1) * FEATS].bitcast(F32)
+
+        def raw_slot(g, s):
+            if g == 0:
+                return raw_first[s // 2][:, (s % 2) * FEATS : (s % 2 + 1) * FEATS]
+            return raw_later[g - 1][:, s * FEATS : (s + 1) * FEATS]
+
+        def copy_out(engine, dst, src):
+            if engine == "vector":
+                nc.vector.tensor_copy(out=dst, in_=src)
+            else:
+                nc.scalar.copy(out=dst, in_=src)
+
+        def spread_scale(h, engine):
+            xt = psum.tile([P, 4, P], F32, tag="sum", name="spread")
             for m in range(4):
                 nc.tensor.transpose(xt[:, m, :], scale_cols[:, h, m : m + 1].to_broadcast([P, P]), ident[:])
-            nc.scalar.copy(
-                out=scale_all[:, CHUNK * h : CHUNK * (h + 1)].rearrange("p (n m) -> p n m", m=4),
-                in_=xt[:].rearrange("p m n -> p n m"),
-            )
+            copy_out(engine, scale_all[:, CHUNK * h : CHUNK * (h + 1)].rearrange("p (n m) -> p n m", m=4), xt[:].rearrange("p m n -> p n m"))
+
+        turned = {}
+        grouped = {}
 
         def cap_turn(t):
-            xt = psum.tile([P, PASSES, 2, P], F32, tag="turn", name="xt", bufs=4)
-            words = cap[t][:].bitcast(F32)
+            xt = psum.tile([P, PASSES, 2, P], F32, tag="turn", name="cap_xt")
+            words = cap_words(t)
             for h in range(PASSES):
                 for u in range(2):
                     nc.tensor.transpose(xt[:, h, u, :], words[:, 256 * h + u : 256 * (h + 1) : 2], ident[:])
-            grouped = work.tile([P, 1024], BF16, align_bytes=64, tag="grouped", name="cap_grouped", bufs=7)
-            nc.scalar.copy(
-                out=grouped[:].bitcast(F32).rearrange("p (h j u) -> p h j u", h=PASSES, u=2),
-                in_=xt[:].rearrange("p h u j -> p h j u"),
-            )
-            return grouped
+            turned["cap", t] = xt
 
-        def cap_quant(t, grouped):
-            nc.vector.quantize_mx(
-                out=cap_codes[:, t, :, :].rearrange("p h j -> p (h j)").bitcast(FP8X4),
-                scales=cap_planes[:, t, :, :].rearrange("p h j -> p (h j)"),
-                in_=grouped[:],
+        def cap_exit(t, engine="scalar"):
+            grouped["cap", t] = work.tile([P, 1024], BF16, align_bytes=64, tag="grouped", name="cap_grouped", bufs=7)
+            copy_out(
+                engine,
+                grouped["cap", t][:].bitcast(F32).rearrange("p (h j u) -> p h j u", h=PASSES, u=2),
+                turned["cap", t][:].rearrange("p h u j -> p h j u"),
             )
+
+        def cap_quant(t):
+            nc.vector.quantize_mx(out=cap_codes[t][:].bitcast(FP8X4), scales=cap_planes[t][:], in_=grouped["cap", t][:])
 
         audio = {}
+        ordered = set()
 
         def widen(g, s, first=0, end=FEATS):
-            if first == 0:
+            if (g, s) not in audio:
                 audio[g, s] = work.tile([P, FEATS], BF16, align_bytes=64, tag="audio", name="audio", bufs=6)
             nc.vector.tensor_tensor(
-                out=audio[g, s][:, first:end],
-                in0=raw[g][:, s * FEATS + first : s * FEATS + end].bitcast(FP8),
-                in1=scale_all[:, first:end],
-                op=MULT,
+                out=audio[g, s][:, first:end], in0=raw_slot(g, s)[:, first:end].bitcast(FP8), in1=scale_all[:, first:end], op=MULT
             )
 
         def sort(g, s):
-            if g < SORT:
-                return
             flat = work.tile([P, FEATS], BF16, align_bytes=64, tag="sorted", name="flat", bufs=4)
             nc.vector.tensor_copy(
                 out=flat[:].bitcast(F32).rearrange("p (h u w) -> p h u w", h=PASSES, u=2),
                 in_=audio[g, s][:].bitcast(F32).rearrange("p (h w u) -> p h u w", h=PASSES, u=2),
             )
             audio[g, s] = flat
+            ordered.add((g, s))
 
-        def aud_turn(g, top, halves=range(PASSES)):
-            res = []
-            for h in halves:
-                xt = psum.tile([P, 2, 2, P], F32, tag="turn", name="xt", bufs=4)
+        def aud_turn(g, a, h):
+            xt = psum.tile([P, 2, 2, P], F32, tag="turn", name="aud_xt")
+            for e in range(2):
+                words = audio[g, 2 * a + e][:].bitcast(F32)
                 for u in range(2):
-                    for e in range(2):
-                        words = audio[g, 2 * top + e][:].bitcast(F32)
-                        if g < SORT:
-                            words = words[:, 256 * h + u : 256 * (h + 1) : 2]
-                        else:
-                            words = words[:, 256 * h + P * u : 256 * h + P * (u + 1)]
-                        nc.tensor.transpose(xt[:, u, e, :], words, ident[:])
-                grouped = work.tile([P, 1024], BF16, align_bytes=64, tag="grouped", name="aud_grouped", bufs=7)
-                nc.scalar.copy(
-                    out=grouped[:].bitcast(F32).rearrange("p (q e u) -> p q e u", e=2, u=2),
-                    in_=xt[:].rearrange("p u e q -> p q e u"),
-                )
-                res.append(grouped)
-            return res
+                    if (g, 2 * a + e) in ordered:
+                        src = words[:, 256 * h + P * u : 256 * h + P * (u + 1)]
+                    else:
+                        src = words[:, 256 * h + u : 256 * (h + 1) : 2]
+                    nc.tensor.transpose(xt[:, u, e, :], src, ident[:])
+            turned["aud", g, a, h] = xt
 
-        def aud_quant(g, top, res):
-            for h in range(PASSES):
-                cols = slice(256 * top, 256 * (top + 1))
-                nc.vector.quantize_mx(
-                    out=aud_codes[:, g, h, cols].bitcast(FP8X4), scales=aud_planes[:, g, h, cols], in_=res[h][:]
-                )
-
-        sigs = {}
-        resids = {}
-
-        def logits(t, g):
-            pair = g // 2
-            if g % 2 == 0:
-                sigs[t, pair] = work.tile([P, 2, CHUNK], F32, tag="sig", name="sig", bufs=16)
-            acc = psum.tile([P, CHUNK], F32, tag="sum", name="acc", bufs=4)
-            for h in range(PASSES):
-                nc.tensor.matmul_mx(
-                    out=acc[:],
-                    lhsT=cap_codes[:, t, h, :].bitcast(FP8X4),
-                    lhsT_scale=cap_planes[:, t, h, :],
-                    rhs=aud_codes[:, g, h, :].bitcast(FP8X4),
-                    rhs_scale=aud_planes[:, g, h, :],
-                    start=(h == 0),
-                    stop=(h == PASSES - 1),
-                )
-            nc.scalar.activation(out=sigs[t, pair][:, g % 2, :], in_=acc[:], func=SIGMOID, bias=bias_cols[:, t : t + 1])
-
-        def weigh(t, pair):
-            resids[t, pair] = work.tile([P, 2, CHUNK], BF16, align_bytes=64, tag="resid", name="resid", bufs=10)
-            nc.vector.tensor_tensor(
-                out=resids[t, pair][:],
-                in0=sigs[t, pair][:],
-                in1=weight_ord[:, 2 * CHUNK * pair : 2 * CHUNK * (pair + 1)].rearrange("p (a c) -> p a c", a=2),
-                op=MULT,
+        def aud_exit(g, a, h, engine="scalar"):
+            key = ("aud", g, a, h)
+            grouped[key] = work.tile([P, 1024], BF16, align_bytes=64, tag="grouped", name="aud_grouped", bufs=7)
+            copy_out(
+                engine,
+                grouped[key][:].bitcast(F32).rearrange("p (q e u) -> p q e u", e=2, u=2),
+                turned[key][:].rearrange("p u e q -> p q e u"),
             )
 
-        def pair_turn(t, pair):
-            xt = psum.tile([P, 2, 2, P], F32, tag="turn", name="xt", bufs=4)
-            for a in range(2):
-                words = resids[t, pair][:, a, :].bitcast(F32)
-                for top in range(2):
-                    nc.tensor.transpose(xt[:, a, top, :], words[:, P * top : P * (top + 1)], ident[:])
-            grouped = work.tile([P, 1024], BF16, align_bytes=64, tag="grouped", name="r_grouped", bufs=7)
-            nc.scalar.copy(
-                out=grouped[:].bitcast(F32).rearrange("p (a j u) -> p a j u", a=2, u=2),
-                in_=xt[:].rearrange("p a u j -> p a j u"),
-            )
-            return grouped
-
-        def pair_quant(t, pair, grouped):
-            two = slice(2 * pair, 2 * pair + 2)
+        def aud_quant(g, a, h):
+            cols = slice(HALF * a, HALF * (a + 1))
             nc.vector.quantize_mx(
-                out=r_codes[:, t, two, :].rearrange("p a j -> p (a j)").bitcast(FP8X4),
-                scales=r_planes[:, t, two, :].rearrange("p a j -> p (a j)"),
-                in_=grouped[:],
+                out=aud_codes[g][:, h, cols].bitcast(FP8X4), scales=aud_planes[g][:, h, cols], in_=grouped["aud", g, a, h][:]
             )
 
         sums = {}
+        sigs = {}
+        resids = {}
 
-        def grad(t):
-            for h in range(2):
-                sums[t, h] = psum.tile([P, 512], F32, tag="sum", name="gradsum", bufs=4)
-                for g in range(CHUNKS):
-                    nc.tensor.matmul_mx(
-                        out=sums[t, h][:],
-                        lhsT=r_codes[:, t, g, :].bitcast(FP8X4),
-                        lhsT_scale=r_planes[:, t, g, :],
-                        rhs=bank[:, g, 1024 * h : 1024 * (h + 1)].bitcast(FP4X4),
-                        rhs_scale=bank_sc[:, g, 512 * h : 512 * (h + 1)],
-                        start=(g == 0),
-                        stop=(g == CHUNKS - 1),
-                    )
+        def logits(t, g, first=0, end=CHUNK):
+            sums[t, g] = psum.tile([P, end - first], F32, tag="sum", name="logit_sum")
+            for h in range(PASSES):
+                nc.tensor.matmul_mx(
+                    out=sums[t, g][:],
+                    lhsT=cap_codes[t][:, P * h : P * (h + 1)].bitcast(FP8X4),
+                    lhsT_scale=cap_planes[t][:, P * h : P * (h + 1)],
+                    rhs=aud_codes[g][:, h, first:end].bitcast(FP8X4),
+                    rhs_scale=aud_planes[g][:, h, first:end],
+                    start=(h == 0),
+                    stop=(h == PASSES - 1),
+                )
 
-        def finish(t):
-            res = work.tile([P, FEATS], F32, tag="res", name="res")
-            rows = slice(t * P, (t + 1) * P)
-            last = t == CAP_TILES - 1
-            for h in range(2):
-                cols = slice(512 * h, 512 * (h + 1))
-                if last and h == 1:
-                    for x in range(2):
-                        part = slice(512 + 256 * x, 512 + 256 * (x + 1))
-                        nc.vector.tensor_copy(out=res[:, part], in_=sums[t, h][:, 256 * x : 256 * (x + 1)])
-                        nc.sync.dma_start(out=out[rows, part], in_=res[:, part])
-                else:
-                    nc.scalar.copy(out=res[:, cols], in_=sums[t, h][:])
-                    if last:
-                        nc.sync.dma_start(out=out[rows, cols], in_=res[:, cols])
-            if not last:
-                nc.sync.dma_start(out=out[rows, :], in_=res[:])
+        def sigmoid(t, g, first=0, end=CHUNK):
+            pair = g // 2
+            if (t, pair) not in sigs:
+                sigs[t, pair] = work.tile([P, 2, CHUNK], F32, tag="sig", name="sig", bufs=16)
+            nc.scalar.activation(out=sigs[t, pair][:, g % 2, first:end], in_=sums[t, g][:], func=SIGMOID, bias=bias_cols[:, t : t + 1])
 
-        def order_weights():
-            nc.vector.tensor_copy(
-                out=weight_ord[:].bitcast(F32).rearrange("p (g u q) -> p g u q", g=CHUNKS, u=2),
-                in_=weight_all[:].bitcast(F32).rearrange("p (g q u) -> p g u q", g=CHUNKS, u=2),
+        def weigh(t, pair):
+            resids[t, pair] = work.tile([P, 2 * CHUNK], BF16, align_bytes=64, tag="resid", name="resid", bufs=10)
+            weights = weight_all[:, 2 * CHUNK * pair : 2 * CHUNK * (pair + 1)]
+            nc.vector.tensor_tensor(
+                out=resids[t, pair][:].rearrange("p (u c q e) -> p u c q e", u=2, c=2, e=2),
+                in0=sigs[t, pair][:].rearrange("p c (u q e) -> p u c q e", u=2, e=2),
+                in1=weights.rearrange("p (c q u e) -> p u c q e", c=2, u=2, e=2),
+                op=MULT,
             )
 
-        ctx.enter_context(tc.manual_schedule())
-        for h in range(PASSES):
-            spread_scale(h)
-        c0 = cap_turn(0)
-        for h in range(PASSES):
-            for s in range(2):
-                widen(0, s, CHUNK * h, CHUNK * (h + 1))
-        a0 = aud_turn(0, 0, [0])
-        c1 = cap_turn(1)
-        a0 += aud_turn(0, 0, [1])
-        bias_ps = psum.tile([P, P], BF16, tag="turn", name="bias_ps", bufs=4)
-        nc.tensor.transpose(bias_ps[:], bias_rows[:], ident_b[:])
-        widen(0, 2)
-        c2 = cap_turn(2)
-        widen(0, 3)
-        c3 = cap_turn(3)
-        aud_quant(0, 0, a0)
-        cap_quant(0, c0)
-        cap_quant(1, c1)
-        a1 = aud_turn(0, 1)
-        c4 = cap_turn(4)
-        cap_quant(2, c2)
-        nc.vector.tensor_copy(out=bias_cols[:], in_=bias_ps[:, 0:CAP_TILES])
-        aud_quant(0, 1, a1)
-        cap_quant(3, c3)
-        widen(1, 0)
-        c5 = cap_turn(5)
-        cap_quant(4, c4)
-        widen(1, 1)
+        def r_turn(t, pair):
+            xt = psum.tile([P, 2, 2, P], F32, tag="turn", name="r_xt")
+            words = resids[t, pair][:].bitcast(F32)
+            for u in range(2):
+                for c in range(2):
+                    nc.tensor.transpose(xt[:, c, u, :], words[:, 256 * u + P * c : 256 * u + P * (c + 1)], ident[:])
+            turned["r", t, pair] = xt
+
+        def r_exit(t, pair):
+            key = ("r", t, pair)
+            grouped[key] = work.tile([P, 1024], BF16, align_bytes=64, tag="grouped", name="r_grouped", bufs=7)
+            nc.scalar.copy(
+                out=grouped[key][:].bitcast(F32).rearrange("p (c j u) -> p c j u", c=2, u=2),
+                in_=turned[key][:].rearrange("p c u j -> p c j u"),
+            )
+
+        def r_quant(t, pair):
+            cols = slice(2 * P * pair, 2 * P * (pair + 1))
+            nc.vector.quantize_mx(out=r_codes[t][:, cols].bitcast(FP8X4), scales=r_planes[t][:, cols], in_=grouped["r", t, pair][:])
+
+        def grad(t, first, end, engine="scalar"):
+            acc = psum.tile([P, end - first], F32, tag="sum", name="grad_sum")
+            for g in range(CHUNKS):
+                nc.tensor.matmul_mx(
+                    out=acc[:],
+                    lhsT=r_codes[t][:, P * g : P * (g + 1)].bitcast(FP8X4),
+                    lhsT_scale=r_planes[t][:, P * g : P * (g + 1)],
+                    rhs=bank[:, g, 2 * first : 2 * end].bitcast(FP4X4),
+                    rhs_scale=bank_sc[:, g, first:end],
+                    start=(g == 0),
+                    stop=(g == CHUNKS - 1),
+                )
+            res = work.tile([P, end - first], F32, tag="res", name="res", bufs=6)
+            copy_out(engine, res[:], acc[:])
+            nc.sync.dma_start(out=out_view[:, t, first:end], in_=res[:])
+
+        def cap_prepare(t):
+            cap_turn(t)
+            cap_exit(t)
+
+        def aud_prepare(g, a, passes=range(PASSES)):
+            for h in passes:
+                aud_turn(g, a, h)
+                aud_exit(g, a, h)
+
+        def aud_quants(g, a):
+            for h in range(PASSES):
+                aud_quant(g, a, h)
+
+        def probs(tiles, g, first=0, end=CHUNK):
+            for t in tiles:
+                logits(t, g, first, end)
+                sigmoid(t, g, first, end)
 
         def turns(t):
-            return [pair_turn(t, 0), pair_turn(t, 1)]
+            for pair in range(2):
+                r_turn(t, pair)
+                r_exit(t, pair)
 
-        def quants(t, r):
-            pair_quant(t, 0, r[0])
-            pair_quant(t, 1, r[1])
+        def quants(t):
+            for pair in range(2):
+                r_quant(t, pair)
 
-        for t in range(3):
-            logits(t, 0)
+        def grads(t):
+            grad(t, 0, CHUNK)
+            grad(t, CHUNK, FEATS)
+
+        spread_scale(0, "vector")
+        spread_scale(1, "scalar")
+        cap_prepare(0)
+        for h in range(PASSES):
+            widen(0, 0, CHUNK * h, CHUNK * (h + 1))
+            widen(0, 1, CHUNK * h, CHUNK * (h + 1))
+        cap_prepare(1)
+        aud_prepare(0, 0, [0])
+        cap_prepare(2)
+        aud_prepare(0, 0, [1])
+        widen(0, 2)
+        widen(0, 3)
+        cap_prepare(3)
+        cap_quant(0)
+        aud_quants(0, 0)
+        cap_quant(1)
+        cap_prepare(4)
+        aud_prepare(0, 1)
+        cap_quant(2)
+        probs(range(3), 0, 0, HALF)
+        widen(1, 0)
+        aud_quants(0, 1)
+        cap_quant(3)
+        widen(1, 1)
+        probs(range(3), 0, HALF, CHUNK)
+        probs([3], 0)
+        cap_quant(4)
         widen(1, 2)
-        c6 = cap_turn(6)
-        n0 = aud_turn(1, 0)
-        cap_quant(5, c5)
+        cap_prepare(5)
+        cap_prepare(6)
+        aud_prepare(1, 0)
         widen(1, 3)
-        for t in range(3, 5):
-            logits(t, 0)
-        aud_quant(1, 0, n0)
-        cap_quant(6, c6)
-        c7 = cap_turn(7)
-        n1 = aud_turn(1, 1)
+        cap_quant(5)
+        cap_quant(6)
+        probs(range(4, 6), 0)
         widen(2, 0)
-        cap_quant(7, c7)
-        for t in range(5, 8):
-            logits(t, 0)
-        aud_quant(1, 1, n1)
+        aud_quants(1, 0)
+        aud_prepare(1, 1)
+        cap_prepare(7)
         widen(2, 1)
-        sort(2, 0)
+        aud_quants(1, 1)
+        cap_quant(7)
+        probs([6], 0)
         widen(2, 2)
-        sort(2, 1)
         widen(2, 3)
-        sort(2, 2)
-        for g in range(1, CHUNKS):
-            more = g + 1 < CHUNKS
-            for t in range(4):
-                logits(t, g)
-            if g == 1:
-                widen(3, 0)
-                sort(2, 3)
-            if more:
-                n0 = aud_turn(g + 1, 0)
-                n1 = aud_turn(g + 1, 1)
-            if g == 1:
-                widen(3, 1)
-                sort(3, 0)
-            if more:
-                aud_quant(g + 1, 0, n0)
-            if g == 1:
-                sort(3, 1)
-            if more:
-                aud_quant(g + 1, 1, n1)
-                for t in range(4, 8):
-                    logits(t, g)
-            if g == 1:
-                widen(3, 2)
-                widen(3, 3)
-                sort(3, 2)
-                sort(3, 3)
-                order_weights()
-                weigh(0, 0)
-                weigh(1, 0)
-        weigh(2, 0)
-        weigh(0, 1)
-        logits(4, 3)
-        weigh(1, 1)
-        logits(5, 3)
-        weigh(2, 1)
-        r0 = turns(0)
-        r1 = turns(1)
-        quants(0, r0)
-        logits(6, 3)
-        logits(7, 3)
-        weigh(3, 0)
-        weigh(3, 1)
-        quants(1, r1)
+        probs(range(2), 1)
+        probs([7], 0)
+        probs(range(2, 4), 1)
+        aud_prepare(2, 0)
+        aud_prepare(2, 1)
+        widen(3, 0)
+        widen(3, 1)
+        aud_quants(2, 0)
+        sort(3, 0)
+        aud_quants(2, 1)
+        probs(range(4, 8), 1)
+        sort(3, 1)
+        widen(3, 2)
+        widen(3, 3)
+        sort(3, 2)
+        sort(3, 3)
+        probs(range(4), 2)
+        weigh(0, 0)
+        for a in range(2):
+            aud_turn(3, a, 0)
+            aud_exit(3, a, 0, "vector")
+            aud_turn(3, a, 1)
+            aud_exit(3, a, 1)
+        aud_quants(3, 0)
+        aud_quants(3, 1)
+        weigh(1, 0)
+        probs(range(4, 8), 2)
 
-        grad(0)
-        finish(0)
-        r2 = turns(2)
-        r3 = turns(3)
-        weigh(4, 0)
-        quants(2, r2)
-        weigh(4, 1)
-        quants(3, r3)
-        grad(1)
-        finish(1)
-        weigh(5, 0)
-        weigh(5, 1)
-        grad(2)
-        finish(2)
-        r4 = turns(4)
-        r5 = turns(5)
-        weigh(6, 0)
-        quants(4, r4)
-        weigh(6, 1)
-        quants(5, r5)
-        weigh(7, 0)
-        weigh(7, 1)
-        grad(3)
-        finish(3)
-        grad(4)
-        finish(4)
-        r6 = turns(6)
-        r7 = turns(7)
-        quants(6, r6)
-        quants(7, r7)
-        grad(5)
-        finish(5)
-        grad(6)
-        finish(6)
-        grad(7)
-        finish(7)
+        last = CHUNKS - 1
+        weigh(2, 0)
+        probs(range(4), last)
+        weigh(0, 1)
+        weigh(1, 1)
+        probs([4], last)
+        for pair in range(2):
+            for t in range(2):
+                r_turn(t, pair)
+                r_exit(t, pair)
+        weigh(2, 1)
+        probs(range(5, 8), last)
+        quants(0)
+        weigh(3, 0)
+        quants(1)
+        weigh(3, 1)
+        grads(0)
+        for t in range(2, TILES, 2):
+            turns(t)
+            turns(t + 1)
+            if t + 2 < TILES:
+                weigh(t + 2, 0)
+            quants(t)
+            if t + 2 < TILES:
+                weigh(t + 2, 1)
+            quants(t + 1)
+            grads(t - 1)
+            if t + 2 < TILES:
+                weigh(t + 3, 0)
+                weigh(t + 3, 1)
+            grads(t)
+        grad(TILES - 1, 0, CHUNK)
+        grad(TILES - 1, CHUNK, CHUNK + HALF, "vector")
+        grad(TILES - 1, CHUNK + HALF, FEATS)

@@ -32,7 +32,7 @@ def tile_siglip_negative_caption_gradient_s13_kernel(
     with ExitStack() as ctx:
         keep = ctx.enter_context(tc.tile_pool(name="keep", bufs=1))
         work = ctx.enter_context(tc.tile_pool(name="work", bufs=3))
-        psum = ctx.enter_context(tc.psum_pool(name="psum", bufs=4))
+        psum = ctx.enter_context(tc.psum_pool(name="psum", bufs=8))
 
         scale_cols = keep.tile([P, PASSES, 4], F32, name="scale_cols")
         scale_all = keep.tile([P, FEATS], F32, name="scale_all")
@@ -54,12 +54,20 @@ def tile_siglip_negative_caption_gradient_s13_kernel(
 
         ctx.enter_context(tc.manual_schedule())
 
+        zeros = keep.tile([P, CHUNK], F32, name="zeros")
+        nc.vector.memset(zeros[:], 0.0)
+
         table = keep.tile([P, 1], F32, name="table")
         nc.vector.memset(table[:], 0.0)
         nc.scalar.activation(out=table[:], in_=table[:], func=SIGMOID)
 
         make_identity(nc, ident[:])
         nc.gpsimd.memset(bank_sc[:].rearrange("p g d -> p (g d)").bitcast(U32), 0)
+
+        def keep_clock_up(n):
+            idle = psum.tile([P, n], F32, tag="bank", name="idle")
+            nc.tensor.matmul(idle[:], lhsT=zeros[:, :P], rhs=zeros[:, :n], start=True, stop=True)
+
 
         aud_view = audio_bytes.rearrange("(g q s) d -> g q (s d)", q=P, s=4)
         cap_view = captions.rearrange("(p t) d -> p (t d)", t=TILES)
@@ -75,8 +83,8 @@ def tile_siglip_negative_caption_gradient_s13_kernel(
             nc.sync.dma_start(out=raw_first[a][:], in_=aud_view[0][:, 2 * a * FEATS : 2 * (a + 1) * FEATS])
 
         nc.sync.dma_start(out=scale_cols[:], in_=audio_scale.rearrange("o (h n m) -> n (o h) m", h=PASSES, m=4))
-        load_raw_first(0)
         load_cap_one(0)
+        load_raw_first(0)
         load_cap_one(1)
         load_cap_two(1)
         load_raw_first(1)
@@ -111,7 +119,7 @@ def tile_siglip_negative_caption_gradient_s13_kernel(
                 nc.scalar.copy(out=dst, in_=src)
 
         def spread_scale(h, engine):
-            xt = psum.tile([P, 4, P], F32, tag="sum", name="spread")
+            xt = psum.tile([P, 4, P], F32, tag="bank", name="spread")
             for m in range(4):
                 nc.tensor.transpose(xt[:, m, :], scale_cols[:, h, m : m + 1].to_broadcast([P, P]), ident[:])
             copy_out(engine, scale_all[:, CHUNK * h : CHUNK * (h + 1)].rearrange("p (n m) -> p n m", m=4), xt[:].rearrange("p m n -> p n m"))
@@ -120,7 +128,7 @@ def tile_siglip_negative_caption_gradient_s13_kernel(
         grouped = {}
 
         def cap_turn(t):
-            xt = psum.tile([P, PASSES, 2, P], F32, tag="turn", name="cap_xt")
+            xt = psum.tile([P, PASSES, 2, P], F32, tag="bank", name="cap_xt")
             words = cap_words(t)
             for h in range(PASSES):
                 for u in range(2):
@@ -128,7 +136,7 @@ def tile_siglip_negative_caption_gradient_s13_kernel(
             turned["cap", t] = xt
 
         def cap_exit(t, engine="scalar"):
-            grouped["cap", t] = work.tile([P, 1024], BF16, align_bytes=64, tag="grouped", name="cap_grouped", bufs=7)
+            grouped["cap", t] = work.tile([P, 1024], BF16, align_bytes=64, tag="grouped", name="cap_grouped", bufs=9)
             copy_out(
                 engine,
                 grouped["cap", t][:].bitcast(F32).rearrange("p (h j u) -> p h j u", h=PASSES, u=2),
@@ -151,31 +159,31 @@ def tile_siglip_negative_caption_gradient_s13_kernel(
         def sort(g, s):
             flat = work.tile([P, FEATS], BF16, align_bytes=64, tag="sorted", name="flat", bufs=4)
             nc.vector.tensor_copy(
-                out=flat[:].bitcast(F32).rearrange("p (h u w) -> p h u w", h=PASSES, u=2),
-                in_=audio[g, s][:].bitcast(F32).rearrange("p (h w u) -> p h u w", h=PASSES, u=2),
+                out=flat[:].bitcast(F32).rearrange("p (u w) -> p u w", u=2),
+                in_=audio[g, s][:].bitcast(F32).rearrange("p (w u) -> p u w", u=2),
             )
             audio[g, s] = flat
             ordered.add((g, s))
 
         def aud_turn(g, a, h):
-            xt = psum.tile([P, 2, 2, P], F32, tag="turn", name="aud_xt")
+            xt = psum.tile([P, 2, 2, P], F32, tag="bank", name="aud_xt")
             for e in range(2):
                 words = audio[g, 2 * a + e][:].bitcast(F32)
                 for u in range(2):
                     if (g, 2 * a + e) in ordered:
-                        src = words[:, 256 * h + P * u : 256 * h + P * (u + 1)]
+                        src = words[:, 256 * u + P * h : 256 * u + P * (h + 1)]
                     else:
                         src = words[:, 256 * h + u : 256 * (h + 1) : 2]
-                    nc.tensor.transpose(xt[:, u, e, :], src, ident[:])
+                    nc.tensor.transpose(xt[:, e, u, :], src, ident[:])
             turned["aud", g, a, h] = xt
 
         def aud_exit(g, a, h, engine="scalar"):
             key = ("aud", g, a, h)
-            grouped[key] = work.tile([P, 1024], BF16, align_bytes=64, tag="grouped", name="aud_grouped", bufs=7)
+            grouped[key] = work.tile([P, 1024], BF16, align_bytes=64, tag="grouped", name="aud_grouped", bufs=9)
             copy_out(
                 engine,
                 grouped[key][:].bitcast(F32).rearrange("p (q e u) -> p q e u", e=2, u=2),
-                turned[key][:].rearrange("p u e q -> p q e u"),
+                turned[key][:].rearrange("p e u q -> p q e u"),
             )
 
         def aud_quant(g, a, h):
@@ -189,7 +197,7 @@ def tile_siglip_negative_caption_gradient_s13_kernel(
         resids = {}
 
         def logits(t, g, first=0, end=CHUNK):
-            sums[t, g] = psum.tile([P, end - first], F32, tag="sum", name="logit_sum")
+            sums[t, g] = psum.tile([P, end - first], F32, tag="bank", name="logit_sum")
             for h in range(PASSES):
                 nc.tensor.matmul_mx(
                     out=sums[t, g][:],
@@ -208,7 +216,7 @@ def tile_siglip_negative_caption_gradient_s13_kernel(
             nc.scalar.activation(out=sigs[t, pair][:, g % 2, first:end], in_=sums[t, g][:], func=SIGMOID, bias=bias_cols[:, t : t + 1])
 
         def weigh(t, pair):
-            resids[t, pair] = work.tile([P, 2 * CHUNK], BF16, align_bytes=64, tag="resid", name="resid", bufs=10)
+            resids[t, pair] = work.tile([P, 2 * CHUNK], BF16, align_bytes=64, tag="resid", name="resid", bufs=9)
             weights = weight_all[:, 2 * CHUNK * pair : 2 * CHUNK * (pair + 1)]
             nc.vector.tensor_tensor(
                 out=resids[t, pair][:].rearrange("p (u c q e) -> p u c q e", u=2, c=2, e=2),
@@ -218,19 +226,20 @@ def tile_siglip_negative_caption_gradient_s13_kernel(
             )
 
         def r_turn(t, pair):
-            xt = psum.tile([P, 2, 2, P], F32, tag="turn", name="r_xt")
+            xt = psum.tile([P, 2, 2, P], F32, tag="bank", name="r_xt")
             words = resids[t, pair][:].bitcast(F32)
             for u in range(2):
                 for c in range(2):
                     nc.tensor.transpose(xt[:, c, u, :], words[:, 256 * u + P * c : 256 * u + P * (c + 1)], ident[:])
             turned["r", t, pair] = xt
 
-        def r_exit(t, pair):
+        def r_exit(t, pair, engine="scalar"):
             key = ("r", t, pair)
-            grouped[key] = work.tile([P, 1024], BF16, align_bytes=64, tag="grouped", name="r_grouped", bufs=7)
-            nc.scalar.copy(
-                out=grouped[key][:].bitcast(F32).rearrange("p (c j u) -> p c j u", c=2, u=2),
-                in_=turned[key][:].rearrange("p c u j -> p c j u"),
+            grouped[key] = work.tile([P, 1024], BF16, align_bytes=64, tag="grouped", name="r_grouped", bufs=9)
+            copy_out(
+                engine,
+                grouped[key][:].bitcast(F32).rearrange("p (c j u) -> p c j u", c=2, u=2),
+                turned[key][:].rearrange("p c u j -> p c j u"),
             )
 
         def r_quant(t, pair):
@@ -238,7 +247,7 @@ def tile_siglip_negative_caption_gradient_s13_kernel(
             nc.vector.quantize_mx(out=r_codes[t][:, cols].bitcast(FP8X4), scales=r_planes[t][:, cols], in_=grouped["r", t, pair][:])
 
         def grad(t, first, end, engine="scalar"):
-            acc = psum.tile([P, end - first], F32, tag="sum", name="grad_sum")
+            acc = psum.tile([P, end - first], F32, tag="bank", name="grad_sum")
             for g in range(CHUNKS):
                 nc.tensor.matmul_mx(
                     out=acc[:],
@@ -249,7 +258,8 @@ def tile_siglip_negative_caption_gradient_s13_kernel(
                     start=(g == 0),
                     stop=(g == CHUNKS - 1),
                 )
-            res = work.tile([P, end - first], F32, tag="res", name="res", bufs=6)
+            tag = "res" if end - first == CHUNK else "res_part"
+            res = work.tile([P, end - first], F32, tag=tag, name="res", bufs=4)
             copy_out(engine, res[:], acc[:])
             nc.sync.dma_start(out=out_view[:, t, first:end], in_=res[:])
 
@@ -284,24 +294,29 @@ def tile_siglip_negative_caption_gradient_s13_kernel(
             grad(t, 0, CHUNK)
             grad(t, CHUNK, FEATS)
 
-        spread_scale(0, "vector")
+        keep_clock_up(384)
+        spread_scale(0, "scalar")
         spread_scale(1, "scalar")
         cap_prepare(0)
+        keep_clock_up(128)
         for h in range(PASSES):
             widen(0, 0, CHUNK * h, CHUNK * (h + 1))
             widen(0, 1, CHUNK * h, CHUNK * (h + 1))
         cap_prepare(1)
+        keep_clock_up(128)
         aud_prepare(0, 0, [0])
         cap_prepare(2)
         aud_prepare(0, 0, [1])
         widen(0, 2)
         widen(0, 3)
         cap_prepare(3)
+        keep_clock_up(128)
         cap_quant(0)
         aud_quants(0, 0)
         cap_quant(1)
         cap_prepare(4)
         aud_prepare(0, 1)
+        cap_prepare(5)
         cap_quant(2)
         probs(range(3), 0, 0, HALF)
         widen(1, 0)
@@ -311,47 +326,46 @@ def tile_siglip_negative_caption_gradient_s13_kernel(
         probs(range(3), 0, HALF, CHUNK)
         probs([3], 0)
         cap_quant(4)
-        widen(1, 2)
-        cap_prepare(5)
-        cap_prepare(6)
-        aud_prepare(1, 0)
-        widen(1, 3)
         cap_quant(5)
-        cap_quant(6)
-        probs(range(4, 6), 0)
-        widen(2, 0)
-        aud_quants(1, 0)
-        aud_prepare(1, 1)
+        cap_prepare(6)
         cap_prepare(7)
-        widen(2, 1)
-        aud_quants(1, 1)
+        aud_prepare(1, 0)
+        widen(1, 2)
+        widen(1, 3)
+        probs(range(4, 6), 0)
+        aud_quants(1, 0)
+        cap_quant(6)
         cap_quant(7)
-        probs([6], 0)
+        aud_prepare(1, 1)
+        widen(2, 0)
+        probs(range(4), 1, 0, HALF)
+        aud_quants(1, 1)
+        widen(2, 1)
+        probs(range(6, 8), 0)
         widen(2, 2)
         widen(2, 3)
-        probs(range(2), 1)
-        probs([7], 0)
-        probs(range(2, 4), 1)
+        probs(range(4), 1, HALF, CHUNK)
         aud_prepare(2, 0)
         aud_prepare(2, 1)
         widen(3, 0)
         widen(3, 1)
         aud_quants(2, 0)
-        sort(3, 0)
         aud_quants(2, 1)
         probs(range(4, 8), 1)
+        sort(3, 0)
         sort(3, 1)
         widen(3, 2)
         widen(3, 3)
-        sort(3, 2)
-        sort(3, 3)
         probs(range(4), 2)
         weigh(0, 0)
-        for a in range(2):
-            aud_turn(3, a, 0)
-            aud_exit(3, a, 0, "vector")
-            aud_turn(3, a, 1)
-            aud_exit(3, a, 1)
+        aud_turn(3, 0, 0)
+        aud_exit(3, 0, 0, "vector")
+        aud_turn(3, 0, 1)
+        aud_exit(3, 0, 1)
+        aud_turn(3, 1, 0)
+        aud_turn(3, 1, 1)
+        aud_exit(3, 1, 0, "vector")
+        aud_exit(3, 1, 1)
         aud_quants(3, 0)
         aud_quants(3, 1)
         weigh(1, 0)

@@ -54,19 +54,12 @@ def tile_siglip_negative_caption_gradient_s13_kernel(
 
         ctx.enter_context(tc.manual_schedule())
 
-        zeros = keep.tile([P, CHUNK], F32, name="zeros")
-        nc.vector.memset(zeros[:], 0.0)
-
         table = keep.tile([P, 1], F32, name="table")
         nc.vector.memset(table[:], 0.0)
         nc.scalar.activation(out=table[:], in_=table[:], func=SIGMOID)
 
         make_identity(nc, ident[:])
         nc.gpsimd.memset(bank_sc[:].rearrange("p g d -> p (g d)").bitcast(U32), 0)
-
-        def keep_clock_up(n):
-            idle = psum.tile([P, n], F32, tag="bank", name="idle")
-            nc.tensor.matmul(idle[:], lhsT=zeros[:, :P], rhs=zeros[:, :n], start=True, stop=True)
 
 
         aud_view = audio_bytes.rearrange("(g q s) d -> g q (s d)", q=P, s=4)
@@ -294,23 +287,19 @@ def tile_siglip_negative_caption_gradient_s13_kernel(
             grad(t, 0, CHUNK)
             grad(t, CHUNK, FEATS)
 
-        keep_clock_up(384)
         spread_scale(0, "scalar")
         spread_scale(1, "scalar")
         cap_prepare(0)
-        keep_clock_up(128)
         for h in range(PASSES):
             widen(0, 0, CHUNK * h, CHUNK * (h + 1))
             widen(0, 1, CHUNK * h, CHUNK * (h + 1))
         cap_prepare(1)
-        keep_clock_up(128)
         aud_prepare(0, 0, [0])
         cap_prepare(2)
         aud_prepare(0, 0, [1])
         widen(0, 2)
         widen(0, 3)
         cap_prepare(3)
-        keep_clock_up(128)
         cap_quant(0)
         aud_quants(0, 0)
         cap_quant(1)

@@ -12,6 +12,7 @@ FP8 = mybir.dt.float8_e4m3fn
 FP8X4 = mybir.dt.float8_e4m3fn_x4
 FP4X4 = mybir.dt.float4_e2m1fn_x4
 MULT = mybir.AluOpType.mult
+ADD = mybir.AluOpType.add
 SIGMOID = mybir.ActivationFunctionType.Sigmoid
 
 CLIPS, CAPS, FEATS = 2048, 1024, 1024
@@ -21,6 +22,8 @@ HALF = CHUNK // 2
 CHUNKS = CLIPS // CHUNK
 PASSES = FEATS // CHUNK
 TILES = CAPS // P
+LAST = CHUNKS - 1
+DIRECT = TILES // 2 - 1
 
 FLOPS = 2 * 2 * CLIPS * CAPS * FEATS
 
@@ -41,16 +44,26 @@ def tile_siglip_negative_caption_gradient_s13_kernel(
         cap_one = [keep.tile([P, FEATS], BF16, name="cap_one%d" % t) for t in range(2)]
         cap_two = [keep.tile([P, 2 * FEATS], BF16, name="cap_two%d" % i) for i in range(1, TILES // 2)]
         weight_all = keep.tile([P, CLIPS], BF16, name="weight_all")
-        bias_cols = keep.tile([P, TILES], BF16, name="bias_cols")
+        bias_cols = keep.tile([P, TILES - 2], BF16, name="bias_cols")
         bank = keep.tile([P, CHUNKS, 2 * FEATS], U8, align_bytes=64, name="bank")
         bank_sc = keep.tile([P, CHUNKS, FEATS], U8, align_bytes=64, name="bank_sc")
         ident = keep.tile([P, P], F32, name="ident")
         aud_codes = [keep.tile([P, PASSES, CHUNK], U32, align_bytes=64, name="aud_codes%d" % g) for g in range(CHUNKS)]
         aud_planes = [keep.tile([P, PASSES, CHUNK], U8, align_bytes=64, name="aud_planes%d" % g) for g in range(CHUNKS)]
-        cap_codes = [keep.tile([P, PASSES * P], U32, align_bytes=64, name="cap_codes%d" % t) for t in range(TILES)]
-        cap_planes = [keep.tile([P, PASSES * P], U8, align_bytes=64, name="cap_planes%d" % t) for t in range(TILES)]
-        r_codes = [keep.tile([P, CHUNKS * P], U32, align_bytes=64, name="r_codes%d" % t) for t in range(TILES)]
-        r_planes = [keep.tile([P, CHUNKS * P], U8, align_bytes=64, name="r_planes%d" % t) for t in range(TILES)]
+        cap_own = [keep.tile([P, PASSES, P], U32, align_bytes=64, name="cap_codes%d" % t) for t in range(2 * DIRECT)]
+        cap_own_planes = [keep.tile([P, PASSES, P], U8, align_bytes=64, name="cap_planes%d" % t) for t in range(2 * DIRECT)]
+        cap_pair = keep.tile([P, PASSES, 2 * P], U32, align_bytes=64, name="cap_pair")
+        cap_pair_planes = keep.tile([P, PASSES, 2 * P], U8, align_bytes=64, name="cap_pair_planes")
+        bias_row = keep.tile([P, 2 * P], BF16, name="bias_row")
+        weight_cols = keep.tile([P, CHUNKS, 4], BF16, name="weight_cols")
+        r_operand = {}
+
+        def quantise_resid(name, src, owners):
+            codes = keep.tile([P, 2 * P], U32, align_bytes=64, name="r_codes_" + name)
+            planes = keep.tile([P, 2 * P], U8, align_bytes=64, name="r_planes_" + name)
+            nc.vector.quantize_mx(out=codes[:].bitcast(FP8X4), scales=planes[:], in_=src)
+            for n, owner in enumerate(owners):
+                r_operand[owner] = (codes[:, P * n : P * (n + 1)], planes[:, P * n : P * (n + 1)])
 
         ctx.enter_context(tc.manual_schedule())
 
@@ -61,33 +74,38 @@ def tile_siglip_negative_caption_gradient_s13_kernel(
         make_identity(nc, ident[:])
         nc.gpsimd.memset(bank_sc[:].rearrange("p g d -> p (g d)").bitcast(U32), 0)
 
-
         aud_view = audio_bytes.rearrange("(g q s) d -> g q (s d)", q=P, s=4)
-        cap_view = captions.rearrange("(p t) d -> p (t d)", t=TILES)
-        out_view = out.rearrange("(p t) d -> p t d", t=TILES)
+        cap_view = captions.rearrange("(i p s) d -> i p (s d)", p=P, s=2)
+        out_view = out.rearrange("(i p s) d -> i p s d", p=P, s=2)
 
         def load_cap_one(t):
-            nc.sync.dma_start(out=cap_one[t][:], in_=cap_view[:, t * FEATS : (t + 1) * FEATS])
+            nc.sync.dma_start(out=cap_one[t][:], in_=cap_view[0][:, t * FEATS : (t + 1) * FEATS])
 
         def load_cap_two(i):
-            nc.sync.dma_start(out=cap_two[i - 1][:], in_=cap_view[:, 2 * i * FEATS : 2 * (i + 1) * FEATS])
+            nc.sync.dma_start(out=cap_two[i - 1][:], in_=cap_view[i])
+
+        def load_cap_direct():
+            rows = captions[2 * P * DIRECT :, :].rearrange("(s p) d -> p s d", p=P)
+            nc.sync.dma_start(out=cap_two[DIRECT - 1][:].rearrange("p (s d) -> p s d", s=2), in_=rows)
 
         def load_raw_first(a):
             nc.sync.dma_start(out=raw_first[a][:], in_=aud_view[0][:, 2 * a * FEATS : 2 * (a + 1) * FEATS])
 
         nc.sync.dma_start(out=scale_cols[:], in_=audio_scale.rearrange("o (h n m) -> n (o h) m", h=PASSES, m=4))
-        load_cap_one(0)
         load_raw_first(0)
+        load_cap_one(0)
         load_cap_one(1)
         load_cap_two(1)
         load_raw_first(1)
-        nc.sync.dma_start(out=bias_cols[:], in_=bias.rearrange("(p t) -> p t", t=TILES))
+        nc.sync.dma_start(out=bias_cols[:].rearrange("p (i s) -> p i s", s=2), in_=bias[: 2 * P * DIRECT].rearrange("(i p s) -> p i s", p=P, s=2))
         load_cap_two(2)
         nc.sync.dma_start(out=raw_later[0][:], in_=aud_view[1])
-        load_cap_two(3)
         nc.sync.dma_start(out=raw_later[1][:], in_=aud_view[2])
         nc.sync.dma_start(out=raw_later[2][:], in_=aud_view[3])
+        load_cap_direct()
         nc.sync.dma_start(out=weight_all[:], in_=clip_weight.partition_broadcast(P))
+        nc.sync.dma_start(out=bias_row[:], in_=bias[2 * P * DIRECT :].partition_broadcast(P))
+        nc.sync.dma_start(out=weight_cols[:], in_=clip_weight.rearrange("(g p t) -> p g t", p=P, t=4))
         nc.sync.dma_start(out=bank[:], in_=bank_words.rearrange("g p n -> p g n"))
         for q in range(4):
             nc.sync.dma_start(
@@ -111,21 +129,25 @@ def tile_siglip_negative_caption_gradient_s13_kernel(
             else:
                 nc.scalar.copy(out=dst, in_=src)
 
-        def spread_scale(h, engine):
-            xt = psum.tile([P, 4, P], F32, tag="bank", name="spread")
-            for m in range(4):
-                nc.tensor.transpose(xt[:, m, :], scale_cols[:, h, m : m + 1].to_broadcast([P, P]), ident[:])
-            copy_out(engine, scale_all[:, CHUNK * h : CHUNK * (h + 1)].rearrange("p (n m) -> p n m", m=4), xt[:].rearrange("p m n -> p n m"))
-
         turned = {}
         grouped = {}
 
+        def spread_turn(h):
+            xt = psum.tile([P, 4, P], F32, tag="bank", name="spread")
+            for m in range(4):
+                nc.tensor.transpose(xt[:, m, :], scale_cols[:, h, m : m + 1].to_broadcast([P, P]), ident[:])
+            turned["scale", h] = xt
+
+        def spread_exit(h, engine="scalar"):
+            copy_out(engine, scale_all[:, CHUNK * h : CHUNK * (h + 1)].rearrange("p (n m) -> p n m", m=4), turned["scale", h][:].rearrange("p m n -> p n m"))
+
+
         def cap_turn(t):
             xt = psum.tile([P, PASSES, 2, P], F32, tag="bank", name="cap_xt")
-            words = cap_words(t)
             for h in range(PASSES):
                 for u in range(2):
-                    nc.tensor.transpose(xt[:, h, u, :], words[:, 256 * h + u : 256 * (h + 1) : 2], ident[:])
+                    src = cap_words(t)[:, 256 * h + u : 256 * (h + 1) : 2]
+                    nc.tensor.transpose(xt[:, h, u, :], src, ident[:])
             turned["cap", t] = xt
 
         def cap_exit(t, engine="scalar"):
@@ -137,10 +159,22 @@ def tile_siglip_negative_caption_gradient_s13_kernel(
             )
 
         def cap_quant(t):
-            nc.vector.quantize_mx(out=cap_codes[t][:].bitcast(FP8X4), scales=cap_planes[t][:], in_=grouped["cap", t][:])
+            if t < 2 * DIRECT:
+                nc.vector.quantize_mx(
+                    out=cap_own[t][:].rearrange("p h j -> p (h j)").bitcast(FP8X4),
+                    scales=cap_own_planes[t][:].rearrange("p h j -> p (h j)"),
+                    in_=grouped["cap", t][:],
+                )
+                return
+            cols = slice(P * (t % 2), P * (t % 2 + 1))
+            for h in range(PASSES):
+                nc.vector.quantize_mx(
+                    out=cap_pair[:, h, cols].bitcast(FP8X4),
+                    scales=cap_pair_planes[:, h, cols],
+                    in_=grouped["cap", t][:, CHUNK * h : CHUNK * (h + 1)],
+                )
 
         audio = {}
-        ordered = set()
 
         def widen(g, s, first=0, end=FEATS):
             if (g, s) not in audio:
@@ -149,24 +183,12 @@ def tile_siglip_negative_caption_gradient_s13_kernel(
                 out=audio[g, s][:, first:end], in0=raw_slot(g, s)[:, first:end].bitcast(FP8), in1=scale_all[:, first:end], op=MULT
             )
 
-        def sort(g, s):
-            flat = work.tile([P, FEATS], BF16, align_bytes=64, tag="sorted", name="flat", bufs=4)
-            nc.vector.tensor_copy(
-                out=flat[:].bitcast(F32).rearrange("p (u w) -> p u w", u=2),
-                in_=audio[g, s][:].bitcast(F32).rearrange("p (w u) -> p u w", u=2),
-            )
-            audio[g, s] = flat
-            ordered.add((g, s))
-
         def aud_turn(g, a, h):
             xt = psum.tile([P, 2, 2, P], F32, tag="bank", name="aud_xt")
             for e in range(2):
                 words = audio[g, 2 * a + e][:].bitcast(F32)
                 for u in range(2):
-                    if (g, 2 * a + e) in ordered:
-                        src = words[:, 256 * u + P * h : 256 * u + P * (h + 1)]
-                    else:
-                        src = words[:, 256 * h + u : 256 * (h + 1) : 2]
+                    src = words[:, 256 * h + u : 256 * (h + 1) : 2]
                     nc.tensor.transpose(xt[:, e, u, :], src, ident[:])
             turned["aud", g, a, h] = xt
 
@@ -175,9 +197,10 @@ def tile_siglip_negative_caption_gradient_s13_kernel(
             grouped[key] = work.tile([P, 1024], BF16, align_bytes=64, tag="grouped", name="aud_grouped", bufs=9)
             copy_out(
                 engine,
-                grouped[key][:].bitcast(F32).rearrange("p (q e u) -> p q e u", e=2, u=2),
-                turned[key][:].rearrange("p e u q -> p q e u"),
+                grouped[key][:].bitcast(F32).rearrange("p (e q u) -> p e q u", e=2, u=2),
+                turned[key][:].rearrange("p e u q -> p e q u"),
             )
+
 
         def aud_quant(g, a, h):
             cols = slice(HALF * a, HALF * (a + 1))
@@ -194,8 +217,8 @@ def tile_siglip_negative_caption_gradient_s13_kernel(
             for h in range(PASSES):
                 nc.tensor.matmul_mx(
                     out=sums[t, g][:],
-                    lhsT=cap_codes[t][:, P * h : P * (h + 1)].bitcast(FP8X4),
-                    lhsT_scale=cap_planes[t][:, P * h : P * (h + 1)],
+                    lhsT=cap_own[t][:, h, :].bitcast(FP8X4),
+                    lhsT_scale=cap_own_planes[t][:, h, :],
                     rhs=aud_codes[g][:, h, first:end].bitcast(FP8X4),
                     rhs_scale=aud_planes[g][:, h, first:end],
                     start=(h == 0),
@@ -205,8 +228,13 @@ def tile_siglip_negative_caption_gradient_s13_kernel(
         def sigmoid(t, g, first=0, end=CHUNK):
             pair = g // 2
             if (t, pair) not in sigs:
-                sigs[t, pair] = work.tile([P, 2, CHUNK], F32, tag="sig", name="sig", bufs=16)
-            nc.scalar.activation(out=sigs[t, pair][:, g % 2, first:end], in_=sums[t, g][:], func=SIGMOID, bias=bias_cols[:, t : t + 1])
+                sigs[t, pair] = work.tile([P, 2, CHUNK], F32, tag="sig", name="sig", bufs=12)
+            nc.scalar.activation(
+                out=sigs[t, pair][:, g % 2, first:end].rearrange("p (a q e) -> p a q e", q=P, e=2),
+                in_=sums[t, g][:].rearrange("p (a e q) -> p a q e", q=P, e=2),
+                func=SIGMOID,
+                bias=bias_cols[:, t : t + 1],
+            )
 
         def weigh(t, pair):
             resids[t, pair] = work.tile([P, 2 * CHUNK], BF16, align_bytes=64, tag="resid", name="resid", bufs=9)
@@ -236,25 +264,82 @@ def tile_siglip_negative_caption_gradient_s13_kernel(
             )
 
         def r_quant(t, pair):
-            cols = slice(2 * P * pair, 2 * P * (pair + 1))
-            nc.vector.quantize_mx(out=r_codes[t][:, cols].bitcast(FP8X4), scales=r_planes[t][:, cols], in_=grouped["r", t, pair][:])
+            quantise_resid("%d_%d" % (t, pair), grouped["r", t, pair][:], [(t, 2 * pair), (t, 2 * pair + 1)])
 
-        def grad(t, first, end, engine="scalar"):
+        direct = {}
+
+        def direct_logits(g, a):
+            acc = psum.tile([P, 2, HALF], F32, tag="bank", name="direct_sum")
+            for e in range(2):
+                cols = slice(HALF * a + P * e, HALF * a + P * (e + 1))
+                for h in range(PASSES):
+                    nc.tensor.matmul_mx(
+                        out=acc[:, e, :],
+                        lhsT=aud_codes[g][:, h, cols].bitcast(FP8X4),
+                        lhsT_scale=aud_planes[g][:, h, cols],
+                        rhs=cap_pair[:, h, :].bitcast(FP8X4),
+                        rhs_scale=cap_pair_planes[:, h, :],
+                        start=(h == 0),
+                        stop=(h == PASSES - 1),
+                    )
+            direct["sum", g, a] = acc
+
+        def direct_bias(g, a):
+            biased = work.tile([P, 2, HALF], F32, tag="biased", name="biased", bufs=4)
+            nc.vector.tensor_tensor(
+                out=biased[:], in0=direct["sum", g, a][:], in1=bias_row[:].unsqueeze(1).to_broadcast([P, 2, HALF]), op=ADD
+            )
+            direct["biased", g, a] = biased
+
+        def direct_sigmoid(g, a):
+            prob = work.tile([P, 2, HALF], F32, tag="prob", name="prob", bufs=6)
+            nc.scalar.activation(out=prob[:], in_=direct["biased", g, a][:], func=SIGMOID)
+            direct["prob", g, a] = prob
+
+        def direct_weigh(g, a):
+            if a == 0:
+                direct["planes", g] = work.tile([P, 4, HALF], BF16, align_bytes=64, tag="resid", name="planes", bufs=9)
+            for e in range(2):
+                nc.vector.tensor_scalar(
+                    out=direct["planes", g][:, 2 * a + e, :],
+                    in0=direct["prob", g, a][:, e, :],
+                    scalar1=weight_cols[:, g, 2 * a + e : 2 * a + e + 1],
+                    scalar2=None,
+                    op0=MULT,
+                )
+
+        def direct_group(g, engine="scalar"):
+            grouped["direct", g] = work.tile([P, 1024], BF16, align_bytes=64, tag="grouped", name="d_grouped", bufs=9)
+            copy_out(engine, grouped["direct", g][:].rearrange("p (j t) -> p j t", t=4), direct["planes", g][:].rearrange("p t j -> p j t"))
+
+        def direct_quant(g):
+            quantise_resid("direct_%d" % g, grouped["direct", g][:], [(2 * DIRECT, g), (2 * DIRECT + 1, g)])
+
+        def grad_sum(t, first, end):
             acc = psum.tile([P, end - first], F32, tag="bank", name="grad_sum")
             for g in range(CHUNKS):
                 nc.tensor.matmul_mx(
                     out=acc[:],
-                    lhsT=r_codes[t][:, P * g : P * (g + 1)].bitcast(FP8X4),
-                    lhsT_scale=r_planes[t][:, P * g : P * (g + 1)],
+                    lhsT=r_operand[t, g][0].bitcast(FP8X4),
+                    lhsT_scale=r_operand[t, g][1],
                     rhs=bank[:, g, 2 * first : 2 * end].bitcast(FP4X4),
                     rhs_scale=bank_sc[:, g, first:end],
                     start=(g == 0),
                     stop=(g == CHUNKS - 1),
                 )
+            sums["grad", t, first] = acc
+
+        def store(t, first, end, engine="scalar"):
+            acc = sums["grad", t, first]
             tag = "res" if end - first == CHUNK else "res_part"
-            res = work.tile([P, end - first], F32, tag=tag, name="res", bufs=4)
+            res = work.tile([P, end - first], F32, tag=tag, name="res", bufs=5)
             copy_out(engine, res[:], acc[:])
-            nc.sync.dma_start(out=out_view[:, t, first:end], in_=res[:])
+            rows = out_view[t // 2][:, t % 2, :] if t // 2 < DIRECT else out[P * t : P * (t + 1), :]
+            nc.sync.dma_start(out=rows[:, first:end], in_=res[:])
+
+        def grad(t, first, end, engine="scalar"):
+            grad_sum(t, first, end)
+            store(t, first, end, engine)
 
         def cap_prepare(t):
             cap_turn(t)
@@ -287,8 +372,14 @@ def tile_siglip_negative_caption_gradient_s13_kernel(
             grad(t, 0, CHUNK)
             grad(t, CHUNK, FEATS)
 
-        spread_scale(0, "scalar")
-        spread_scale(1, "scalar")
+        def both(step, g):
+            for a in range(2):
+                step(g, a)
+
+        spread_turn(0)
+        spread_exit(0, "vector")
+        spread_turn(1)
+        spread_exit(1)
         cap_prepare(0)
         for h in range(PASSES):
             widen(0, 0, CHUNK * h, CHUNK * (h + 1))
@@ -305,7 +396,6 @@ def tile_siglip_negative_caption_gradient_s13_kernel(
         cap_quant(1)
         cap_prepare(4)
         aud_prepare(0, 1)
-        cap_prepare(5)
         cap_quant(2)
         probs(range(3), 0, 0, HALF)
         widen(1, 0)
@@ -315,81 +405,90 @@ def tile_siglip_negative_caption_gradient_s13_kernel(
         probs(range(3), 0, HALF, CHUNK)
         probs([3], 0)
         cap_quant(4)
+        widen(1, 2)
+        cap_prepare(5)
+        aud_prepare(1, 0)
+        widen(1, 3)
         cap_quant(5)
+        probs([4], 0)
+        aud_prepare(1, 1)
         cap_prepare(6)
         cap_prepare(7)
-        aud_prepare(1, 0)
-        widen(1, 2)
-        widen(1, 3)
-        probs(range(4, 6), 0)
         aud_quants(1, 0)
-        cap_quant(6)
-        cap_quant(7)
-        aud_prepare(1, 1)
         widen(2, 0)
-        probs(range(4), 1, 0, HALF)
         aud_quants(1, 1)
         widen(2, 1)
-        probs(range(6, 8), 0)
-        widen(2, 2)
-        widen(2, 3)
-        probs(range(4), 1, HALF, CHUNK)
-        aud_prepare(2, 0)
-        aud_prepare(2, 1)
-        widen(3, 0)
-        widen(3, 1)
-        aud_quants(2, 0)
-        aud_quants(2, 1)
-        probs(range(4, 8), 1)
-        sort(3, 0)
-        sort(3, 1)
-        widen(3, 2)
-        widen(3, 3)
-        probs(range(4), 2)
-        weigh(0, 0)
-        aud_turn(3, 0, 0)
-        aud_exit(3, 0, 0, "vector")
-        aud_turn(3, 0, 1)
-        aud_exit(3, 0, 1)
-        aud_turn(3, 1, 0)
-        aud_turn(3, 1, 1)
-        aud_exit(3, 1, 0, "vector")
-        aud_exit(3, 1, 1)
-        aud_quants(3, 0)
-        aud_quants(3, 1)
-        weigh(1, 0)
-        probs(range(4, 8), 2)
+        probs([5], 0)
 
-        last = CHUNKS - 1
+        for g in range(2, CHUNKS):
+            widen(g, 2)
+            widen(g, 3)
+            probs(range(3), g - 1)
+            both(aud_prepare, g)
+            if g < LAST:
+                widen(g + 1, 0)
+                aud_quants(g, 0)
+                widen(g + 1, 1, 0, CHUNK)
+                aud_quants(g, 1)
+                widen(g + 1, 1, CHUNK, FEATS)
+            else:
+                weigh(0, 0)
+                cap_quant(6)
+                cap_quant(7)
+                both(aud_quants, g)
+                weigh(1, 0)
+            probs(range(3, 6), g - 1)
+
         weigh(2, 0)
-        probs(range(4), last)
+        probs(range(4), LAST)
         weigh(0, 1)
         weigh(1, 1)
-        probs([4], last)
-        for pair in range(2):
-            for t in range(2):
-                r_turn(t, pair)
-                r_exit(t, pair)
+        both(direct_logits, 0)
+        turns(0)
+        turns(1)
         weigh(2, 1)
-        probs(range(5, 8), last)
         quants(0)
+        probs(range(4, 6), LAST)
         weigh(3, 0)
-        quants(1)
         weigh(3, 1)
+        quants(1)
+        both(direct_bias, 0)
         grads(0)
-        for t in range(2, TILES, 2):
-            turns(t)
-            turns(t + 1)
-            if t + 2 < TILES:
-                weigh(t + 2, 0)
-            quants(t)
-            if t + 2 < TILES:
-                weigh(t + 2, 1)
-            quants(t + 1)
-            grads(t - 1)
-            if t + 2 < TILES:
-                weigh(t + 3, 0)
-                weigh(t + 3, 1)
+
+        turns(2)
+        turns(3)
+        weigh(4, 0)
+        quants(2)
+        weigh(4, 1)
+        grads(1)
+        both(direct_sigmoid, 0)
+        weigh(5, 0)
+        weigh(5, 1)
+        grads(2)
+        turns(4)
+        turns(5)
+        quants(3)
+        both(direct_weigh, 0)
+        for g in range(1, CHUNKS):
+            both(direct_logits, g)
+            if g == LAST:
+                quants(4)
+            both(direct_bias, g)
+            both(direct_sigmoid, g)
+        direct_group(0, "vector")
+        both(direct_weigh, 1)
+        direct_quant(0)
+        grad(3, 0, CHUNK)
+        direct_group(1)
+        both(direct_weigh, 2)
+        grad(3, CHUNK, FEATS)
+        direct_group(2)
+        quants(5)
+        both(direct_weigh, 3)
+        direct_group(3, "vector")
+        for g in range(1, CHUNKS):
+            direct_quant(g)
+        for t in range(4, TILES - 1):
             grads(t)
         grad(TILES - 1, 0, CHUNK)
         grad(TILES - 1, CHUNK, CHUNK + HALF, "vector")

@@ -423,8 +423,14 @@ def tile_siglip_negative_caption_gradient_s13_kernel(
         for g in range(2, CHUNKS):
             widen(g, 2)
             widen(g, 3)
-            probs(range(3), g - 1)
-            both(aud_prepare, g)
+            if g == 2:
+                probs(range(2), g - 1)
+                aud_prepare(g, 0)
+                probs(range(2, 3), g - 1)
+                aud_prepare(g, 1)
+            else:
+                probs(range(3), g - 1)
+                both(aud_prepare, g)
             if g < LAST:
                 widen(g + 1, 0)
                 aud_quants(g, 0)

@@ -92,17 +92,17 @@ def tile_siglip_negative_caption_gradient_s13_kernel(
             nc.sync.dma_start(out=raw_first[a][:], in_=aud_view[0][:, 2 * a * FEATS : 2 * (a + 1) * FEATS])
 
         nc.sync.dma_start(out=scale_cols[:], in_=audio_scale.rearrange("o (h n m) -> n (o h) m", h=PASSES, m=4))
-        load_raw_first(0)
         load_cap_one(0)
+        load_raw_first(0)
         load_cap_one(1)
         load_cap_two(1)
         load_raw_first(1)
         nc.sync.dma_start(out=bias_cols[:].rearrange("p (i s) -> p i s", s=2), in_=bias[: 2 * P * DIRECT].rearrange("(i p s) -> p i s", p=P, s=2))
         load_cap_two(2)
         nc.sync.dma_start(out=raw_later[0][:], in_=aud_view[1])
+        load_cap_direct()
         nc.sync.dma_start(out=raw_later[1][:], in_=aud_view[2])
         nc.sync.dma_start(out=raw_later[2][:], in_=aud_view[3])
-        load_cap_direct()
         nc.sync.dma_start(out=weight_all[:], in_=clip_weight.partition_broadcast(P))
         nc.sync.dma_start(out=bias_row[:], in_=bias[2 * P * DIRECT :].partition_broadcast(P))
         nc.sync.dma_start(out=weight_cols[:], in_=clip_weight.rearrange("(g p t) -> p g t", p=P, t=4))
@@ -138,8 +138,9 @@ def tile_siglip_negative_caption_gradient_s13_kernel(
                 nc.tensor.transpose(xt[:, m, :], scale_cols[:, h, m : m + 1].to_broadcast([P, P]), ident[:])
             turned["scale", h] = xt
 
-        def spread_exit(h, engine="scalar"):
-            copy_out(engine, scale_all[:, CHUNK * h : CHUNK * (h + 1)].rearrange("p (n m) -> p n m", m=4), turned["scale", h][:].rearrange("p m n -> p n m"))
+        def spread_exit(h, engine="scalar", first=0, end=P):
+            dst = scale_all[:, CHUNK * h + 4 * first : CHUNK * h + 4 * end].rearrange("p (n m) -> p n m", m=4)
+            copy_out(engine, dst, turned["scale", h][:, :, first:end].rearrange("p m n -> p n m"))
 
 
         def cap_turn(t):
@@ -332,7 +333,7 @@ def tile_siglip_negative_caption_gradient_s13_kernel(
         def store(t, first, end, engine="scalar"):
             acc = sums["grad", t, first]
             tag = "res" if end - first == CHUNK else "res_part"
-            res = work.tile([P, end - first], F32, tag=tag, name="res", bufs=5)
+            res = work.tile([P, end - first], F32, tag=tag, name="res", bufs=6)
             copy_out(engine, res[:], acc[:])
             rows = out_view[t // 2][:, t % 2, :] if t // 2 < DIRECT else out[P * t : P * (t + 1), :]
             nc.sync.dma_start(out=rows[:, first:end], in_=res[:])
@@ -377,13 +378,14 @@ def tile_siglip_negative_caption_gradient_s13_kernel(
                 step(g, a)
 
         spread_turn(0)
-        spread_exit(0, "vector")
+        spread_exit(0, "scalar", 0, 48)
+        spread_exit(0, "scalar", 48, P)
         spread_turn(1)
         spread_exit(1)
         cap_prepare(0)
-        for h in range(PASSES):
-            widen(0, 0, CHUNK * h, CHUNK * (h + 1))
-            widen(0, 1, CHUNK * h, CHUNK * (h + 1))
+        for first, end in ((0, 192), (192, CHUNK), (CHUNK, FEATS)):
+            widen(0, 0, first, end)
+            widen(0, 1, first, end)
         cap_prepare(1)
         aud_prepare(0, 0, [0])
         cap_prepare(2)
@@ -396,6 +398,7 @@ def tile_siglip_negative_caption_gradient_s13_kernel(
         cap_quant(1)
         cap_prepare(4)
         aud_prepare(0, 1)
+        cap_prepare(5)
         cap_quant(2)
         probs(range(3), 0, 0, HALF)
         widen(1, 0)
@@ -406,7 +409,6 @@ def tile_siglip_negative_caption_gradient_s13_kernel(
         probs([3], 0)
         cap_quant(4)
         widen(1, 2)
-        cap_prepare(5)
         aud_prepare(1, 0)
         widen(1, 3)
         cap_quant(5)
@@ -475,25 +477,26 @@ def tile_siglip_negative_caption_gradient_s13_kernel(
         turns(5)
         quants(3)
         both(direct_weigh, 0)
+        direct_group(0, "vector")
         for g in range(1, CHUNKS):
             both(direct_logits, g)
             if g == LAST:
                 quants(4)
+                direct_quant(0)
             both(direct_bias, g)
             both(direct_sigmoid, g)
-        direct_group(0, "vector")
         both(direct_weigh, 1)
-        direct_quant(0)
         grad(3, 0, CHUNK)
         direct_group(1)
         both(direct_weigh, 2)
-        grad(3, CHUNK, FEATS)
-        direct_group(2)
         quants(5)
+        direct_group(2, "vector")
         both(direct_weigh, 3)
+        direct_quant(1)
         direct_group(3, "vector")
-        for g in range(1, CHUNKS):
-            direct_quant(g)
+        direct_quant(2)
+        direct_quant(3)
+        grad(3, CHUNK, FEATS)
         for t in range(4, TILES - 1):
             grads(t)
         grad(TILES - 1, 0, CHUNK)

@@ -293,25 +293,21 @@ def tile_siglip_negative_caption_gradient_s13_kernel(
             direct["biased", g, a] = biased
 
         def direct_sigmoid(g, a):
-            prob = work.tile([P, 2, HALF], F32, tag="prob", name="prob", bufs=6)
-            nc.scalar.activation(out=prob[:], in_=direct["biased", g, a][:], func=SIGMOID)
-            direct["prob", g, a] = prob
-
-        def direct_weigh(g, a):
             if a == 0:
-                direct["planes", g] = work.tile([P, 4, HALF], BF16, align_bytes=64, tag="resid", name="planes", bufs=9)
-            for e in range(2):
-                nc.vector.tensor_scalar(
-                    out=direct["planes", g][:, 2 * a + e, :],
-                    in0=direct["prob", g, a][:, e, :],
-                    scalar1=weight_cols[:, g, 2 * a + e : 2 * a + e + 1],
-                    scalar2=None,
-                    op0=MULT,
-                )
+                direct["prob", g] = work.tile([P, 2, HALF, 2], F32, tag="prob", name="prob", bufs=3)
+            nc.scalar.activation(
+                out=direct["prob", g][:, a, :, :], in_=direct["biased", g, a][:].rearrange("p e j -> p j e"), func=SIGMOID
+            )
 
-        def direct_group(g, engine="scalar"):
+        def direct_weigh(g):
             grouped["direct", g] = work.tile([P, 1024], BF16, align_bytes=64, tag="grouped", name="d_grouped", bufs=9)
-            copy_out(engine, grouped["direct", g][:].rearrange("p (j t) -> p j t", t=4), direct["planes", g][:].rearrange("p t j -> p j t"))
+            weights = weight_cols[:, g, :].rearrange("p (a e) -> p a e", a=2).unsqueeze(1)
+            nc.vector.tensor_tensor(
+                out=grouped["direct", g][:].rearrange("p (j a e) -> p j a e", a=2, e=2),
+                in0=direct["prob", g][:].rearrange("p a j e -> p j a e"),
+                in1=weights.to_broadcast([P, HALF, 2, 2]),
+                op=MULT,
+            )
 
         def direct_quant(g):
             quantise_resid("direct_%d" % g, grouped["direct", g][:], [(2 * DIRECT, g), (2 * DIRECT + 1, g)])
@@ -476,8 +472,7 @@ def tile_siglip_negative_caption_gradient_s13_kernel(
         turns(4)
         turns(5)
         quants(3)
-        both(direct_weigh, 0)
-        direct_group(0, "vector")
+        direct_weigh(0)
         for g in range(1, CHUNKS):
             both(direct_logits, g)
             if g == LAST:
@@ -485,19 +480,13 @@ def tile_siglip_negative_caption_gradient_s13_kernel(
                 direct_quant(0)
             both(direct_bias, g)
             both(direct_sigmoid, g)
-        both(direct_weigh, 1)
-        grad(3, 0, CHUNK)
-        direct_group(1)
-        both(direct_weigh, 2)
+        direct_weigh(1)
         quants(5)
-        direct_group(2, "vector")
-        both(direct_weigh, 3)
-        direct_quant(1)
-        direct_group(3, "vector")
-        direct_quant(2)
-        direct_quant(3)
-        grad(3, CHUNK, FEATS)
-        for t in range(4, TILES - 1):
+        for g in range(2, CHUNKS):
+            direct_weigh(g)
+            direct_quant(g - 1)
+        direct_quant(LAST)
+        for t in range(3, TILES - 1):
             grads(t)
         grad(TILES - 1, 0, CHUNK)
         grad(TILES - 1, CHUNK, CHUNK + HALF, "vector")

@@ -23,7 +23,7 @@ CHUNKS = CLIPS // CHUNK
 PASSES = FEATS // CHUNK
 TILES = CAPS // P
 LAST = CHUNKS - 1
-DIRECT = TILES // 2 - 1
+TURNED = TILES - 2
 
 FLOPS = 2 * 2 * CLIPS * CAPS * FEATS
 
@@ -41,17 +41,16 @@ def tile_siglip_negative_caption_gradient_s13_kernel(
         scale_all = keep.tile([P, FEATS], F32, name="scale_all")
         raw_first = [keep.tile([P, 2 * FEATS], U8, name="raw_first%d" % a) for a in range(2)]
         raw_later = [keep.tile([P, 4 * FEATS], U8, name="raw_later%d" % g) for g in range(1, CHUNKS)]
-        cap_one = [keep.tile([P, FEATS], BF16, name="cap_one%d" % t) for t in range(2)]
-        cap_two = [keep.tile([P, 2 * FEATS], BF16, name="cap_two%d" % i) for i in range(1, TILES // 2)]
+        cap_one = [keep.tile([P, FEATS], BF16, name="cap_one%d" % t) for t in range(TILES)]
         weight_all = keep.tile([P, CLIPS], BF16, name="weight_all")
-        bias_cols = keep.tile([P, TILES - 2], BF16, name="bias_cols")
+        bias_cols = keep.tile([P, TURNED], BF16, name="bias_cols")
         bank = keep.tile([P, CHUNKS, 2 * FEATS], U8, align_bytes=64, name="bank")
         bank_sc = keep.tile([P, CHUNKS, FEATS], U8, align_bytes=64, name="bank_sc")
         ident = keep.tile([P, P], F32, name="ident")
         aud_codes = [keep.tile([P, PASSES, CHUNK], U32, align_bytes=64, name="aud_codes%d" % g) for g in range(CHUNKS)]
         aud_planes = [keep.tile([P, PASSES, CHUNK], U8, align_bytes=64, name="aud_planes%d" % g) for g in range(CHUNKS)]
-        cap_own = [keep.tile([P, PASSES, P], U32, align_bytes=64, name="cap_codes%d" % t) for t in range(2 * DIRECT)]
-        cap_own_planes = [keep.tile([P, PASSES, P], U8, align_bytes=64, name="cap_planes%d" % t) for t in range(2 * DIRECT)]
+        cap_own = [keep.tile([P, PASSES, P], U32, align_bytes=64, name="cap_codes%d" % t) for t in range(TURNED)]
+        cap_own_planes = [keep.tile([P, PASSES, P], U8, align_bytes=64, name="cap_planes%d" % t) for t in range(TURNED)]
         cap_pair = keep.tile([P, PASSES, 2 * P], U32, align_bytes=64, name="cap_pair")
         cap_pair_planes = keep.tile([P, PASSES, 2 * P], U8, align_bytes=64, name="cap_pair_planes")
         bias_row = keep.tile([P, 2 * P], BF16, name="bias_row")
@@ -75,36 +74,33 @@ def tile_siglip_negative_caption_gradient_s13_kernel(
         nc.gpsimd.memset(bank_sc[:].rearrange("p g d -> p (g d)").bitcast(U32), 0)
 
         aud_view = audio_bytes.rearrange("(g q s) d -> g q (s d)", q=P, s=4)
-        cap_view = captions.rearrange("(i p s) d -> i p (s d)", p=P, s=2)
-        out_view = out.rearrange("(i p s) d -> i p s d", p=P, s=2)
+        cap_view = captions[: P * TURNED, :].rearrange("(p t) d -> p t d", t=TURNED)
+        out_view = out[: P * TURNED, :].rearrange("(p t) d -> p t d", t=TURNED)
 
-        def load_cap_one(t):
-            nc.sync.dma_start(out=cap_one[t][:], in_=cap_view[0][:, t * FEATS : (t + 1) * FEATS])
-
-        def load_cap_two(i):
-            nc.sync.dma_start(out=cap_two[i - 1][:], in_=cap_view[i])
-
-        def load_cap_direct():
-            rows = captions[2 * P * DIRECT :, :].rearrange("(s p) d -> p s d", p=P)
-            nc.sync.dma_start(out=cap_two[DIRECT - 1][:].rearrange("p (s d) -> p s d", s=2), in_=rows)
+        def load_cap(t):
+            rows = cap_view[:, t, :] if t < TURNED else captions[P * t : P * (t + 1), :]
+            nc.sync.dma_start(out=cap_one[t][:], in_=rows)
 
         def load_raw_first(a):
             nc.sync.dma_start(out=raw_first[a][:], in_=aud_view[0][:, 2 * a * FEATS : 2 * (a + 1) * FEATS])
 
         nc.sync.dma_start(out=scale_cols[:], in_=audio_scale.rearrange("o (h n m) -> n (o h) m", h=PASSES, m=4))
-        load_cap_one(0)
+        load_cap(0)
         load_raw_first(0)
-        load_cap_one(1)
-        load_cap_two(1)
+        load_cap(1)
+        load_cap(2)
         load_raw_first(1)
-        nc.sync.dma_start(out=bias_cols[:].rearrange("p (i s) -> p i s", s=2), in_=bias[: 2 * P * DIRECT].rearrange("(i p s) -> p i s", p=P, s=2))
-        load_cap_two(2)
+        load_cap(3)
+        load_cap(4)
         nc.sync.dma_start(out=raw_later[0][:], in_=aud_view[1])
-        load_cap_direct()
+        load_cap(5)
+        nc.sync.dma_start(out=bias_cols[:], in_=bias[: P * TURNED].rearrange("(p t) -> p t", t=TURNED))
+        load_cap(6)
+        load_cap(7)
         nc.sync.dma_start(out=raw_later[1][:], in_=aud_view[2])
         nc.sync.dma_start(out=raw_later[2][:], in_=aud_view[3])
         nc.sync.dma_start(out=weight_all[:], in_=clip_weight.partition_broadcast(P))
-        nc.sync.dma_start(out=bias_row[:], in_=bias[2 * P * DIRECT :].partition_broadcast(P))
+        nc.sync.dma_start(out=bias_row[:], in_=bias[P * TURNED :].partition_broadcast(P))
         nc.sync.dma_start(out=weight_cols[:], in_=clip_weight.rearrange("(g p t) -> p g t", p=P, t=4))
         nc.sync.dma_start(out=bank[:], in_=bank_words.rearrange("g p n -> p g n"))
         for q in range(4):
@@ -114,9 +110,7 @@ def tile_siglip_negative_caption_gradient_s13_kernel(
             )
 
         def cap_words(t):
-            if t < 2:
-                return cap_one[t][:].bitcast(F32)
-            return cap_two[t // 2 - 1][:, (t % 2) * FEATS : (t % 2 + 1) * FEATS].bitcast(F32)
+            return cap_one[t][:].bitcast(F32)
 
         def raw_slot(g, s):
             if g == 0:
@@ -160,7 +154,7 @@ def tile_siglip_negative_caption_gradient_s13_kernel(
             )
 
         def cap_quant(t):
-            if t < 2 * DIRECT:
+            if t < TURNED:
                 nc.vector.quantize_mx(
                     out=cap_own[t][:].rearrange("p h j -> p (h j)").bitcast(FP8X4),
                     scales=cap_own_planes[t][:].rearrange("p h j -> p (h j)"),
@@ -310,7 +304,7 @@ def tile_siglip_negative_caption_gradient_s13_kernel(
             )
 
         def direct_quant(g):
-            quantise_resid("direct_%d" % g, grouped["direct", g][:], [(2 * DIRECT, g), (2 * DIRECT + 1, g)])
+            quantise_resid("direct_%d" % g, grouped["direct", g][:], [(TURNED, g), (TURNED + 1, g)])
 
         def grad_sum(t, first, end):
             acc = psum.tile([P, end - first], F32, tag="bank", name="grad_sum")
@@ -331,7 +325,7 @@ def tile_siglip_negative_caption_gradient_s13_kernel(
             tag = "res" if end - first == CHUNK else "res_part"
             res = work.tile([P, end - first], F32, tag=tag, name="res", bufs=6)
             copy_out(engine, res[:], acc[:])
-            rows = out_view[t // 2][:, t % 2, :] if t // 2 < DIRECT else out[P * t : P * (t + 1), :]
+            rows = out_view[:, t, :] if t < TURNED else out[P * t : P * (t + 1), :]
             nc.sync.dma_start(out=rows[:, first:end], in_=res[:])
 
         def grad(t, first, end, engine="scalar"):

@@ -20,10 +20,12 @@ P = 128
 CHUNK = 512
 HALF = CHUNK // 2
 CHUNKS = CLIPS // CHUNK
+LAST = CHUNKS - 1
 PASSES = FEATS // CHUNK
 TILES = CAPS // P
-LAST = CHUNKS - 1
 TURNED = TILES - 2
+GROUP = TURNED // 2
+WIDE = 4 * HALF
 
 FLOPS = 2 * 2 * CLIPS * CAPS * FEATS
 
@@ -41,28 +43,20 @@ def tile_siglip_negative_caption_gradient_s13_kernel(
         scale_all = keep.tile([P, FEATS], F32, name="scale_all")
         raw_first = [keep.tile([P, 2 * FEATS], U8, name="raw_first%d" % a) for a in range(2)]
         raw_later = [keep.tile([P, 4 * FEATS], U8, name="raw_later%d" % g) for g in range(1, CHUNKS)]
-        cap_one = [keep.tile([P, FEATS], BF16, name="cap_one%d" % t) for t in range(TILES)]
+        cap_rows = [keep.tile([P, FEATS], BF16, name="cap_rows%d" % t) for t in range(TILES)]
         weight_all = keep.tile([P, CLIPS], BF16, name="weight_all")
         bias_cols = keep.tile([P, TURNED], BF16, name="bias_cols")
         bank = keep.tile([P, CHUNKS, 2 * FEATS], U8, align_bytes=64, name="bank")
         bank_sc = keep.tile([P, CHUNKS, FEATS], U8, align_bytes=64, name="bank_sc")
         ident = keep.tile([P, P], F32, name="ident")
         aud_codes = [keep.tile([P, PASSES, CHUNK], U32, align_bytes=64, name="aud_codes%d" % g) for g in range(CHUNKS)]
-        aud_planes = [keep.tile([P, PASSES, CHUNK], U8, align_bytes=64, name="aud_planes%d" % g) for g in range(CHUNKS)]
-        cap_own = [keep.tile([P, PASSES, P], U32, align_bytes=64, name="cap_codes%d" % t) for t in range(TURNED)]
-        cap_own_planes = [keep.tile([P, PASSES, P], U8, align_bytes=64, name="cap_planes%d" % t) for t in range(TURNED)]
-        cap_pair = keep.tile([P, PASSES, 2 * P], U32, align_bytes=64, name="cap_pair")
-        cap_pair_planes = keep.tile([P, PASSES, 2 * P], U8, align_bytes=64, name="cap_pair_planes")
+        aud_sc = [keep.tile([P, PASSES, CHUNK], U8, align_bytes=64, name="aud_sc%d" % g) for g in range(CHUNKS)]
+        cap_codes = [keep.tile([P, PASSES, P], U32, align_bytes=64, name="cap_codes%d" % t) for t in range(TURNED)]
+        cap_sc = [keep.tile([P, PASSES, P], U8, align_bytes=64, name="cap_sc%d" % t) for t in range(TURNED)]
+        pair_codes = keep.tile([P, PASSES, 2 * P], U32, align_bytes=64, name="pair_codes")
+        pair_sc = keep.tile([P, PASSES, 2 * P], U8, align_bytes=64, name="pair_sc")
         bias_row = keep.tile([P, 2 * P], BF16, name="bias_row")
         weight_cols = keep.tile([P, CHUNKS, 4], BF16, name="weight_cols")
-        r_operand = {}
-
-        def quantise_resid(name, src, owners):
-            codes = keep.tile([P, 2 * P], U32, align_bytes=64, name="r_codes_" + name)
-            planes = keep.tile([P, 2 * P], U8, align_bytes=64, name="r_planes_" + name)
-            nc.vector.quantize_mx(out=codes[:].bitcast(FP8X4), scales=planes[:], in_=src)
-            for n, owner in enumerate(owners):
-                r_operand[owner] = (codes[:, P * n : P * (n + 1)], planes[:, P * n : P * (n + 1)])
 
         ctx.enter_context(tc.manual_schedule())
 
@@ -79,222 +73,207 @@ def tile_siglip_negative_caption_gradient_s13_kernel(
 
         def load_cap(t):
             rows = cap_view[:, t, :] if t < TURNED else captions[P * t : P * (t + 1), :]
-            nc.sync.dma_start(out=cap_one[t][:], in_=rows)
+            nc.sync.dma_start(out=cap_rows[t][:], in_=rows)
 
-        def load_raw_first(a):
+        def load_first_half(a):
             nc.sync.dma_start(out=raw_first[a][:], in_=aud_view[0][:, 2 * a * FEATS : 2 * (a + 1) * FEATS])
+
+        def load_chunk(g):
+            nc.sync.dma_start(out=raw_later[g - 1][:], in_=aud_view[g])
 
         nc.sync.dma_start(out=scale_cols[:], in_=audio_scale.rearrange("o (h n m) -> n (o h) m", h=PASSES, m=4))
         load_cap(0)
-        load_raw_first(0)
+        load_first_half(0)
         load_cap(1)
         load_cap(2)
-        load_raw_first(1)
-        load_cap(3)
-        load_cap(4)
-        nc.sync.dma_start(out=raw_later[0][:], in_=aud_view[1])
-        load_cap(5)
+        load_first_half(1)
+        for t in range(3, TURNED):
+            load_cap(t)
         nc.sync.dma_start(out=bias_cols[:], in_=bias[: P * TURNED].rearrange("(p t) -> p t", t=TURNED))
-        load_cap(6)
-        load_cap(7)
-        nc.sync.dma_start(out=raw_later[1][:], in_=aud_view[2])
-        nc.sync.dma_start(out=raw_later[2][:], in_=aud_view[3])
+        load_chunk(1)
+        for t in range(TURNED, TILES):
+            load_cap(t)
+        for g in range(2, CHUNKS):
+            load_chunk(g)
         nc.sync.dma_start(out=weight_all[:], in_=clip_weight.partition_broadcast(P))
         nc.sync.dma_start(out=bias_row[:], in_=bias[P * TURNED :].partition_broadcast(P))
-        nc.sync.dma_start(out=weight_cols[:], in_=clip_weight.rearrange("(g p t) -> p g t", p=P, t=4))
         nc.sync.dma_start(out=bank[:], in_=bank_words.rearrange("g p n -> p g n"))
-        for q in range(4):
+        for r in range(4):
             nc.sync.dma_start(
-                out=bank_sc[32 * q : 32 * q + 4, :, :].bitcast(I32),
-                in_=bank_scales[:, 4 * q : 4 * q + 4, :].rearrange("g r n -> r g n").bitcast(I32),
+                out=bank_sc[32 * r : 32 * r + 4, :, :].bitcast(I32),
+                in_=bank_scales[:, 4 * r : 4 * r + 4, :].rearrange("g r n -> r g n").bitcast(I32),
             )
+        nc.sync.dma_start(out=weight_cols[:], in_=clip_weight.rearrange("(g p t) -> p g t", p=P, t=4))
 
-        def cap_words(t):
-            return cap_one[t][:].bitcast(F32)
+        def grouped_tile(name):
+            return work.tile([P, WIDE], BF16, align_bytes=64, tag="grouped", name=name, bufs=9)
 
-        def raw_slot(g, s):
-            if g == 0:
-                return raw_first[s // 2][:, (s % 2) * FEATS : (s % 2 + 1) * FEATS]
-            return raw_later[g - 1][:, s * FEATS : (s + 1) * FEATS]
-
-        def copy_out(engine, dst, src):
-            if engine == "vector":
-                nc.vector.tensor_copy(out=dst, in_=src)
-            else:
-                nc.scalar.copy(out=dst, in_=src)
-
-        turned = {}
         grouped = {}
 
-        def spread_turn(h):
+        def spread_scale(h):
             xt = psum.tile([P, 4, P], F32, tag="bank", name="spread")
             for m in range(4):
                 nc.tensor.transpose(xt[:, m, :], scale_cols[:, h, m : m + 1].to_broadcast([P, P]), ident[:])
-            turned["scale", h] = xt
-
-        def spread_exit(h, engine="scalar", first=0, end=P):
-            dst = scale_all[:, CHUNK * h + 4 * first : CHUNK * h + 4 * end].rearrange("p (n m) -> p n m", m=4)
-            copy_out(engine, dst, turned["scale", h][:, :, first:end].rearrange("p m n -> p n m"))
-
+            nc.scalar.copy(
+                out=scale_all[:, CHUNK * h : CHUNK * (h + 1)].rearrange("p (n m) -> p n m", m=4),
+                in_=xt[:].rearrange("p m n -> p n m"),
+            )
 
         def cap_turn(t):
             xt = psum.tile([P, PASSES, 2, P], F32, tag="bank", name="cap_xt")
+            words = cap_rows[t][:].bitcast(F32)
             for h in range(PASSES):
                 for u in range(2):
-                    src = cap_words(t)[:, 256 * h + u : 256 * (h + 1) : 2]
-                    nc.tensor.transpose(xt[:, h, u, :], src, ident[:])
-            turned["cap", t] = xt
-
-        def cap_exit(t, engine="scalar"):
-            grouped["cap", t] = work.tile([P, 1024], BF16, align_bytes=64, tag="grouped", name="cap_grouped", bufs=9)
-            copy_out(
-                engine,
-                grouped["cap", t][:].bitcast(F32).rearrange("p (h j u) -> p h j u", h=PASSES, u=2),
-                turned["cap", t][:].rearrange("p h u j -> p h j u"),
+                    nc.tensor.transpose(xt[:, h, u, :], words[:, HALF * h + u : HALF * (h + 1) : 2], ident[:])
+            grouped["cap", t] = grouped_tile("cap_grouped")
+            nc.scalar.copy(
+                out=grouped["cap", t][:].bitcast(F32).rearrange("p (h j u) -> p h j u", h=PASSES, u=2),
+                in_=xt[:].rearrange("p h u j -> p h j u"),
             )
 
         def cap_quant(t):
-            if t < TURNED:
-                nc.vector.quantize_mx(
-                    out=cap_own[t][:].rearrange("p h j -> p (h j)").bitcast(FP8X4),
-                    scales=cap_own_planes[t][:].rearrange("p h j -> p (h j)"),
-                    in_=grouped["cap", t][:],
-                )
-                return
-            cols = slice(P * (t % 2), P * (t % 2 + 1))
-            for h in range(PASSES):
-                nc.vector.quantize_mx(
-                    out=cap_pair[:, h, cols].bitcast(FP8X4),
-                    scales=cap_pair_planes[:, h, cols],
-                    in_=grouped["cap", t][:, CHUNK * h : CHUNK * (h + 1)],
-                )
+            nc.vector.quantize_mx(
+                out=cap_codes[t][:].rearrange("p h j -> p (h j)").bitcast(FP8X4),
+                scales=cap_sc[t][:].rearrange("p h j -> p (h j)"),
+                in_=grouped["cap", t][:],
+            )
+
+        def pair_quant():
+            for i in range(2):
+                cols = slice(P * i, P * (i + 1))
+                for h in range(PASSES):
+                    nc.vector.quantize_mx(
+                        out=pair_codes[:, h, cols].bitcast(FP8X4),
+                        scales=pair_sc[:, h, cols],
+                        in_=grouped["cap", TURNED + i][:, CHUNK * h : CHUNK * (h + 1)],
+                    )
 
         audio = {}
 
-        def widen(g, s, first=0, end=FEATS):
-            if (g, s) not in audio:
-                audio[g, s] = work.tile([P, FEATS], BF16, align_bytes=64, tag="audio", name="audio", bufs=6)
-            nc.vector.tensor_tensor(
-                out=audio[g, s][:, first:end], in0=raw_slot(g, s)[:, first:end].bitcast(FP8), in1=scale_all[:, first:end], op=MULT
-            )
+        def widen(g, a, first=0, end=FEATS):
+            for e in range(2):
+                s = 2 * a + e
+                if first == 0:
+                    audio[g, s] = work.tile([P, FEATS], BF16, align_bytes=64, tag="audio", name="audio", bufs=6)
+                raw = raw_first[a][:, e * FEATS : (e + 1) * FEATS] if g == 0 else raw_later[g - 1][:, s * FEATS : (s + 1) * FEATS]
+                nc.vector.tensor_tensor(
+                    out=audio[g, s][:, first:end], in0=raw[:, first:end].bitcast(FP8), in1=scale_all[:, first:end], op=MULT
+                )
 
         def aud_turn(g, a, h):
             xt = psum.tile([P, 2, 2, P], F32, tag="bank", name="aud_xt")
             for e in range(2):
                 words = audio[g, 2 * a + e][:].bitcast(F32)
                 for u in range(2):
-                    src = words[:, 256 * h + u : 256 * (h + 1) : 2]
-                    nc.tensor.transpose(xt[:, e, u, :], src, ident[:])
-            turned["aud", g, a, h] = xt
-
-        def aud_exit(g, a, h, engine="scalar"):
-            key = ("aud", g, a, h)
-            grouped[key] = work.tile([P, 1024], BF16, align_bytes=64, tag="grouped", name="aud_grouped", bufs=9)
-            copy_out(
-                engine,
-                grouped[key][:].bitcast(F32).rearrange("p (e q u) -> p e q u", e=2, u=2),
-                turned[key][:].rearrange("p e u q -> p e q u"),
+                    nc.tensor.transpose(xt[:, e, u, :], words[:, HALF * h + u : HALF * (h + 1) : 2], ident[:])
+            grouped["aud", g, a, h] = grouped_tile("aud_grouped")
+            nc.scalar.copy(
+                out=grouped["aud", g, a, h][:].bitcast(F32).rearrange("p (e q u) -> p e q u", e=2, u=2),
+                in_=xt[:].rearrange("p e u q -> p e q u"),
             )
 
-
-        def aud_quant(g, a, h):
+        def aud_quant(g, a):
             cols = slice(HALF * a, HALF * (a + 1))
-            nc.vector.quantize_mx(
-                out=aud_codes[g][:, h, cols].bitcast(FP8X4), scales=aud_planes[g][:, h, cols], in_=grouped["aud", g, a, h][:]
-            )
-
-        sums = {}
-        sigs = {}
-        resids = {}
-
-        def logits(t, g, first=0, end=CHUNK):
-            sums[t, g] = psum.tile([P, end - first], F32, tag="bank", name="logit_sum")
             for h in range(PASSES):
-                nc.tensor.matmul_mx(
-                    out=sums[t, g][:],
-                    lhsT=cap_own[t][:, h, :].bitcast(FP8X4),
-                    lhsT_scale=cap_own_planes[t][:, h, :],
-                    rhs=aud_codes[g][:, h, first:end].bitcast(FP8X4),
-                    rhs_scale=aud_planes[g][:, h, first:end],
-                    start=(h == 0),
-                    stop=(h == PASSES - 1),
+                nc.vector.quantize_mx(
+                    out=aud_codes[g][:, h, cols].bitcast(FP8X4), scales=aud_sc[g][:, h, cols], in_=grouped["aud", g, a, h][:]
                 )
 
-        def sigmoid(t, g, first=0, end=CHUNK):
-            pair = g // 2
-            if (t, pair) not in sigs:
-                sigs[t, pair] = work.tile([P, 2, CHUNK], F32, tag="sig", name="sig", bufs=12)
-            nc.scalar.activation(
-                out=sigs[t, pair][:, g % 2, first:end].rearrange("p (a q e) -> p a q e", q=P, e=2),
-                in_=sums[t, g][:].rearrange("p (a e q) -> p a q e", q=P, e=2),
-                func=SIGMOID,
-                bias=bias_cols[:, t : t + 1],
-            )
+        sigs = {}
+        resids = {}
+        r_operand = {}
 
-        def weigh(t, pair):
-            resids[t, pair] = work.tile([P, 2 * CHUNK], BF16, align_bytes=64, tag="resid", name="resid", bufs=9)
-            weights = weight_all[:, 2 * CHUNK * pair : 2 * CHUNK * (pair + 1)]
-            nc.vector.tensor_tensor(
-                out=resids[t, pair][:].rearrange("p (u c q e) -> p u c q e", u=2, c=2, e=2),
-                in0=sigs[t, pair][:].rearrange("p c (u q e) -> p u c q e", u=2, e=2),
-                in1=weights.rearrange("p (c q u e) -> p u c q e", c=2, u=2, e=2),
-                op=MULT,
-            )
-
-        def r_turn(t, pair):
-            xt = psum.tile([P, 2, 2, P], F32, tag="bank", name="r_xt")
-            words = resids[t, pair][:].bitcast(F32)
-            for u in range(2):
-                for c in range(2):
-                    nc.tensor.transpose(xt[:, c, u, :], words[:, 256 * u + P * c : 256 * u + P * (c + 1)], ident[:])
-            turned["r", t, pair] = xt
-
-        def r_exit(t, pair, engine="scalar"):
-            key = ("r", t, pair)
-            grouped[key] = work.tile([P, 1024], BF16, align_bytes=64, tag="grouped", name="r_grouped", bufs=9)
-            copy_out(
-                engine,
-                grouped[key][:].bitcast(F32).rearrange("p (c j u) -> p c j u", c=2, u=2),
-                turned[key][:].rearrange("p c u j -> p c j u"),
-            )
-
-        def r_quant(t, pair):
-            quantise_resid("%d_%d" % (t, pair), grouped["r", t, pair][:], [(t, 2 * pair), (t, 2 * pair + 1)])
-
-        direct = {}
-
-        def direct_logits(g, a):
-            acc = psum.tile([P, 2, HALF], F32, tag="bank", name="direct_sum")
-            for e in range(2):
-                cols = slice(HALF * a + P * e, HALF * a + P * (e + 1))
+        def probs(tiles, g, first=0, end=CHUNK):
+            for t in tiles:
+                acc = psum.tile([P, end - first], F32, tag="bank", name="logit_sum")
                 for h in range(PASSES):
                     nc.tensor.matmul_mx(
-                        out=acc[:, e, :],
-                        lhsT=aud_codes[g][:, h, cols].bitcast(FP8X4),
-                        lhsT_scale=aud_planes[g][:, h, cols],
-                        rhs=cap_pair[:, h, :].bitcast(FP8X4),
-                        rhs_scale=cap_pair_planes[:, h, :],
+                        out=acc[:],
+                        lhsT=cap_codes[t][:, h, :].bitcast(FP8X4),
+                        lhsT_scale=cap_sc[t][:, h, :],
+                        rhs=aud_codes[g][:, h, first:end].bitcast(FP8X4),
+                        rhs_scale=aud_sc[g][:, h, first:end],
                         start=(h == 0),
                         stop=(h == PASSES - 1),
                     )
-            direct["sum", g, a] = acc
+                if g % 2 == 0 and first == 0:
+                    sigs[t, g // 2] = work.tile([P, 2, CHUNK], F32, tag="sig", name="sig", bufs=2 * TURNED)
+                nc.scalar.activation(
+                    out=sigs[t, g // 2][:, g % 2, first:end].rearrange("p (a q e) -> p a q e", q=P, e=2),
+                    in_=acc[:].rearrange("p (a e q) -> p a q e", q=P, e=2),
+                    func=SIGMOID,
+                    bias=bias_cols[:, t : t + 1],
+                )
 
-        def direct_bias(g, a):
-            biased = work.tile([P, 2, HALF], F32, tag="biased", name="biased", bufs=4)
+        def weigh(t, d):
+            resids[t, d] = work.tile([P, 2 * CHUNK], BF16, align_bytes=64, tag="resid", name="resid", bufs=9)
+            weights = weight_all[:, 2 * CHUNK * d : 2 * CHUNK * (d + 1)]
             nc.vector.tensor_tensor(
-                out=biased[:], in0=direct["sum", g, a][:], in1=bias_row[:].unsqueeze(1).to_broadcast([P, 2, HALF]), op=ADD
+                out=resids[t, d][:].rearrange("p (a c q e) -> p a c q e", a=2, c=2, e=2),
+                in0=sigs[t, d][:].rearrange("p c (a q e) -> p a c q e", a=2, e=2),
+                in1=weights.rearrange("p (c q a e) -> p a c q e", c=2, a=2, e=2),
+                op=MULT,
             )
-            direct["biased", g, a] = biased
 
-        def direct_sigmoid(g, a):
-            if a == 0:
-                direct["prob", g] = work.tile([P, 2, HALF, 2], F32, tag="prob", name="prob", bufs=3)
-            nc.scalar.activation(
-                out=direct["prob", g][:, a, :, :], in_=direct["biased", g, a][:].rearrange("p e j -> p j e"), func=SIGMOID
-            )
+        def resid_turn(t):
+            for d in range(2):
+                xt = psum.tile([P, 2, 2, P], F32, tag="bank", name="r_xt")
+                words = resids[t, d][:].bitcast(F32)
+                for a in range(2):
+                    for c in range(2):
+                        nc.tensor.transpose(xt[:, c, a, :], words[:, HALF * a + P * c : HALF * a + P * (c + 1)], ident[:])
+                grouped["r", t, d] = grouped_tile("r_grouped")
+                nc.scalar.copy(
+                    out=grouped["r", t, d][:].bitcast(F32).rearrange("p (c j a) -> p c j a", c=2, a=2),
+                    in_=xt[:].rearrange("p c a j -> p c j a"),
+                )
+
+        def quantise_resid(name, src, owners):
+            codes = keep.tile([P, 2 * P], U32, align_bytes=64, name="r_codes_" + name)
+            scales = keep.tile([P, 2 * P], U8, align_bytes=64, name="r_sc_" + name)
+            nc.vector.quantize_mx(out=codes[:].bitcast(FP8X4), scales=scales[:], in_=src)
+            for n, owner in enumerate(owners):
+                r_operand[owner] = (codes[:, P * n : P * (n + 1)], scales[:, P * n : P * (n + 1)])
+
+        def resid_quant(t):
+            for d in range(2):
+                quantise_resid("%d_%d" % (t, d), grouped["r", t, d][:], [(t, 2 * d), (t, 2 * d + 1)])
+
+        direct = {}
+
+        def direct_logits(g):
+            for a in range(2):
+                acc = psum.tile([P, 2, HALF], F32, tag="bank", name="direct_sum")
+                for e in range(2):
+                    cols = slice(HALF * a + P * e, HALF * a + P * (e + 1))
+                    for h in range(PASSES):
+                        nc.tensor.matmul_mx(
+                            out=acc[:, e, :],
+                            lhsT=aud_codes[g][:, h, cols].bitcast(FP8X4),
+                            lhsT_scale=aud_sc[g][:, h, cols],
+                            rhs=pair_codes[:, h, :].bitcast(FP8X4),
+                            rhs_scale=pair_sc[:, h, :],
+                            start=(h == 0),
+                            stop=(h == PASSES - 1),
+                        )
+                direct["sum", g, a] = acc
+
+        def direct_bias(g):
+            for a in range(2):
+                biased = work.tile([P, 2, HALF], F32, tag="biased", name="biased", bufs=4)
+                row = bias_row[:].unsqueeze(1).to_broadcast([P, 2, HALF])
+                nc.vector.tensor_tensor(out=biased[:], in0=direct["sum", g, a][:], in1=row, op=ADD)
+                direct["biased", g, a] = biased
+
+        def direct_sigmoid(g):
+            direct["prob", g] = work.tile([P, 2, HALF, 2], F32, tag="prob", name="prob", bufs=3)
+            for a in range(2):
+                nc.scalar.activation(
+                    out=direct["prob", g][:, a, :, :], in_=direct["biased", g, a][:].rearrange("p e j -> p j e"), func=SIGMOID
+                )
 
         def direct_weigh(g):
-            grouped["direct", g] = work.tile([P, 1024], BF16, align_bytes=64, tag="grouped", name="d_grouped", bufs=9)
+            grouped["direct", g] = grouped_tile("d_grouped")
             weights = weight_cols[:, g, :].rearrange("p (a e) -> p a e", a=2).unsqueeze(1)
             nc.vector.tensor_tensor(
                 out=grouped["direct", g][:].rearrange("p (j a e) -> p j a e", a=2, e=2),
@@ -306,7 +285,7 @@ def tile_siglip_negative_caption_gradient_s13_kernel(
         def direct_quant(g):
             quantise_resid("direct_%d" % g, grouped["direct", g][:], [(TURNED, g), (TURNED + 1, g)])
 
-        def grad_sum(t, first, end):
+        def grad(t, first, end, on_vector=False):
             acc = psum.tile([P, end - first], F32, tag="bank", name="grad_sum")
             for g in range(CHUNKS):
                 nc.tensor.matmul_mx(
@@ -316,172 +295,103 @@ def tile_siglip_negative_caption_gradient_s13_kernel(
                     rhs=bank[:, g, 2 * first : 2 * end].bitcast(FP4X4),
                     rhs_scale=bank_sc[:, g, first:end],
                     start=(g == 0),
-                    stop=(g == CHUNKS - 1),
+                    stop=(g == LAST),
                 )
-            sums["grad", t, first] = acc
-
-        def store(t, first, end, engine="scalar"):
-            acc = sums["grad", t, first]
-            tag = "res" if end - first == CHUNK else "res_part"
-            res = work.tile([P, end - first], F32, tag=tag, name="res", bufs=6)
-            copy_out(engine, res[:], acc[:])
+            if end - first == CHUNK:
+                res = work.tile([P, CHUNK], F32, tag="res", name="res", bufs=6)
+            else:
+                res = work.tile([P, end - first], F32, tag="res_part", name="res_part", bufs=2)
+            if on_vector:
+                nc.vector.tensor_copy(out=res[:], in_=acc[:])
+            else:
+                nc.scalar.copy(out=res[:], in_=acc[:])
             rows = out_view[:, t, :] if t < TURNED else out[P * t : P * (t + 1), :]
             nc.sync.dma_start(out=rows[:, first:end], in_=res[:])
-
-        def grad(t, first, end, engine="scalar"):
-            grad_sum(t, first, end)
-            store(t, first, end, engine)
-
-        def cap_prepare(t):
-            cap_turn(t)
-            cap_exit(t)
-
-        def aud_prepare(g, a, passes=range(PASSES)):
-            for h in passes:
-                aud_turn(g, a, h)
-                aud_exit(g, a, h)
-
-        def aud_quants(g, a):
-            for h in range(PASSES):
-                aud_quant(g, a, h)
-
-        def probs(tiles, g, first=0, end=CHUNK):
-            for t in tiles:
-                logits(t, g, first, end)
-                sigmoid(t, g, first, end)
-
-        def turns(t):
-            for pair in range(2):
-                r_turn(t, pair)
-                r_exit(t, pair)
-
-        def quants(t):
-            for pair in range(2):
-                r_quant(t, pair)
 
         def grads(t):
             grad(t, 0, CHUNK)
             grad(t, CHUNK, FEATS)
 
-        def both(step, g):
-            for a in range(2):
-                step(g, a)
-
-        spread_turn(0)
-        spread_exit(0, "scalar", 0, 48)
-        spread_exit(0, "scalar", 48, P)
-        spread_turn(1)
-        spread_exit(1)
-        cap_prepare(0)
-        for first, end in ((0, 192), (192, CHUNK), (CHUNK, FEATS)):
-            widen(0, 0, first, end)
-            widen(0, 1, first, end)
-        cap_prepare(1)
-        aud_prepare(0, 0, [0])
-        cap_prepare(2)
-        aud_prepare(0, 0, [1])
-        widen(0, 2)
-        widen(0, 3)
-        cap_prepare(3)
-        cap_quant(0)
-        aud_quants(0, 0)
-        cap_quant(1)
-        cap_prepare(4)
-        aud_prepare(0, 1)
-        cap_prepare(5)
-        cap_quant(2)
-        probs(range(3), 0, 0, HALF)
+        for h in range(PASSES):
+            spread_scale(h)
+        cap_turn(0)
+        for h in range(PASSES):
+            widen(0, 0, CHUNK * h, CHUNK * (h + 1))
+        cap_turn(1)
+        for a in range(2):
+            for h in range(PASSES):
+                aud_turn(0, a, h)
+                cap_turn(2 + PASSES * a + h)
+            if a == 0:
+                widen(0, 1)
+                aud_quant(0, 0)
+                for t in range(GROUP):
+                    cap_quant(t)
+        probs(range(GROUP), 0, 0, HALF)
         widen(1, 0)
-        aud_quants(0, 1)
-        cap_quant(3)
-        widen(1, 1)
-        probs(range(3), 0, HALF, CHUNK)
-        probs([3], 0)
-        cap_quant(4)
-        widen(1, 2)
-        aud_prepare(1, 0)
-        widen(1, 3)
-        cap_quant(5)
-        probs([4], 0)
-        aud_prepare(1, 1)
-        cap_prepare(6)
-        cap_prepare(7)
-        aud_quants(1, 0)
-        widen(2, 0)
-        aud_quants(1, 1)
-        widen(2, 1)
-        probs([5], 0)
+        aud_quant(0, 1)
 
-        for g in range(2, CHUNKS):
-            widen(g, 2)
-            widen(g, 3)
-            if g == 2:
-                probs(range(2), g - 1)
-                aud_prepare(g, 0)
-                probs(range(2, 3), g - 1)
-                aud_prepare(g, 1)
-            else:
-                probs(range(3), g - 1)
-                both(aud_prepare, g)
-            if g < LAST:
-                widen(g + 1, 0)
-                aud_quants(g, 0)
-                widen(g + 1, 1, 0, CHUNK)
-                aud_quants(g, 1)
-                widen(g + 1, 1, CHUNK, FEATS)
-            else:
-                weigh(0, 0)
-                cap_quant(6)
-                cap_quant(7)
-                both(aud_quants, g)
-                weigh(1, 0)
-            probs(range(3, 6), g - 1)
+        for g in range(1, CHUNKS):
+            for a in range(2):
+                for h in range(PASSES):
+                    aud_turn(g, a, h)
+                if g == 1:
+                    cap_turn(TURNED + a)
+                if (g, a) == (1, 0):
+                    probs(range(GROUP), 0, HALF, CHUNK)
+                else:
+                    probs(range(GROUP * a, GROUP * (a + 1)), g - 1)
+                if (g, a) == (LAST, 1):
+                    weigh(0, 0)
+                    pair_quant()
+                else:
+                    widen(g + a, 1 - a)
+                aud_quant(g, a)
+                if (g, a) == (1, 0):
+                    for t in range(GROUP, TURNED):
+                        cap_quant(t)
 
+        weigh(1, 0)
         weigh(2, 0)
         probs(range(4), LAST)
         weigh(0, 1)
         weigh(1, 1)
-        both(direct_logits, 0)
-        turns(0)
-        turns(1)
-        weigh(2, 1)
-        quants(0)
-        probs(range(4, 6), LAST)
-        weigh(3, 0)
-        weigh(3, 1)
-        quants(1)
-        both(direct_bias, 0)
-        grads(0)
+        direct_logits(0)
 
-        turns(2)
-        turns(3)
-        weigh(4, 0)
-        quants(2)
-        weigh(4, 1)
-        grads(1)
-        both(direct_sigmoid, 0)
-        weigh(5, 0)
-        weigh(5, 1)
-        grads(2)
-        turns(4)
-        turns(5)
-        quants(3)
+        for t in range(0, TURNED - 2, 2):
+            resid_turn(t)
+            resid_turn(t + 1)
+            if t == 0:
+                weigh(2, 1)
+                probs(range(4, TURNED), LAST)
+            else:
+                direct_bias(0)
+                grads(t - 1)
+                direct_sigmoid(0)
+            resid_quant(t)
+            for tile, d in ((t + 2, 0), (t + 2, 1), (t + 3, 0), (t + 3, 1)):
+                if (tile, d) not in resids:
+                    weigh(tile, d)
+            resid_quant(t + 1)
+            grads(t)
+        resid_turn(TURNED - 2)
+        resid_turn(TURNED - 1)
+
         direct_weigh(0)
         for g in range(1, CHUNKS):
-            both(direct_logits, g)
-            if g == LAST:
-                quants(4)
-                direct_quant(0)
-            both(direct_bias, g)
-            both(direct_sigmoid, g)
+            direct_logits(g)
+            direct_bias(g)
+            direct_sigmoid(g)
+        resid_quant(TURNED - 2)
+        direct_quant(0)
         direct_weigh(1)
-        quants(5)
+        resid_quant(TURNED - 1)
         for g in range(2, CHUNKS):
             direct_weigh(g)
             direct_quant(g - 1)
         direct_quant(LAST)
-        for t in range(3, TILES - 1):
+        for t in range(TURNED - 3, TILES - 1):
             grads(t)
         grad(TILES - 1, 0, CHUNK)
-        grad(TILES - 1, CHUNK, CHUNK + HALF, "vector")
+        grad(TILES - 1, CHUNK, CHUNK + HALF, on_vector=True)
         grad(TILES - 1, CHUNK + HALF, FEATS)

@@ -23,8 +23,8 @@ CHUNKS = CLIPS // CHUNK
 LAST = CHUNKS - 1
 PASSES = FEATS // CHUNK
 TILES = CAPS // P
-TURNED = TILES - 2
-GROUP = TURNED // 2
+PAIRS = TILES // 2
+QUARTERS = FEATS // HALF
 WIDE = 4 * HALF
 
 FLOPS = 2 * 2 * CLIPS * CAPS * FEATS
@@ -39,23 +39,21 @@ def tile_siglip_negative_caption_gradient_s13_kernel(
         work = ctx.enter_context(tc.tile_pool(name="work", bufs=3))
         psum = ctx.enter_context(tc.psum_pool(name="psum", bufs=8))
 
-        scale_cols = keep.tile([P, PASSES, 4], F32, name="scale_cols")
+        scale_cols = keep.tile([P, QUARTERS, 2], F32, name="scale_cols")
         scale_all = keep.tile([P, FEATS], F32, name="scale_all")
         raw_first = [keep.tile([P, 2 * FEATS], U8, name="raw_first%d" % a) for a in range(2)]
         raw_later = [keep.tile([P, 4 * FEATS], U8, name="raw_later%d" % g) for g in range(1, CHUNKS)]
         cap_rows = [keep.tile([P, FEATS], BF16, name="cap_rows%d" % t) for t in range(TILES)]
         weight_all = keep.tile([P, CLIPS], BF16, name="weight_all")
-        bias_cols = keep.tile([P, TURNED], BF16, name="bias_cols")
+        bias_cols = keep.tile([P, PAIRS, 2], BF16, name="bias_cols")
         bank = keep.tile([P, CHUNKS, 2 * FEATS], U8, align_bytes=64, name="bank")
         bank_sc = keep.tile([P, CHUNKS, FEATS], U8, align_bytes=64, name="bank_sc")
         ident = keep.tile([P, P], F32, name="ident")
         aud_codes = [keep.tile([P, PASSES, CHUNK], U32, align_bytes=64, name="aud_codes%d" % g) for g in range(CHUNKS)]
         aud_sc = [keep.tile([P, PASSES, CHUNK], U8, align_bytes=64, name="aud_sc%d" % g) for g in range(CHUNKS)]
-        cap_codes = [keep.tile([P, PASSES, P], U32, align_bytes=64, name="cap_codes%d" % t) for t in range(TURNED)]
-        cap_sc = [keep.tile([P, PASSES, P], U8, align_bytes=64, name="cap_sc%d" % t) for t in range(TURNED)]
-        pair_codes = keep.tile([P, PASSES, 2 * P], U32, align_bytes=64, name="pair_codes")
-        pair_sc = keep.tile([P, PASSES, 2 * P], U8, align_bytes=64, name="pair_sc")
-        bias_row = keep.tile([P, 2 * P], BF16, name="bias_row")
+        cap_codes = [keep.tile([P, PASSES, 2 * P], U32, align_bytes=64, name="cap_codes%d" % k) for k in range(PAIRS)]
+        cap_sc = [keep.tile([P, PASSES, 2 * P], U8, align_bytes=64, name="cap_sc%d" % k) for k in range(PAIRS)]
+        bias_row = keep.tile([P, HALF], BF16, name="bias_row")
         weight_cols = keep.tile([P, CHUNKS, 4], BF16, name="weight_cols")
 
         ctx.enter_context(tc.manual_schedule())
@@ -68,12 +66,11 @@ def tile_siglip_negative_caption_gradient_s13_kernel(
         nc.gpsimd.memset(bank_sc[:].rearrange("p g d -> p (g d)").bitcast(U32), 0)
 
         aud_view = audio_bytes.rearrange("(g q s) d -> g q (s d)", q=P, s=4)
-        cap_view = captions[: P * TURNED, :].rearrange("(p t) d -> p t d", t=TURNED)
-        out_view = out[: P * TURNED, :].rearrange("(p t) d -> p t d", t=TURNED)
+        cap_view = captions.rearrange("(k p i) d -> k i p d", p=P, i=2)
+        out_view = out.rearrange("(k p i) d -> k i p d", p=P, i=2)
 
         def load_cap(t):
-            rows = cap_view[:, t, :] if t < TURNED else captions[P * t : P * (t + 1), :]
-            nc.sync.dma_start(out=cap_rows[t][:], in_=rows)
+            nc.sync.dma_start(out=cap_rows[t][:], in_=cap_view[t // 2, t % 2])
 
         def load_first_half(a):
             nc.sync.dma_start(out=raw_first[a][:], in_=aud_view[0][:, 2 * a * FEATS : 2 * (a + 1) * FEATS])
@@ -81,22 +78,18 @@ def tile_siglip_negative_caption_gradient_s13_kernel(
         def load_chunk(g):
             nc.sync.dma_start(out=raw_later[g - 1][:], in_=aud_view[g])
 
-        nc.sync.dma_start(out=scale_cols[:], in_=audio_scale.rearrange("o (h n m) -> n (o h) m", h=PASSES, m=4))
-        load_cap(0)
+        nc.sync.dma_start(out=scale_cols[:], in_=audio_scale.rearrange("o (c n m) -> n (o c) m", c=QUARTERS, m=2))
         load_first_half(0)
-        load_cap(1)
-        load_cap(2)
+        for t in range(3):
+            load_cap(t)
         load_first_half(1)
-        for t in range(3, TURNED):
+        for t in range(3, TILES):
             load_cap(t)
-        nc.sync.dma_start(out=bias_cols[:], in_=bias[: P * TURNED].rearrange("(p t) -> p t", t=TURNED))
-        load_chunk(1)
-        for t in range(TURNED, TILES):
-            load_cap(t)
-        for g in range(2, CHUNKS):
+        nc.sync.dma_start(out=bias_cols[:], in_=bias.rearrange("(k p i) -> p k i", p=P, i=2))
+        for g in range(1, CHUNKS):
             load_chunk(g)
         nc.sync.dma_start(out=weight_all[:], in_=clip_weight.partition_broadcast(P))
-        nc.sync.dma_start(out=bias_row[:], in_=bias[P * TURNED :].partition_broadcast(P))
+        nc.sync.dma_start(out=bias_row[:], in_=bias[HALF * 3 :].partition_broadcast(P))
         nc.sync.dma_start(out=bank[:], in_=bank_words.rearrange("g p n -> p g n"))
         for r in range(4):
             nc.sync.dma_start(
@@ -106,16 +99,16 @@ def tile_siglip_negative_caption_gradient_s13_kernel(
         nc.sync.dma_start(out=weight_cols[:], in_=clip_weight.rearrange("(g p t) -> p g t", p=P, t=4))
 
         def grouped_tile(name):
-            return work.tile([P, WIDE], BF16, align_bytes=64, tag="grouped", name=name, bufs=9)
+            return work.tile([P, WIDE], BF16, align_bytes=64, tag="grouped", name=name, bufs=7)
 
         grouped = {}
 
-        def spread_scale(h):
-            xt = psum.tile([P, 4, P], F32, tag="bank", name="spread")
-            for m in range(4):
-                nc.tensor.transpose(xt[:, m, :], scale_cols[:, h, m : m + 1].to_broadcast([P, P]), ident[:])
+        def spread_scale(c):
+            xt = psum.tile([P, 2, P], F32, tag="bank", name="spread")
+            for m in range(2):
+                nc.tensor.transpose(xt[:, m, :], scale_cols[:, c, m : m + 1].to_broadcast([P, P]), ident[:])
             nc.scalar.copy(
-                out=scale_all[:, CHUNK * h : CHUNK * (h + 1)].rearrange("p (n m) -> p n m", m=4),
+                out=scale_all[:, HALF * c : HALF * (c + 1)].rearrange("p (n m) -> p n m", m=2),
                 in_=xt[:].rearrange("p m n -> p n m"),
             )
 
@@ -125,28 +118,21 @@ def tile_siglip_negative_caption_gradient_s13_kernel(
             for h in range(PASSES):
                 for u in range(2):
                     nc.tensor.transpose(xt[:, h, u, :], words[:, HALF * h + u : HALF * (h + 1) : 2], ident[:])
-            grouped["cap", t] = grouped_tile("cap_grouped")
+            if t % 2 == 0:
+                grouped["cap", t // 2] = work.tile(
+                    [P, PASSES, 2, CHUNK], BF16, align_bytes=64, tag="cap_grouped", name="cap_grouped", bufs=3
+                )
             nc.scalar.copy(
-                out=grouped["cap", t][:].bitcast(F32).rearrange("p (h j u) -> p h j u", h=PASSES, u=2),
+                out=grouped["cap", t // 2][:, :, t % 2, :].bitcast(F32).rearrange("p h (j u) -> p h j u", u=2),
                 in_=xt[:].rearrange("p h u j -> p h j u"),
             )
 
-        def cap_quant(t):
+        def cap_quant(k):
             nc.vector.quantize_mx(
-                out=cap_codes[t][:].rearrange("p h j -> p (h j)").bitcast(FP8X4),
-                scales=cap_sc[t][:].rearrange("p h j -> p (h j)"),
-                in_=grouped["cap", t][:],
+                out=cap_codes[k][:].rearrange("p h j -> p (h j)").bitcast(FP8X4),
+                scales=cap_sc[k][:].rearrange("p h j -> p (h j)"),
+                in_=grouped["cap", k][:].rearrange("p h i c -> p (h i c)"),
             )
-
-        def pair_quant():
-            for i in range(2):
-                cols = slice(P * i, P * (i + 1))
-                for h in range(PASSES):
-                    nc.vector.quantize_mx(
-                        out=pair_codes[:, h, cols].bitcast(FP8X4),
-                        scales=pair_sc[:, h, cols],
-                        in_=grouped["cap", TURNED + i][:, CHUNK * h : CHUNK * (h + 1)],
-                    )
 
         audio = {}
 
@@ -172,9 +158,9 @@ def tile_siglip_negative_caption_gradient_s13_kernel(
                 in_=xt[:].rearrange("p e u q -> p e q u"),
             )
 
-        def aud_quant(g, a):
+        def aud_quant(g, a, passes=range(PASSES)):
             cols = slice(HALF * a, HALF * (a + 1))
-            for h in range(PASSES):
+            for h in passes:
                 nc.vector.quantize_mx(
                     out=aud_codes[g][:, h, cols].bitcast(FP8X4), scales=aud_sc[g][:, h, cols], in_=grouped["aud", g, a, h][:]
                 )
@@ -185,28 +171,29 @@ def tile_siglip_negative_caption_gradient_s13_kernel(
 
         def probs(tiles, g, first=0, end=CHUNK):
             for t in tiles:
+                cols = slice(P * (t % 2), P * (t % 2 + 1))
                 acc = psum.tile([P, end - first], F32, tag="bank", name="logit_sum")
                 for h in range(PASSES):
                     nc.tensor.matmul_mx(
                         out=acc[:],
-                        lhsT=cap_codes[t][:, h, :].bitcast(FP8X4),
-                        lhsT_scale=cap_sc[t][:, h, :],
+                        lhsT=cap_codes[t // 2][:, h, cols].bitcast(FP8X4),
+                        lhsT_scale=cap_sc[t // 2][:, h, cols],
                         rhs=aud_codes[g][:, h, first:end].bitcast(FP8X4),
                         rhs_scale=aud_sc[g][:, h, first:end],
                         start=(h == 0),
                         stop=(h == PASSES - 1),
                     )
-                if g % 2 == 0 and first == 0:
-                    sigs[t, g // 2] = work.tile([P, 2, CHUNK], F32, tag="sig", name="sig", bufs=2 * TURNED)
+                if (t, g // 2) not in sigs:
+                    sigs[t, g // 2] = work.tile([P, 2, CHUNK], F32, tag="sig", name="sig", bufs=12)
                 nc.scalar.activation(
                     out=sigs[t, g // 2][:, g % 2, first:end].rearrange("p (a q e) -> p a q e", q=P, e=2),
                     in_=acc[:].rearrange("p (a e q) -> p a q e", q=P, e=2),
                     func=SIGMOID,
-                    bias=bias_cols[:, t : t + 1],
+                    bias=bias_cols[:, t // 2, t % 2 : t % 2 + 1],
                 )
 
         def weigh(t, d):
-            resids[t, d] = work.tile([P, 2 * CHUNK], BF16, align_bytes=64, tag="resid", name="resid", bufs=9)
+            resids[t, d] = work.tile([P, 2 * CHUNK], BF16, align_bytes=64, tag="resid", name="resid", bufs=6)
             weights = weight_all[:, 2 * CHUNK * d : 2 * CHUNK * (d + 1)]
             nc.vector.tensor_tensor(
                 out=resids[t, d][:].rearrange("p (a c q e) -> p a c q e", a=2, c=2, e=2),
@@ -215,18 +202,17 @@ def tile_siglip_negative_caption_gradient_s13_kernel(
                 op=MULT,
             )
 
-        def resid_turn(t):
-            for d in range(2):
-                xt = psum.tile([P, 2, 2, P], F32, tag="bank", name="r_xt")
-                words = resids[t, d][:].bitcast(F32)
-                for a in range(2):
-                    for c in range(2):
-                        nc.tensor.transpose(xt[:, c, a, :], words[:, HALF * a + P * c : HALF * a + P * (c + 1)], ident[:])
-                grouped["r", t, d] = grouped_tile("r_grouped")
-                nc.scalar.copy(
-                    out=grouped["r", t, d][:].bitcast(F32).rearrange("p (c j a) -> p c j a", c=2, a=2),
-                    in_=xt[:].rearrange("p c a j -> p c j a"),
-                )
+        def resid_turn(t, d):
+            xt = psum.tile([P, 2, 2, P], F32, tag="bank", name="r_xt")
+            words = resids[t, d][:].bitcast(F32)
+            for a in range(2):
+                for c in range(2):
+                    nc.tensor.transpose(xt[:, c, a, :], words[:, HALF * a + P * c : HALF * a + P * (c + 1)], ident[:])
+            grouped["r", t, d] = grouped_tile("r_grouped")
+            nc.scalar.copy(
+                out=grouped["r", t, d][:].bitcast(F32).rearrange("p (c j a) -> p c j a", c=2, a=2),
+                in_=xt[:].rearrange("p c a j -> p c j a"),
+            )
 
         def quantise_resid(name, src, owners):
             codes = keep.tile([P, 2 * P], U32, align_bytes=64, name="r_codes_" + name)
@@ -235,13 +221,12 @@ def tile_siglip_negative_caption_gradient_s13_kernel(
             for n, owner in enumerate(owners):
                 r_operand[owner] = (codes[:, P * n : P * (n + 1)], scales[:, P * n : P * (n + 1)])
 
-        def resid_quant(t):
-            for d in range(2):
-                quantise_resid("%d_%d" % (t, d), grouped["r", t, d][:], [(t, 2 * d), (t, 2 * d + 1)])
+        def resid_quant(t, d):
+            quantise_resid("%d_%d" % (t, d), grouped["r", t, d][:], [(t, 2 * d), (t, 2 * d + 1)])
 
         direct = {}
 
-        def direct_logits(g):
+        def direct_logits(k, g):
             for a in range(2):
                 acc = psum.tile([P, 2, HALF], F32, tag="bank", name="direct_sum")
                 for e in range(2):
@@ -251,45 +236,55 @@ def tile_siglip_negative_caption_gradient_s13_kernel(
                             out=acc[:, e, :],
                             lhsT=aud_codes[g][:, h, cols].bitcast(FP8X4),
                             lhsT_scale=aud_sc[g][:, h, cols],
-                            rhs=pair_codes[:, h, :].bitcast(FP8X4),
-                            rhs_scale=pair_sc[:, h, :],
+                            rhs=cap_codes[k][:, h, :].bitcast(FP8X4),
+                            rhs_scale=cap_sc[k][:, h, :],
                             start=(h == 0),
                             stop=(h == PASSES - 1),
                         )
-                direct["sum", g, a] = acc
+                direct["sum", k, g, a] = acc
 
-        def direct_bias(g):
+        def direct_bias(k, g):
             for a in range(2):
                 biased = work.tile([P, 2, HALF], F32, tag="biased", name="biased", bufs=4)
-                row = bias_row[:].unsqueeze(1).to_broadcast([P, 2, HALF])
-                nc.vector.tensor_tensor(out=biased[:], in0=direct["sum", g, a][:], in1=row, op=ADD)
-                direct["biased", g, a] = biased
+                row = bias_row[:, HALF * (k - 3) : HALF * (k - 3 + 1)].rearrange("p (j i) -> p i j", i=2)
+                nc.vector.tensor_tensor(
+                    out=biased[:].rearrange("p e (i j) -> p e i j", i=2),
+                    in0=direct["sum", k, g, a][:].rearrange("p e (i j) -> p e i j", i=2),
+                    in1=row.unsqueeze(1).to_broadcast([P, 2, 2, P]),
+                    op=ADD,
+                )
+                direct["biased", k, g, a] = biased
 
-        def direct_sigmoid(g):
-            direct["prob", g] = work.tile([P, 2, HALF, 2], F32, tag="prob", name="prob", bufs=3)
+        def direct_sigmoid(k, g):
+            direct["prob", k, g] = work.tile([P, 2, HALF, 2], F32, tag="prob", name="prob", bufs=4)
             for a in range(2):
                 nc.scalar.activation(
-                    out=direct["prob", g][:, a, :, :], in_=direct["biased", g, a][:].rearrange("p e j -> p j e"), func=SIGMOID
+                    out=direct["prob", k, g][:, a, :, :],
+                    in_=direct["biased", k, g, a][:].rearrange("p e j -> p j e"),
+                    func=SIGMOID,
                 )
 
-        def direct_weigh(g):
-            grouped["direct", g] = grouped_tile("d_grouped")
+        def direct_weigh(k, g):
+            grouped["direct", k, g] = grouped_tile("d_grouped")
             weights = weight_cols[:, g, :].rearrange("p (a e) -> p a e", a=2).unsqueeze(1)
             nc.vector.tensor_tensor(
-                out=grouped["direct", g][:].rearrange("p (j a e) -> p j a e", a=2, e=2),
-                in0=direct["prob", g][:].rearrange("p a j e -> p j a e"),
+                out=grouped["direct", k, g][:].rearrange("p (j a e) -> p j a e", a=2, e=2),
+                in0=direct["prob", k, g][:].rearrange("p a j e -> p j a e"),
                 in1=weights.to_broadcast([P, HALF, 2, 2]),
                 op=MULT,
             )
 
-        def direct_quant(g):
-            quantise_resid("direct_%d" % g, grouped["direct", g][:], [(TURNED, g), (TURNED + 1, g)])
+        def direct_quant(k, g):
+            quantise_resid("direct_%d_%d" % (k, g), grouped["direct", k, g][:], [(2 * k, g), (2 * k + 1, g)])
 
-        def grad(t, first, end, on_vector=False):
-            acc = psum.tile([P, end - first], F32, tag="bank", name="grad_sum")
-            for g in range(CHUNKS):
+        sums = {}
+
+        def grad_passes(t, first, end, chunks):
+            if (t, first) not in sums:
+                sums[t, first] = psum.tile([P, end - first], F32, tag="bank", name="grad_sum")
+            for g in chunks:
                 nc.tensor.matmul_mx(
-                    out=acc[:],
+                    out=sums[t, first][:],
                     lhsT=r_operand[t, g][0].bitcast(FP8X4),
                     lhsT_scale=r_operand[t, g][1],
                     rhs=bank[:, g, 2 * first : 2 * end].bitcast(FP4X4),
@@ -297,101 +292,143 @@ def tile_siglip_negative_caption_gradient_s13_kernel(
                     start=(g == 0),
                     stop=(g == LAST),
                 )
+
+        def store(t, first, end, on_vector=False):
             if end - first == CHUNK:
-                res = work.tile([P, CHUNK], F32, tag="res", name="res", bufs=6)
+                res = work.tile([P, CHUNK], F32, tag="res", name="res", bufs=5)
             else:
                 res = work.tile([P, end - first], F32, tag="res_part", name="res_part", bufs=2)
             if on_vector:
-                nc.vector.tensor_copy(out=res[:], in_=acc[:])
+                nc.vector.tensor_copy(out=res[:], in_=sums[t, first][:])
             else:
-                nc.scalar.copy(out=res[:], in_=acc[:])
-            rows = out_view[:, t, :] if t < TURNED else out[P * t : P * (t + 1), :]
-            nc.sync.dma_start(out=rows[:, first:end], in_=res[:])
+                nc.scalar.copy(out=res[:], in_=sums[t, first][:])
+            nc.sync.dma_start(out=out_view[t // 2, t % 2][:, first:end], in_=res[:])
+
+        def grad(t, first, end, on_vector=False):
+            grad_passes(t, first, end, range(CHUNKS))
+            store(t, first, end, on_vector)
 
         def grads(t):
             grad(t, 0, CHUNK)
             grad(t, CHUNK, FEATS)
 
-        for h in range(PASSES):
-            spread_scale(h)
-        cap_turn(0)
-        for h in range(PASSES):
-            widen(0, 0, CHUNK * h, CHUNK * (h + 1))
-        cap_turn(1)
-        for a in range(2):
+        def turn_half(g, a):
             for h in range(PASSES):
-                aud_turn(0, a, h)
-                cap_turn(2 + PASSES * a + h)
-            if a == 0:
-                widen(0, 1)
-                aud_quant(0, 0)
-                for t in range(GROUP):
-                    cap_quant(t)
-        probs(range(GROUP), 0, 0, HALF)
-        widen(1, 0)
+                aud_turn(g, a, h)
+
+        for c in range(QUARTERS):
+            spread_scale(c)
+            widen(0, 0, HALF * c, HALF * (c + 1))
+        cap_turn(0)
+        cap_turn(1)
+        aud_turn(0, 0, 0)
+        cap_turn(2)
+        aud_turn(0, 0, 1)
+        for h in range(PASSES):
+            widen(0, 1, CHUNK * h, CHUNK * (h + 1))
+        cap_turn(3)
+        cap_turn(4)
+        aud_turn(0, 1, 0)
+        aud_turn(0, 1, 1)
+        aud_quant(0, 0)
+        cap_quant(0)
         aud_quant(0, 1)
-
-        for g in range(1, CHUNKS):
-            for a in range(2):
-                for h in range(PASSES):
-                    aud_turn(g, a, h)
-                if g == 1:
-                    cap_turn(TURNED + a)
-                if (g, a) == (1, 0):
-                    probs(range(GROUP), 0, HALF, CHUNK)
-                else:
-                    probs(range(GROUP * a, GROUP * (a + 1)), g - 1)
-                if (g, a) == (LAST, 1):
-                    weigh(0, 0)
-                    pair_quant()
-                else:
-                    widen(g + a, 1 - a)
-                aud_quant(g, a)
-                if (g, a) == (1, 0):
-                    for t in range(GROUP, TURNED):
-                        cap_quant(t)
-
+        cap_quant(1)
+        cap_turn(5)
+        cap_turn(6)
+        cap_turn(7)
+        probs(range(4), 0)
+        widen(1, 0)
+        cap_quant(2)
+        turn_half(1, 0)
+        probs(range(4, 6), 0)
+        widen(1, 1)
+        cap_quant(3)
+        turn_half(1, 1)
+        aud_quant(1, 0)
+        direct_logits(3, 0)
+        probs(range(3), 1, 0, HALF)
+        widen(2, 0)
+        aud_quant(1, 1)
+        turn_half(2, 0)
+        probs(range(3), 1, HALF, CHUNK)
+        probs(range(3, 4), 1)
+        widen(2, 1)
+        aud_quant(2, 0)
+        turn_half(2, 1)
+        probs(range(4, 6), 1)
+        widen(3, 0)
+        aud_quant(2, 1)
+        turn_half(3, 0)
+        probs(range(3), 2)
+        widen(3, 1)
+        aud_quant(3, 0)
+        turn_half(3, 1)
+        probs(range(3, 6), 2)
+        direct_bias(3, 0)
+        aud_quant(3, 1)
+        weigh(0, 0)
         weigh(1, 0)
         weigh(2, 0)
-        probs(range(4), LAST)
+        probs(range(6), LAST)
         weigh(0, 1)
         weigh(1, 1)
-        direct_logits(0)
 
-        for t in range(0, TURNED - 2, 2):
-            resid_turn(t)
-            resid_turn(t + 1)
-            if t == 0:
-                weigh(2, 1)
-                probs(range(4, TURNED), LAST)
-            else:
-                direct_bias(0)
-                grads(t - 1)
-                direct_sigmoid(0)
-            resid_quant(t)
-            for tile, d in ((t + 2, 0), (t + 2, 1), (t + 3, 0), (t + 3, 1)):
-                if (tile, d) not in resids:
-                    weigh(tile, d)
-            resid_quant(t + 1)
-            grads(t)
-        resid_turn(TURNED - 2)
-        resid_turn(TURNED - 1)
+        def turn_pair(k):
+            for t in (2 * k, 2 * k + 1):
+                for d in range(2):
+                    resid_turn(t, d)
 
-        direct_weigh(0)
-        for g in range(1, CHUNKS):
-            direct_logits(g)
-            direct_bias(g)
-            direct_sigmoid(g)
-        resid_quant(TURNED - 2)
-        direct_quant(0)
-        direct_weigh(1)
-        resid_quant(TURNED - 1)
+        def quant_tile(t):
+            for d in range(2):
+                resid_quant(t, d)
+
+        def weigh_tile(t):
+            for d in range(2):
+                weigh(t, d)
+
+        direct_logits(3, 1)
+        turn_pair(0)
+        direct_logits(3, 2)
+        direct_sigmoid(3, 0)
+        weigh(2, 1)
+        quant_tile(0)
+        weigh_tile(3)
+        quant_tile(1)
+        grads(0)
+        direct_bias(3, 1)
+        turn_pair(1)
+        direct_sigmoid(3, 1)
+        weigh(4, 0)
+        grads(1)
+        quant_tile(2)
+        weigh(4, 1)
+        weigh_tile(5)
+        grads(2)
+        quant_tile(3)
+        direct_bias(3, 2)
+        turn_pair(2)
+        direct_logits(3, 3)
+        direct_sigmoid(3, 2)
+        direct_weigh(3, 0)
+        direct_bias(3, 3)
+        grads(3)
+        direct_sigmoid(3, 3)
+        quant_tile(4)
+        direct_weigh(3, 1)
+        quant_tile(5)
+        direct_quant(3, 0)
         for g in range(2, CHUNKS):
-            direct_weigh(g)
-            direct_quant(g - 1)
-        direct_quant(LAST)
-        for t in range(TURNED - 3, TILES - 1):
-            grads(t)
+            direct_weigh(3, g)
+            direct_quant(3, g - 1)
+        direct_quant(3, LAST)
+        grads(4)
+        grads(5)
+        for first in (0, CHUNK):
+            grad_passes(6, first, first + CHUNK, range(LAST))
+        for first in (0, CHUNK):
+            grad_passes(6, first, first + CHUNK, [LAST])
+            store(6, first, first + CHUNK)
         grad(TILES - 1, 0, CHUNK)
         grad(TILES - 1, CHUNK, CHUNK + HALF, on_vector=True)
         grad(TILES - 1, CHUNK + HALF, FEATS)

@@ -24,7 +24,7 @@ LAST = CHUNKS - 1
 PASSES = FEATS // CHUNK
 TILES = CAPS // P
 PAIRS = TILES // 2
-QUARTERS = FEATS // HALF
+TURNED = TILES - 2
 WIDE = 4 * HALF
 
 FLOPS = 2 * 2 * CLIPS * CAPS * FEATS
@@ -39,13 +39,13 @@ def tile_siglip_negative_caption_gradient_s13_kernel(
         work = ctx.enter_context(tc.tile_pool(name="work", bufs=3))
         psum = ctx.enter_context(tc.psum_pool(name="psum", bufs=8))
 
-        scale_cols = keep.tile([P, QUARTERS, 2], F32, name="scale_cols")
+        scale_cols = [keep.tile([P, 4], F32, name="scale_cols%d" % h) for h in range(PASSES)]
         scale_all = keep.tile([P, FEATS], F32, name="scale_all")
         raw_first = [keep.tile([P, 2 * FEATS], U8, name="raw_first%d" % a) for a in range(2)]
         raw_later = [keep.tile([P, 4 * FEATS], U8, name="raw_later%d" % g) for g in range(1, CHUNKS)]
         cap_rows = [keep.tile([P, FEATS], BF16, name="cap_rows%d" % t) for t in range(TILES)]
         weight_all = keep.tile([P, CLIPS], BF16, name="weight_all")
-        bias_cols = keep.tile([P, PAIRS, 2], BF16, name="bias_cols")
+        bias_cols = keep.tile([P, TURNED], BF16, name="bias_cols")
         bank = keep.tile([P, CHUNKS, 2 * FEATS], U8, align_bytes=64, name="bank")
         bank_sc = keep.tile([P, CHUNKS, FEATS], U8, align_bytes=64, name="bank_sc")
         ident = keep.tile([P, P], F32, name="ident")
@@ -66,11 +66,19 @@ def tile_siglip_negative_caption_gradient_s13_kernel(
         nc.gpsimd.memset(bank_sc[:].rearrange("p g d -> p (g d)").bitcast(U32), 0)
 
         aud_view = audio_bytes.rearrange("(g q s) d -> g q (s d)", q=P, s=4)
-        cap_view = captions.rearrange("(k p i) d -> k i p d", p=P, i=2)
-        out_view = out.rearrange("(k p i) d -> k i p d", p=P, i=2)
+
+        def tile_rows(matrix, t):
+            if t < TURNED:
+                return matrix[: P * TURNED, :].rearrange("(p t) d -> p t d", t=TURNED)[:, t, :]
+            return matrix[P * t : P * (t + 1), :]
+
+        def load_scale(h):
+            nc.sync.dma_start(
+                out=scale_cols[h][:], in_=audio_scale[0, CHUNK * h : CHUNK * (h + 1)].rearrange("(n m) -> n m", m=4)
+            )
 
         def load_cap(t):
-            nc.sync.dma_start(out=cap_rows[t][:], in_=cap_view[t // 2, t % 2])
+            nc.sync.dma_start(out=cap_rows[t][:], in_=tile_rows(captions, t))
 
         def load_first_half(a):
             nc.sync.dma_start(out=raw_first[a][:], in_=aud_view[0][:, 2 * a * FEATS : 2 * (a + 1) * FEATS])
@@ -78,18 +86,24 @@ def tile_siglip_negative_caption_gradient_s13_kernel(
         def load_chunk(g):
             nc.sync.dma_start(out=raw_later[g - 1][:], in_=aud_view[g])
 
-        nc.sync.dma_start(out=scale_cols[:], in_=audio_scale.rearrange("o (c n m) -> n (o c) m", c=QUARTERS, m=2))
+        load_scale(0)
+        load_scale(1)
         load_first_half(0)
-        for t in range(3):
-            load_cap(t)
+        load_cap(0)
+        load_cap(1)
+        load_cap(2)
         load_first_half(1)
-        for t in range(3, TILES):
-            load_cap(t)
-        nc.sync.dma_start(out=bias_cols[:], in_=bias.rearrange("(k p i) -> p k i", p=P, i=2))
-        for g in range(1, CHUNKS):
+        load_cap(3)
+        load_cap(4)
+        load_cap(5)
+        load_cap(6)
+        load_cap(7)
+        nc.sync.dma_start(out=bias_cols[:], in_=bias[: P * TURNED].rearrange("(p t) -> p t", t=TURNED))
+        load_chunk(1)
+        for g in range(2, CHUNKS):
             load_chunk(g)
         nc.sync.dma_start(out=weight_all[:], in_=clip_weight.partition_broadcast(P))
-        nc.sync.dma_start(out=bias_row[:], in_=bias[HALF * 3 :].partition_broadcast(P))
+        nc.sync.dma_start(out=bias_row[:], in_=bias[P * TURNED :].partition_broadcast(P))
         nc.sync.dma_start(out=bank[:], in_=bank_words.rearrange("g p n -> p g n"))
         for r in range(4):
             nc.sync.dma_start(
@@ -103,12 +117,12 @@ def tile_siglip_negative_caption_gradient_s13_kernel(
 
         grouped = {}
 
-        def spread_scale(c):
-            xt = psum.tile([P, 2, P], F32, tag="bank", name="spread")
-            for m in range(2):
-                nc.tensor.transpose(xt[:, m, :], scale_cols[:, c, m : m + 1].to_broadcast([P, P]), ident[:])
+        def spread_scale(h):
+            xt = psum.tile([P, 4, P], F32, tag="bank", name="spread")
+            for m in range(4):
+                nc.tensor.transpose(xt[:, m, :], scale_cols[h][:, m : m + 1].to_broadcast([P, P]), ident[:])
             nc.scalar.copy(
-                out=scale_all[:, HALF * c : HALF * (c + 1)].rearrange("p (n m) -> p n m", m=2),
+                out=scale_all[:, CHUNK * h : CHUNK * (h + 1)].rearrange("p (n m) -> p n m", m=4),
                 in_=xt[:].rearrange("p m n -> p n m"),
             )
 
@@ -189,7 +203,7 @@ def tile_siglip_negative_caption_gradient_s13_kernel(
                     out=sigs[t, g // 2][:, g % 2, first:end].rearrange("p (a q e) -> p a q e", q=P, e=2),
                     in_=acc[:].rearrange("p (a e q) -> p a q e", q=P, e=2),
                     func=SIGMOID,
-                    bias=bias_cols[:, t // 2, t % 2 : t % 2 + 1],
+                    bias=bias_cols[:, t : t + 1],
                 )
 
         def weigh(t, d):
@@ -246,13 +260,8 @@ def tile_siglip_negative_caption_gradient_s13_kernel(
         def direct_bias(k, g):
             for a in range(2):
                 biased = work.tile([P, 2, HALF], F32, tag="biased", name="biased", bufs=4)
-                row = bias_row[:, HALF * (k - 3) : HALF * (k - 3 + 1)].rearrange("p (j i) -> p i j", i=2)
-                nc.vector.tensor_tensor(
-                    out=biased[:].rearrange("p e (i j) -> p e i j", i=2),
-                    in0=direct["sum", k, g, a][:].rearrange("p e (i j) -> p e i j", i=2),
-                    in1=row.unsqueeze(1).to_broadcast([P, 2, 2, P]),
-                    op=ADD,
-                )
+                row = bias_row[:].unsqueeze(1).to_broadcast([P, 2, HALF])
+                nc.vector.tensor_tensor(out=biased[:], in0=direct["sum", k, g, a][:], in1=row, op=ADD)
                 direct["biased", k, g, a] = biased
 
         def direct_sigmoid(k, g):
@@ -302,7 +311,7 @@ def tile_siglip_negative_caption_gradient_s13_kernel(
                 nc.vector.tensor_copy(out=res[:], in_=sums[t, first][:])
             else:
                 nc.scalar.copy(out=res[:], in_=sums[t, first][:])
-            nc.sync.dma_start(out=out_view[t // 2, t % 2][:, first:end], in_=res[:])
+            nc.sync.dma_start(out=tile_rows(out, t)[:, first:end], in_=res[:])
 
         def grad(t, first, end, on_vector=False):
             grad_passes(t, first, end, range(CHUNKS))
@@ -316,9 +325,9 @@ def tile_siglip_negative_caption_gradient_s13_kernel(
             for h in range(PASSES):
                 aud_turn(g, a, h)
 
-        for c in range(QUARTERS):
-            spread_scale(c)
-            widen(0, 0, HALF * c, HALF * (c + 1))
+        for h in range(PASSES):
+            spread_scale(h)
+            widen(0, 0, CHUNK * h, CHUNK * (h + 1))
         cap_turn(0)
         cap_turn(1)
         aud_turn(0, 0, 0)

@@ -43,9 +43,12 @@ def tile_siglip_negative_caption_gradient_s13_kernel(
         scale_all = keep.tile([P, FEATS], F32, name="scale_all")
         raw_first = [keep.tile([P, 2 * FEATS], U8, name="raw_first%d" % a) for a in range(2)]
         raw_later = [keep.tile([P, 4 * FEATS], U8, name="raw_later%d" % g) for g in range(1, CHUNKS)]
-        cap_rows = [keep.tile([P, FEATS], BF16, name="cap_rows%d" % t) for t in range(TILES)]
+        cap_rows = [
+            work.tile([P, FEATS], BF16, align_bytes=64, tag="resid", name="cap_rows%d" % t, bufs=9) for t in range(TILES)
+        ]
         weight_all = keep.tile([P, CLIPS], BF16, name="weight_all")
         bias_cols = keep.tile([P, TURNED], BF16, name="bias_cols")
+        bias_cols_last = keep.tile([P, 2], BF16, name="bias_cols_last")
         bank = keep.tile([P, CHUNKS, 2 * FEATS], U8, align_bytes=64, name="bank")
         bank_sc = keep.tile([P, CHUNKS, FEATS], U8, align_bytes=64, name="bank_sc")
         ident = keep.tile([P, P], F32, name="ident")
@@ -70,7 +73,7 @@ def tile_siglip_negative_caption_gradient_s13_kernel(
         def tile_rows(matrix, t):
             if t < TURNED:
                 return matrix[: P * TURNED, :].rearrange("(p t) d -> p t d", t=TURNED)[:, t, :]
-            return matrix[P * t : P * (t + 1), :]
+            return matrix[P * TURNED :, :].rearrange("(p i) d -> p i d", i=2)[:, t - TURNED, :]
 
         def load_scale(h):
             nc.sync.dma_start(
@@ -88,18 +91,19 @@ def tile_siglip_negative_caption_gradient_s13_kernel(
 
         load_scale(0)
         load_scale(1)
-        load_first_half(0)
         load_cap(0)
+        load_first_half(0)
         load_cap(1)
         load_cap(2)
         load_first_half(1)
         load_cap(3)
         load_cap(4)
         load_cap(5)
-        load_cap(6)
-        load_cap(7)
         nc.sync.dma_start(out=bias_cols[:], in_=bias[: P * TURNED].rearrange("(p t) -> p t", t=TURNED))
+        load_cap(6)
         load_chunk(1)
+        load_cap(7)
+        nc.sync.dma_start(out=bias_cols_last[:], in_=bias[P * TURNED :].rearrange("(p i) -> p i", i=2))
         for g in range(2, CHUNKS):
             load_chunk(g)
         nc.sync.dma_start(out=weight_all[:], in_=clip_weight.partition_broadcast(P))
@@ -113,7 +117,7 @@ def tile_siglip_negative_caption_gradient_s13_kernel(
         nc.sync.dma_start(out=weight_cols[:], in_=clip_weight.rearrange("(g p t) -> p g t", p=P, t=4))
 
         def grouped_tile(name):
-            return work.tile([P, WIDE], BF16, align_bytes=64, tag="grouped", name=name, bufs=7)
+            return work.tile([P, WIDE], BF16, align_bytes=64, tag="grouped", name=name, bufs=10)
 
         grouped = {}
 
@@ -198,16 +202,16 @@ def tile_siglip_negative_caption_gradient_s13_kernel(
                         stop=(h == PASSES - 1),
                     )
                 if (t, g // 2) not in sigs:
-                    sigs[t, g // 2] = work.tile([P, 2, CHUNK], F32, tag="sig", name="sig", bufs=12)
+                    sigs[t, g // 2] = work.tile([P, 2, CHUNK], F32, tag="sig", name="sig", bufs=14)
                 nc.scalar.activation(
                     out=sigs[t, g // 2][:, g % 2, first:end].rearrange("p (a q e) -> p a q e", q=P, e=2),
                     in_=acc[:].rearrange("p (a e q) -> p a q e", q=P, e=2),
                     func=SIGMOID,
-                    bias=bias_cols[:, t : t + 1],
+                    bias=bias_cols[:, t : t + 1] if t < TURNED else bias_cols_last[:, t - TURNED : t - TURNED + 1],
                 )
 
         def weigh(t, d):
-            resids[t, d] = work.tile([P, 2 * CHUNK], BF16, align_bytes=64, tag="resid", name="resid", bufs=6)
+            resids[t, d] = work.tile([P, 2 * CHUNK], BF16, align_bytes=64, tag="resid", name="resid", bufs=9)
             weights = weight_all[:, 2 * CHUNK * d : 2 * CHUNK * (d + 1)]
             nc.vector.tensor_tensor(
                 out=resids[t, d][:].rearrange("p (a c q e) -> p a c q e", a=2, c=2, e=2),
@@ -260,12 +264,17 @@ def tile_siglip_negative_caption_gradient_s13_kernel(
         def direct_bias(k, g):
             for a in range(2):
                 biased = work.tile([P, 2, HALF], F32, tag="biased", name="biased", bufs=4)
-                row = bias_row[:].unsqueeze(1).to_broadcast([P, 2, HALF])
-                nc.vector.tensor_tensor(out=biased[:], in0=direct["sum", k, g, a][:], in1=row, op=ADD)
+                row = bias_row[:].rearrange("p (j i) -> p i j", i=2).unsqueeze(1)
+                nc.vector.tensor_tensor(
+                    out=biased[:].rearrange("p e (i j) -> p e i j", i=2),
+                    in0=direct["sum", k, g, a][:].rearrange("p e (i j) -> p e i j", i=2),
+                    in1=row.to_broadcast([P, 2, 2, P]),
+                    op=ADD,
+                )
                 direct["biased", k, g, a] = biased
 
         def direct_sigmoid(k, g):
-            direct["prob", k, g] = work.tile([P, 2, HALF, 2], F32, tag="prob", name="prob", bufs=4)
+            direct["prob", k, g] = work.tile([P, 2, HALF, 2], F32, tag="prob", name="prob", bufs=2)
             for a in range(2):
                 nc.scalar.activation(
                     out=direct["prob", k, g][:, a, :, :],
@@ -325,64 +334,6 @@ def tile_siglip_negative_caption_gradient_s13_kernel(
             for h in range(PASSES):
                 aud_turn(g, a, h)
 
-        for h in range(PASSES):
-            spread_scale(h)
-            widen(0, 0, CHUNK * h, CHUNK * (h + 1))
-        cap_turn(0)
-        cap_turn(1)
-        aud_turn(0, 0, 0)
-        cap_turn(2)
-        aud_turn(0, 0, 1)
-        for h in range(PASSES):
-            widen(0, 1, CHUNK * h, CHUNK * (h + 1))
-        cap_turn(3)
-        cap_turn(4)
-        aud_turn(0, 1, 0)
-        aud_turn(0, 1, 1)
-        aud_quant(0, 0)
-        cap_quant(0)
-        aud_quant(0, 1)
-        cap_quant(1)
-        cap_turn(5)
-        cap_turn(6)
-        cap_turn(7)
-        probs(range(4), 0)
-        widen(1, 0)
-        cap_quant(2)
-        turn_half(1, 0)
-        probs(range(4, 6), 0)
-        widen(1, 1)
-        cap_quant(3)
-        turn_half(1, 1)
-        aud_quant(1, 0)
-        direct_logits(3, 0)
-        probs(range(3), 1, 0, HALF)
-        widen(2, 0)
-        aud_quant(1, 1)
-        turn_half(2, 0)
-        probs(range(3), 1, HALF, CHUNK)
-        probs(range(3, 4), 1)
-        widen(2, 1)
-        aud_quant(2, 0)
-        turn_half(2, 1)
-        probs(range(4, 6), 1)
-        widen(3, 0)
-        aud_quant(2, 1)
-        turn_half(3, 0)
-        probs(range(3), 2)
-        widen(3, 1)
-        aud_quant(3, 0)
-        turn_half(3, 1)
-        probs(range(3, 6), 2)
-        direct_bias(3, 0)
-        aud_quant(3, 1)
-        weigh(0, 0)
-        weigh(1, 0)
-        weigh(2, 0)
-        probs(range(6), LAST)
-        weigh(0, 1)
-        weigh(1, 1)
-
         def turn_pair(k):
             for t in (2 * k, 2 * k + 1):
                 for d in range(2):
@@ -396,18 +347,77 @@ def tile_siglip_negative_caption_gradient_s13_kernel(
             for d in range(2):
                 weigh(t, d)
 
-        direct_logits(3, 1)
-        turn_pair(0)
+        for h in range(PASSES):
+            spread_scale(h)
+        cap_turn(0)
+        for h in range(PASSES):
+            widen(0, 0, CHUNK * h, CHUNK * (h + 1))
+        cap_turn(1)
+        aud_turn(0, 0, 0)
+        cap_turn(2)
+        aud_turn(0, 0, 1)
+        for h in range(PASSES):
+            widen(0, 1, CHUNK * h, CHUNK * (h + 1))
+        cap_turn(3)
+        cap_turn(4)
+        aud_turn(0, 1, 0)
+        cap_turn(5)
+        aud_turn(0, 1, 1)
+        cap_turn(6)
+        aud_quant(0, 0)
+        for k in range(3):
+            cap_quant(k)
+        probs(range(6), 0, 0, HALF)
+        widen(1, 0)
+        aud_quant(0, 1)
+        cap_turn(7)
+        turn_half(1, 0)
+        probs(range(6), 0, HALF, CHUNK)
+        widen(1, 1)
+        cap_quant(3)
+        aud_quant(1, 0)
+        turn_half(1, 1)
+        probs(range(6, 8), 0)
+        probs(range(2), 1, 0, HALF)
+        widen(2, 0)
+        aud_quant(1, 1)
+        turn_half(2, 0)
+        probs(range(2), 1, HALF, CHUNK)
+        probs(range(2, 4), 1)
+        widen(2, 1)
+        aud_quant(2, 0)
+        turn_half(2, 1)
+        probs(range(4, 7), 1)
+        widen(3, 0)
+        aud_quant(2, 1)
+        turn_half(3, 0)
+        probs(range(7, 8), 1)
+        probs(range(2), 2)
+        widen(3, 1)
+        aud_quant(3, 0)
+        turn_half(3, 1)
+        probs(range(2, 6), 2)
+        weigh(0, 0)
+        weigh(1, 0)
+        aud_quant(3, 1)
+        weigh(6, 0)
+        weigh(7, 0)
+        probs(range(6), LAST)
+        weigh(0, 1)
+        weigh(1, 1)
         direct_logits(3, 2)
-        direct_sigmoid(3, 0)
-        weigh(2, 1)
+        turn_pair(0)
+        resid_turn(6, 0)
+        resid_turn(7, 0)
+        direct_logits(3, 3)
+        weigh_tile(2)
         quant_tile(0)
         weigh_tile(3)
         quant_tile(1)
         grads(0)
-        direct_bias(3, 1)
+        direct_bias(3, 2)
         turn_pair(1)
-        direct_sigmoid(3, 1)
+        direct_sigmoid(3, 2)
         weigh(4, 0)
         grads(1)
         quant_tile(2)
@@ -415,29 +425,21 @@ def tile_siglip_negative_caption_gradient_s13_kernel(
         weigh_tile(5)
         grads(2)
         quant_tile(3)
-        direct_bias(3, 2)
-        turn_pair(2)
-        direct_logits(3, 3)
-        direct_sigmoid(3, 2)
-        direct_weigh(3, 0)
         direct_bias(3, 3)
-        grads(3)
+        turn_pair(2)
         direct_sigmoid(3, 3)
+        direct_weigh(3, 2)
+        grads(3)
         quant_tile(4)
-        direct_weigh(3, 1)
+        resid_quant(6, 0)
+        direct_quant(3, 2)
         quant_tile(5)
-        direct_quant(3, 0)
-        for g in range(2, CHUNKS):
-            direct_weigh(3, g)
-            direct_quant(3, g - 1)
-        direct_quant(3, LAST)
+        direct_weigh(3, 3)
+        resid_quant(7, 0)
+        direct_quant(3, 3)
         grads(4)
         grads(5)
-        for first in (0, CHUNK):
-            grad_passes(6, first, first + CHUNK, range(LAST))
-        for first in (0, CHUNK):
-            grad_passes(6, first, first + CHUNK, [LAST])
-            store(6, first, first + CHUNK)
+        grads(6)
         grad(TILES - 1, 0, CHUNK)
         grad(TILES - 1, CHUNK, CHUNK + HALF, on_vector=True)
         grad(TILES - 1, CHUNK + HALF, FEATS)

@@ -138,7 +138,7 @@ def tile_siglip_negative_caption_gradient_s13_kernel(
                     nc.tensor.transpose(xt[:, h, u, :], words[:, HALF * h + u : HALF * (h + 1) : 2], ident[:])
             if t % 2 == 0:
                 grouped["cap", t // 2] = work.tile(
-                    [P, PASSES, 2, CHUNK], BF16, align_bytes=64, tag="cap_grouped", name="cap_grouped", bufs=3
+                    [P, PASSES, 2, CHUNK], BF16, align_bytes=64, tag="cap_grouped", name="cap_grouped", bufs=4
                 )
             nc.scalar.copy(
                 out=grouped["cap", t // 2][:, :, t % 2, :].bitcast(F32).rearrange("p h (j u) -> p h j u", u=2),
@@ -374,45 +374,42 @@ def tile_siglip_negative_caption_gradient_s13_kernel(
         turn_half(1, 0)
         probs(range(6), 0, HALF, CHUNK)
         widen(1, 1)
-        cap_quant(3)
         aud_quant(1, 0)
         turn_half(1, 1)
-        probs(range(6, 8), 0)
-        probs(range(2), 1, 0, HALF)
+        probs(range(6), 1, 0, HALF)
         widen(2, 0)
         aud_quant(1, 1)
+        cap_quant(3)
         turn_half(2, 0)
-        probs(range(2), 1, HALF, CHUNK)
-        probs(range(2, 4), 1)
+        probs(range(6), 1, HALF, CHUNK)
         widen(2, 1)
         aud_quant(2, 0)
+        probs(range(6, 7), 0)
         turn_half(2, 1)
-        probs(range(4, 7), 1)
+        probs(range(7, 8), 0)
+        probs(range(6, 8), 1)
         widen(3, 0)
         aud_quant(2, 1)
         turn_half(3, 0)
-        probs(range(7, 8), 1)
-        probs(range(2), 2)
+        probs(range(3), 2)
         widen(3, 1)
         aud_quant(3, 0)
         turn_half(3, 1)
-        probs(range(2, 6), 2)
+        probs(range(3, 6), 2)
         weigh(0, 0)
-        weigh(1, 0)
         aud_quant(3, 1)
-        weigh(6, 0)
-        weigh(7, 0)
+        weigh(1, 0)
+        weigh(2, 0)
         probs(range(6), LAST)
         weigh(0, 1)
         weigh(1, 1)
         direct_logits(3, 2)
         turn_pair(0)
-        resid_turn(6, 0)
-        resid_turn(7, 0)
         direct_logits(3, 3)
-        weigh_tile(2)
+        weigh(2, 1)
+        weigh(3, 0)
         quant_tile(0)
-        weigh_tile(3)
+        weigh(3, 1)
         quant_tile(1)
         grads(0)
         direct_bias(3, 2)
@@ -428,16 +425,20 @@ def tile_siglip_negative_caption_gradient_s13_kernel(
         direct_bias(3, 3)
         turn_pair(2)
         direct_sigmoid(3, 3)
-        direct_weigh(3, 2)
         grads(3)
         quant_tile(4)
+        weigh(6, 0)
+        weigh(7, 0)
+        grads(4)
+        quant_tile(5)
+        resid_turn(6, 0)
+        resid_turn(7, 0)
+        direct_weigh(3, 2)
+        direct_weigh(3, 3)
         resid_quant(6, 0)
         direct_quant(3, 2)
-        quant_tile(5)
-        direct_weigh(3, 3)
-        resid_quant(7, 0)
         direct_quant(3, 3)
-        grads(4)
+        resid_quant(7, 0)
         grads(5)
         grads(6)
         grad(TILES - 1, 0, CHUNK)

@@ -125,10 +125,14 @@ def tile_siglip_negative_caption_gradient_s13_kernel(
             xt = psum.tile([P, 4, P], F32, tag="bank", name="spread")
             for m in range(4):
                 nc.tensor.transpose(xt[:, m, :], scale_cols[h][:, m : m + 1].to_broadcast([P, P]), ident[:])
-            nc.scalar.copy(
-                out=scale_all[:, CHUNK * h : CHUNK * (h + 1)].rearrange("p (n m) -> p n m", m=4),
-                in_=xt[:].rearrange("p m n -> p n m"),
-            )
+            pieces = 2 if h == 0 else 1
+            width = P // pieces
+            for c in range(pieces):
+                first = CHUNK * h + 4 * width * c
+                nc.scalar.copy(
+                    out=scale_all[:, first : first + 4 * width].rearrange("p (n m) -> p n m", m=4),
+                    in_=xt[:, :, width * c : width * (c + 1)].rearrange("p m n -> p n m"),
+                )
 
         def cap_turn(t):
             xt = psum.tile([P, PASSES, 2, P], F32, tag="bank", name="cap_xt")
@@ -313,9 +317,9 @@ def tile_siglip_negative_caption_gradient_s13_kernel(
 
         def store(t, first, end, on_vector=False):
             if end - first == CHUNK:
-                res = work.tile([P, CHUNK], F32, tag="res", name="res", bufs=5)
+                res = work.tile([P, CHUNK], F32, tag="res", name="res", bufs=4)
             else:
-                res = work.tile([P, end - first], F32, tag="res_part", name="res_part", bufs=2)
+                res = work.tile([P, end - first], F32, tag="res_part", name="res_part", bufs=4)
             if on_vector:
                 nc.vector.tensor_copy(out=res[:], in_=sums[t, first][:])
             else:
@@ -350,8 +354,8 @@ def tile_siglip_negative_caption_gradient_s13_kernel(
         for h in range(PASSES):
             spread_scale(h)
         cap_turn(0)
-        for h in range(PASSES):
-            widen(0, 0, CHUNK * h, CHUNK * (h + 1))
+        for first, end in ((0, HALF), (HALF, CHUNK), (CHUNK, FEATS)):
+            widen(0, 0, first, end)
         cap_turn(1)
         aud_turn(0, 0, 0)
         cap_turn(2)
@@ -441,6 +445,6 @@ def tile_siglip_negative_caption_gradient_s13_kernel(
         resid_quant(7, 0)
         grads(5)
         grads(6)
-        grad(TILES - 1, 0, CHUNK)
-        grad(TILES - 1, CHUNK, CHUNK + HALF, on_vector=True)
-        grad(TILES - 1, CHUNK + HALF, FEATS)
+        edges = (0, HALF, CHUNK, CHUNK + HALF, FEATS - P, FEATS)
+        for n in range(len(edges) - 1):
+            grad(TILES - 1, edges[n], edges[n + 1], on_vector=(n % 2 == 1))

@@ -134,12 +134,23 @@ def tile_siglip_negative_caption_gradient_s13_kernel(
                     in_=xt[:, :, width * c : width * (c + 1)].rearrange("p m n -> p n m"),
                 )
 
+        def cap_sort(t):
+            in_order = grouped_tile("cap_in_order")
+            nc.scalar.copy(
+                out=in_order[:].bitcast(F32).rearrange("p (h u n) -> p h u n", h=PASSES, u=2),
+                in_=cap_rows[t][:].bitcast(F32).rearrange("p (h n u) -> p h u n", h=PASSES, u=2),
+            )
+            grouped["sorted", t] = in_order
+
         def cap_turn(t):
             xt = psum.tile([P, PASSES, 2, P], F32, tag="bank", name="cap_xt")
-            words = cap_rows[t][:].bitcast(F32)
             for h in range(PASSES):
                 for u in range(2):
-                    nc.tensor.transpose(xt[:, h, u, :], words[:, HALF * h + u : HALF * (h + 1) : 2], ident[:])
+                    if ("sorted", t) in grouped:
+                        run = grouped["sorted", t][:].bitcast(F32)[:, HALF * h + P * u : HALF * h + P * (u + 1)]
+                    else:
+                        run = cap_rows[t][:].bitcast(F32)[:, HALF * h + u : HALF * (h + 1) : 2]
+                    nc.tensor.transpose(xt[:, h, u, :], run, ident[:])
             if t % 2 == 0:
                 grouped["cap", t // 2] = work.tile(
                     [P, PASSES, 2, CHUNK], BF16, align_bytes=64, tag="cap_grouped", name="cap_grouped", bufs=4
@@ -317,9 +328,9 @@ def tile_siglip_negative_caption_gradient_s13_kernel(
 
         def store(t, first, end, on_vector=False):
             if end - first == CHUNK:
-                res = work.tile([P, CHUNK], F32, tag="res", name="res", bufs=4)
+                res = work.tile([P, CHUNK], F32, tag="res", name="res", bufs=5)
             else:
-                res = work.tile([P, end - first], F32, tag="res_part", name="res_part", bufs=4)
+                res = work.tile([P, end - first], F32, align_bytes=64, tag="resid", name="res_part", bufs=9)
             if on_vector:
                 nc.vector.tensor_copy(out=res[:], in_=sums[t, first][:])
             else:
@@ -368,6 +379,7 @@ def tile_siglip_negative_caption_gradient_s13_kernel(
         cap_turn(5)
         aud_turn(0, 1, 1)
         cap_turn(6)
+        cap_sort(7)
         aud_quant(0, 0)
         for k in range(3):
             cap_quant(k)

@@ -24,8 +24,16 @@ LAST = CHUNKS - 1
 PASSES = FEATS // CHUNK
 TILES = CAPS // P
 PAIRS = TILES // 2
-TURNED = TILES - 2
+LAST_PAIR = PAIRS - 1
+TURNED = 2 * LAST_PAIR
+FIRST_DIRECT = CHUNKS - 2
 WIDE = 4 * HALF
+
+ROW_BUFS = TILES + 1
+GROUPED_BUFS = 10
+AUDIO_BUFS = 6
+SIG_BUFS = 2 * TURNED + 2
+RES_BUFS = 5
 
 FLOPS = 2 * 2 * CLIPS * CAPS * FEATS
 
@@ -44,7 +52,8 @@ def tile_siglip_negative_caption_gradient_s13_kernel(
         raw_first = [keep.tile([P, 2 * FEATS], U8, name="raw_first%d" % a) for a in range(2)]
         raw_later = [keep.tile([P, 4 * FEATS], U8, name="raw_later%d" % g) for g in range(1, CHUNKS)]
         cap_rows = [
-            work.tile([P, FEATS], BF16, align_bytes=64, tag="resid", name="cap_rows%d" % t, bufs=9) for t in range(TILES)
+            work.tile([P, FEATS], BF16, align_bytes=64, tag="rows", name="cap_rows%d" % t, bufs=ROW_BUFS)
+            for t in range(TILES)
         ]
         weight_all = keep.tile([P, CLIPS], BF16, name="weight_all")
         bias_cols = keep.tile([P, TURNED], BF16, name="bias_cols")
@@ -57,7 +66,7 @@ def tile_siglip_negative_caption_gradient_s13_kernel(
         cap_codes = [keep.tile([P, PASSES, 2 * P], U32, align_bytes=64, name="cap_codes%d" % k) for k in range(PAIRS)]
         cap_sc = [keep.tile([P, PASSES, 2 * P], U8, align_bytes=64, name="cap_sc%d" % k) for k in range(PAIRS)]
         bias_row = keep.tile([P, HALF], BF16, name="bias_row")
-        weight_cols = keep.tile([P, CHUNKS, 4], BF16, name="weight_cols")
+        weight_cols = keep.tile([P, CHUNKS - FIRST_DIRECT, 4], BF16, name="weight_cols")
 
         ctx.enter_context(tc.manual_schedule())
 
@@ -89,35 +98,36 @@ def tile_siglip_negative_caption_gradient_s13_kernel(
         def load_chunk(g):
             nc.sync.dma_start(out=raw_later[g - 1][:], in_=aud_view[g])
 
-        load_scale(0)
-        load_scale(1)
+        for h in range(PASSES):
+            load_scale(h)
         load_cap(0)
         load_first_half(0)
-        load_cap(1)
-        load_cap(2)
+        for t in (1, 2):
+            load_cap(t)
         load_first_half(1)
-        load_cap(3)
-        load_cap(4)
-        load_cap(5)
+        for t in range(3, TURNED):
+            load_cap(t)
         nc.sync.dma_start(out=bias_cols[:], in_=bias[: P * TURNED].rearrange("(p t) -> p t", t=TURNED))
-        load_cap(6)
+        load_cap(TURNED)
         load_chunk(1)
-        load_cap(7)
+        load_cap(TURNED + 1)
         nc.sync.dma_start(out=bias_cols_last[:], in_=bias[P * TURNED :].rearrange("(p i) -> p i", i=2))
         for g in range(2, CHUNKS):
             load_chunk(g)
         nc.sync.dma_start(out=weight_all[:], in_=clip_weight.partition_broadcast(P))
         nc.sync.dma_start(out=bias_row[:], in_=bias[P * TURNED :].partition_broadcast(P))
         nc.sync.dma_start(out=bank[:], in_=bank_words.rearrange("g p n -> p g n"))
-        for r in range(4):
+        for n in range(4):
             nc.sync.dma_start(
-                out=bank_sc[32 * r : 32 * r + 4, :, :].bitcast(I32),
-                in_=bank_scales[:, 4 * r : 4 * r + 4, :].rearrange("g r n -> r g n").bitcast(I32),
+                out=bank_sc[32 * n : 32 * n + 4, :, :].bitcast(I32),
+                in_=bank_scales[:, 4 * n : 4 * n + 4, :].rearrange("g b d -> b g d").bitcast(I32),
             )
-        nc.sync.dma_start(out=weight_cols[:], in_=clip_weight.rearrange("(g p t) -> p g t", p=P, t=4))
+        nc.sync.dma_start(
+            out=weight_cols[:], in_=clip_weight[CHUNK * FIRST_DIRECT :].rearrange("(g q s) -> q g s", q=P, s=4)
+        )
 
         def grouped_tile(name):
-            return work.tile([P, WIDE], BF16, align_bytes=64, tag="grouped", name=name, bufs=10)
+            return work.tile([P, WIDE], BF16, align_bytes=64, tag="grouped", name=name, bufs=GROUPED_BUFS)
 
         grouped = {}
 
@@ -153,7 +163,7 @@ def tile_siglip_negative_caption_gradient_s13_kernel(
                     nc.tensor.transpose(xt[:, h, u, :], run, ident[:])
             if t % 2 == 0:
                 grouped["cap", t // 2] = work.tile(
-                    [P, PASSES, 2, CHUNK], BF16, align_bytes=64, tag="cap_grouped", name="cap_grouped", bufs=4
+                    [P, PASSES, 2, CHUNK], BF16, align_bytes=64, tag="cap_grouped", name="cap_grouped", bufs=PAIRS
                 )
             nc.scalar.copy(
                 out=grouped["cap", t // 2][:, :, t % 2, :].bitcast(F32).rearrange("p h (j u) -> p h j u", u=2),
@@ -173,8 +183,11 @@ def tile_siglip_negative_caption_gradient_s13_kernel(
             for e in range(2):
                 s = 2 * a + e
                 if first == 0:
-                    audio[g, s] = work.tile([P, FEATS], BF16, align_bytes=64, tag="audio", name="audio", bufs=6)
-                raw = raw_first[a][:, e * FEATS : (e + 1) * FEATS] if g == 0 else raw_later[g - 1][:, s * FEATS : (s + 1) * FEATS]
+                    audio[g, s] = work.tile([P, FEATS], BF16, align_bytes=64, tag="audio", name="audio", bufs=AUDIO_BUFS)
+                if g == 0:
+                    raw = raw_first[a][:, e * FEATS : (e + 1) * FEATS]
+                else:
+                    raw = raw_later[g - 1][:, s * FEATS : (s + 1) * FEATS]
                 nc.vector.tensor_tensor(
                     out=audio[g, s][:, first:end], in0=raw[:, first:end].bitcast(FP8), in1=scale_all[:, first:end], op=MULT
                 )
@@ -191,9 +204,9 @@ def tile_siglip_negative_caption_gradient_s13_kernel(
                 in_=xt[:].rearrange("p e u q -> p e q u"),
             )
 
-        def aud_quant(g, a, passes=range(PASSES)):
+        def aud_quant(g, a):
             cols = slice(HALF * a, HALF * (a + 1))
-            for h in passes:
+            for h in range(PASSES):
                 nc.vector.quantize_mx(
                     out=aud_codes[g][:, h, cols].bitcast(FP8X4), scales=aud_sc[g][:, h, cols], in_=grouped["aud", g, a, h][:]
                 )
@@ -217,7 +230,7 @@ def tile_siglip_negative_caption_gradient_s13_kernel(
                         stop=(h == PASSES - 1),
                     )
                 if (t, g // 2) not in sigs:
-                    sigs[t, g // 2] = work.tile([P, 2, CHUNK], F32, tag="sig", name="sig", bufs=14)
+                    sigs[t, g // 2] = work.tile([P, 2, CHUNK], F32, tag="sig", name="sig", bufs=SIG_BUFS)
                 nc.scalar.activation(
                     out=sigs[t, g // 2][:, g % 2, first:end].rearrange("p (a q e) -> p a q e", q=P, e=2),
                     in_=acc[:].rearrange("p (a e q) -> p a q e", q=P, e=2),
@@ -225,25 +238,25 @@ def tile_siglip_negative_caption_gradient_s13_kernel(
                     bias=bias_cols[:, t : t + 1] if t < TURNED else bias_cols_last[:, t - TURNED : t - TURNED + 1],
                 )
 
-        def weigh(t, d):
-            resids[t, d] = work.tile([P, 2 * CHUNK], BF16, align_bytes=64, tag="resid", name="resid", bufs=9)
-            weights = weight_all[:, 2 * CHUNK * d : 2 * CHUNK * (d + 1)]
+        def weigh(t, c2):
+            resids[t, c2] = work.tile([P, 2 * CHUNK], BF16, align_bytes=64, tag="rows", name="resid", bufs=ROW_BUFS)
+            weights = weight_all[:, 2 * CHUNK * c2 : 2 * CHUNK * (c2 + 1)]
             nc.vector.tensor_tensor(
-                out=resids[t, d][:].rearrange("p (a c q e) -> p a c q e", a=2, c=2, e=2),
-                in0=sigs[t, d][:].rearrange("p c (a q e) -> p a c q e", a=2, e=2),
+                out=resids[t, c2][:].rearrange("p (a c q e) -> p a c q e", a=2, c=2, e=2),
+                in0=sigs[t, c2][:].rearrange("p c (a q e) -> p a c q e", a=2, e=2),
                 in1=weights.rearrange("p (c q a e) -> p a c q e", c=2, a=2, e=2),
                 op=MULT,
             )
 
-        def resid_turn(t, d):
+        def resid_turn(t, c2):
             xt = psum.tile([P, 2, 2, P], F32, tag="bank", name="r_xt")
-            words = resids[t, d][:].bitcast(F32)
+            words = resids[t, c2][:].bitcast(F32)
             for a in range(2):
                 for c in range(2):
                     nc.tensor.transpose(xt[:, c, a, :], words[:, HALF * a + P * c : HALF * a + P * (c + 1)], ident[:])
-            grouped["r", t, d] = grouped_tile("r_grouped")
+            grouped["r", t, c2] = grouped_tile("r_grouped")
             nc.scalar.copy(
-                out=grouped["r", t, d][:].bitcast(F32).rearrange("p (c j a) -> p c j a", c=2, a=2),
+                out=grouped["r", t, c2][:].bitcast(F32).rearrange("p (c j a) -> p c j a", c=2, a=2),
                 in_=xt[:].rearrange("p c a j -> p c j a"),
             )
 
@@ -254,12 +267,12 @@ def tile_siglip_negative_caption_gradient_s13_kernel(
             for n, owner in enumerate(owners):
                 r_operand[owner] = (codes[:, P * n : P * (n + 1)], scales[:, P * n : P * (n + 1)])
 
-        def resid_quant(t, d):
-            quantise_resid("%d_%d" % (t, d), grouped["r", t, d][:], [(t, 2 * d), (t, 2 * d + 1)])
+        def resid_quant(t, c2):
+            quantise_resid("%d_%d" % (t, c2), grouped["r", t, c2][:], [(t, 2 * c2), (t, 2 * c2 + 1)])
 
         direct = {}
 
-        def direct_logits(k, g):
+        def direct_logits(g):
             for a in range(2):
                 acc = psum.tile([P, 2, HALF], F32, tag="bank", name="direct_sum")
                 for e in range(2):
@@ -269,55 +282,52 @@ def tile_siglip_negative_caption_gradient_s13_kernel(
                             out=acc[:, e, :],
                             lhsT=aud_codes[g][:, h, cols].bitcast(FP8X4),
                             lhsT_scale=aud_sc[g][:, h, cols],
-                            rhs=cap_codes[k][:, h, :].bitcast(FP8X4),
-                            rhs_scale=cap_sc[k][:, h, :],
+                            rhs=cap_codes[LAST_PAIR][:, h, :].bitcast(FP8X4),
+                            rhs_scale=cap_sc[LAST_PAIR][:, h, :],
                             start=(h == 0),
                             stop=(h == PASSES - 1),
                         )
-                direct["sum", k, g, a] = acc
+                direct["sum", g, a] = acc
 
-        def direct_bias(k, g):
+        def direct_bias(g):
             for a in range(2):
-                biased = work.tile([P, 2, HALF], F32, tag="biased", name="biased", bufs=4)
-                row = bias_row[:].rearrange("p (j i) -> p i j", i=2).unsqueeze(1)
+                biased = work.tile([P, 2, HALF], F32, tag="biased", name="biased", bufs=2 * (CHUNKS - FIRST_DIRECT))
+                row = bias_row[:].rearrange("q (p i) -> q i p", i=2).unsqueeze(1)
                 nc.vector.tensor_tensor(
-                    out=biased[:].rearrange("p e (i j) -> p e i j", i=2),
-                    in0=direct["sum", k, g, a][:].rearrange("p e (i j) -> p e i j", i=2),
+                    out=biased[:].rearrange("q e (i p) -> q e i p", i=2),
+                    in0=direct["sum", g, a][:].rearrange("q e (i p) -> q e i p", i=2),
                     in1=row.to_broadcast([P, 2, 2, P]),
                     op=ADD,
                 )
-                direct["biased", k, g, a] = biased
+                direct["biased", g, a] = biased
 
-        def direct_sigmoid(k, g):
-            direct["prob", k, g] = work.tile([P, 2, HALF, 2], F32, tag="prob", name="prob", bufs=2)
+        def direct_sigmoid(g):
+            direct["prob", g] = work.tile([P, 2, HALF, 2], F32, tag="prob", name="prob", bufs=CHUNKS - FIRST_DIRECT)
             for a in range(2):
                 nc.scalar.activation(
-                    out=direct["prob", k, g][:, a, :, :],
-                    in_=direct["biased", k, g, a][:].rearrange("p e j -> p j e"),
+                    out=direct["prob", g][:, a, :, :],
+                    in_=direct["biased", g, a][:].rearrange("p e j -> p j e"),
                     func=SIGMOID,
                 )
 
-        def direct_weigh(k, g):
-            grouped["direct", k, g] = grouped_tile("d_grouped")
-            weights = weight_cols[:, g, :].rearrange("p (a e) -> p a e", a=2).unsqueeze(1)
+        def direct_weigh(g):
+            grouped["direct", g] = grouped_tile("d_grouped")
+            weights = weight_cols[:, g - FIRST_DIRECT, :].rearrange("p (a e) -> p a e", a=2).unsqueeze(1)
             nc.vector.tensor_tensor(
-                out=grouped["direct", k, g][:].rearrange("p (j a e) -> p j a e", a=2, e=2),
-                in0=direct["prob", k, g][:].rearrange("p a j e -> p j a e"),
+                out=grouped["direct", g][:].rearrange("p (j a e) -> p j a e", a=2, e=2),
+                in0=direct["prob", g][:].rearrange("p a j e -> p j a e"),
                 in1=weights.to_broadcast([P, HALF, 2, 2]),
                 op=MULT,
             )
 
-        def direct_quant(k, g):
-            quantise_resid("direct_%d_%d" % (k, g), grouped["direct", k, g][:], [(2 * k, g), (2 * k + 1, g)])
+        def direct_quant(g):
+            quantise_resid("direct_%d" % g, grouped["direct", g][:], [(TURNED, g), (TURNED + 1, g)])
 
-        sums = {}
-
-        def grad_passes(t, first, end, chunks):
-            if (t, first) not in sums:
-                sums[t, first] = psum.tile([P, end - first], F32, tag="bank", name="grad_sum")
-            for g in chunks:
+        def grad(t, first, end, on_vector=False):
+            acc = psum.tile([P, end - first], F32, tag="bank", name="grad_sum")
+            for g in range(CHUNKS):
                 nc.tensor.matmul_mx(
-                    out=sums[t, first][:],
+                    out=acc[:],
                     lhsT=r_operand[t, g][0].bitcast(FP8X4),
                     lhsT_scale=r_operand[t, g][1],
                     rhs=bank[:, g, 2 * first : 2 * end].bitcast(FP4X4),
@@ -325,21 +335,15 @@ def tile_siglip_negative_caption_gradient_s13_kernel(
                     start=(g == 0),
                     stop=(g == LAST),
                 )
-
-        def store(t, first, end, on_vector=False):
             if end - first == CHUNK:
-                res = work.tile([P, CHUNK], F32, tag="res", name="res", bufs=5)
+                res = work.tile([P, CHUNK], F32, tag="res", name="res", bufs=RES_BUFS)
             else:
-                res = work.tile([P, end - first], F32, align_bytes=64, tag="resid", name="res_part", bufs=9)
+                res = work.tile([P, end - first], F32, align_bytes=64, tag="rows", name="res_part", bufs=ROW_BUFS)
             if on_vector:
-                nc.vector.tensor_copy(out=res[:], in_=sums[t, first][:])
+                nc.vector.tensor_copy(out=res[:], in_=acc[:])
             else:
-                nc.scalar.copy(out=res[:], in_=sums[t, first][:])
+                nc.scalar.copy(out=res[:], in_=acc[:])
             nc.sync.dma_start(out=tile_rows(out, t)[:, first:end], in_=res[:])
-
-        def grad(t, first, end, on_vector=False):
-            grad_passes(t, first, end, range(CHUNKS))
-            store(t, first, end, on_vector)
 
         def grads(t):
             grad(t, 0, CHUNK)
@@ -351,112 +355,118 @@ def tile_siglip_negative_caption_gradient_s13_kernel(
 
         def turn_pair(k):
             for t in (2 * k, 2 * k + 1):
-                for d in range(2):
-                    resid_turn(t, d)
+                for c2 in range(2):
+                    resid_turn(t, c2)
 
         def quant_tile(t):
-            for d in range(2):
-                resid_quant(t, d)
+            for c2 in range(2):
+                resid_quant(t, c2)
 
-        def weigh_tile(t):
-            for d in range(2):
-                weigh(t, d)
+        turned = range(TURNED)
+        last_pair = (TURNED, TURNED + 1)
+        some = TURNED // 2
 
         for h in range(PASSES):
             spread_scale(h)
         cap_turn(0)
         for first, end in ((0, HALF), (HALF, CHUNK), (CHUNK, FEATS)):
             widen(0, 0, first, end)
-        cap_turn(1)
-        aud_turn(0, 0, 0)
-        cap_turn(2)
-        aud_turn(0, 0, 1)
+        for h in range(PASSES):
+            cap_turn(1 + h)
+            aud_turn(0, 0, h)
         for h in range(PASSES):
             widen(0, 1, CHUNK * h, CHUNK * (h + 1))
         cap_turn(3)
-        cap_turn(4)
-        aud_turn(0, 1, 0)
-        cap_turn(5)
-        aud_turn(0, 1, 1)
-        cap_turn(6)
-        cap_sort(7)
+        for h in range(PASSES):
+            cap_turn(4 + h)
+            aud_turn(0, 1, h)
+        cap_turn(TURNED)
+        cap_sort(TURNED + 1)
         aud_quant(0, 0)
-        for k in range(3):
+        for k in range(LAST_PAIR):
             cap_quant(k)
-        probs(range(6), 0, 0, HALF)
+
+        probs(turned, 0, 0, HALF)
         widen(1, 0)
         aud_quant(0, 1)
-        cap_turn(7)
+        cap_turn(TURNED + 1)
         turn_half(1, 0)
-        probs(range(6), 0, HALF, CHUNK)
+        probs(turned, 0, HALF, CHUNK)
+
         widen(1, 1)
         aud_quant(1, 0)
         turn_half(1, 1)
-        probs(range(6), 1, 0, HALF)
+        probs(turned, 1, 0, HALF)
+
         widen(2, 0)
         aud_quant(1, 1)
-        cap_quant(3)
+        cap_quant(LAST_PAIR)
         turn_half(2, 0)
-        probs(range(6), 1, HALF, CHUNK)
+        probs(turned, 1, HALF, CHUNK)
+
         widen(2, 1)
         aud_quant(2, 0)
-        probs(range(6, 7), 0)
+        probs(last_pair[:1], 0)
         turn_half(2, 1)
-        probs(range(7, 8), 0)
-        probs(range(6, 8), 1)
-        widen(3, 0)
-        aud_quant(2, 1)
-        turn_half(3, 0)
-        probs(range(3), 2)
-        widen(3, 1)
-        aud_quant(3, 0)
-        turn_half(3, 1)
-        probs(range(3, 6), 2)
+        probs(last_pair[1:], 0)
+        probs(last_pair, 1)
+
+        for a in range(2):
+            widen(LAST, a)
+            aud_quant(LAST - 1 + a, 1 - a)
+            turn_half(LAST, a)
+            probs(range(some * a, some * (a + 1)), LAST - 1)
+
         weigh(0, 0)
-        aud_quant(3, 1)
+        aud_quant(LAST, 1)
         weigh(1, 0)
         weigh(2, 0)
-        probs(range(6), LAST)
+        probs(turned, LAST)
         weigh(0, 1)
         weigh(1, 1)
-        direct_logits(3, 2)
+        direct_logits(FIRST_DIRECT)
         turn_pair(0)
-        direct_logits(3, 3)
+        direct_logits(LAST)
         weigh(2, 1)
         weigh(3, 0)
         quant_tile(0)
         weigh(3, 1)
         quant_tile(1)
         grads(0)
-        direct_bias(3, 2)
+
+        direct_bias(FIRST_DIRECT)
         turn_pair(1)
-        direct_sigmoid(3, 2)
+        direct_sigmoid(FIRST_DIRECT)
         weigh(4, 0)
         grads(1)
         quant_tile(2)
         weigh(4, 1)
-        weigh_tile(5)
+        for c2 in range(2):
+            weigh(5, c2)
         grads(2)
         quant_tile(3)
-        direct_bias(3, 3)
+
+        direct_bias(LAST)
         turn_pair(2)
-        direct_sigmoid(3, 3)
+        direct_sigmoid(LAST)
         grads(3)
         quant_tile(4)
-        weigh(6, 0)
-        weigh(7, 0)
+        for t in last_pair:
+            weigh(t, 0)
         grads(4)
         quant_tile(5)
-        resid_turn(6, 0)
-        resid_turn(7, 0)
-        direct_weigh(3, 2)
-        direct_weigh(3, 3)
-        resid_quant(6, 0)
-        direct_quant(3, 2)
-        direct_quant(3, 3)
-        resid_quant(7, 0)
-        grads(5)
-        grads(6)
+
+        for t in last_pair:
+            resid_turn(t, 0)
+        for g in range(FIRST_DIRECT, CHUNKS):
+            direct_weigh(g)
+        resid_quant(last_pair[0], 0)
+        for g in range(FIRST_DIRECT, CHUNKS):
+            direct_quant(g)
+        resid_quant(last_pair[1], 0)
+        grads(TURNED - 1)
+        grads(TURNED)
+
         edges = (0, HALF, CHUNK, CHUNK + HALF, FEATS - P, FEATS)
         for n in range(len(edges) - 1):
             grad(TILES - 1, edges[n], edges[n + 1], on_vector=(n % 2 == 1))

@@ -20,6 +20,7 @@ P = 128
 CHUNK = 512
 HALF = CHUNK // 2
 CHUNKS = CLIPS // CHUNK
+HALVES = 2 * CHUNKS
 LAST = CHUNKS - 1
 PASSES = FEATS // CHUNK
 TILES = CAPS // P
@@ -30,8 +31,9 @@ FIRST_DIRECT = CHUNKS - 2
 WIDE = 4 * HALF
 
 ROW_BUFS = TILES + 1
-GROUPED_BUFS = 10
-AUDIO_BUFS = 6
+GROUPED_BUFS = 6
+CAST_BUFS = 4
+RING = 4
 SIG_BUFS = 2 * TURNED + 2
 RES_BUFS = 5
 
@@ -47,10 +49,9 @@ def tile_siglip_negative_caption_gradient_s13_kernel(
         work = ctx.enter_context(tc.tile_pool(name="work", bufs=3))
         psum = ctx.enter_context(tc.psum_pool(name="psum", bufs=8))
 
-        scale_cols = [keep.tile([P, 4], F32, name="scale_cols%d" % h) for h in range(PASSES)]
-        scale_all = keep.tile([P, FEATS], F32, name="scale_all")
-        raw_first = [keep.tile([P, 2 * FEATS], U8, name="raw_first%d" % a) for a in range(2)]
-        raw_later = [keep.tile([P, 4 * FEATS], U8, name="raw_later%d" % g) for g in range(1, CHUNKS)]
+        scale_cols = keep.tile([P, PASSES, 4], F32, name="scale_cols")
+        raw_first = [keep.tile([P, 2 * FEATS], U8, name="raw_first%d" % a) for a in range(4)]
+        raw_later = [keep.tile([P, 4 * FEATS], U8, name="raw_later%d" % g) for g in range(2, CHUNKS)]
         cap_rows = [
             work.tile([P, FEATS], BF16, align_bytes=64, tag="rows", name="cap_rows%d" % t, bufs=ROW_BUFS)
             for t in range(TILES)
@@ -61,8 +62,8 @@ def tile_siglip_negative_caption_gradient_s13_kernel(
         bank = keep.tile([P, CHUNKS, 2 * FEATS], U8, align_bytes=64, name="bank")
         bank_sc = keep.tile([P, CHUNKS, FEATS], U8, align_bytes=64, name="bank_sc")
         ident = keep.tile([P, P], F32, name="ident")
-        aud_codes = [keep.tile([P, PASSES, CHUNK], U32, align_bytes=64, name="aud_codes%d" % g) for g in range(CHUNKS)]
-        aud_sc = [keep.tile([P, PASSES, CHUNK], U8, align_bytes=64, name="aud_sc%d" % g) for g in range(CHUNKS)]
+        aud_codes = [keep.tile([P, PASSES, HALF], U32, align_bytes=64, name="aud_codes%d" % i) for i in range(HALVES)]
+        aud_sc = [keep.tile([P, PASSES, HALF], U8, align_bytes=64, name="aud_sc%d" % i) for i in range(HALVES)]
         cap_codes = [keep.tile([P, PASSES, 2 * P], U32, align_bytes=64, name="cap_codes%d" % k) for k in range(PAIRS)]
         cap_sc = [keep.tile([P, PASSES, 2 * P], U8, align_bytes=64, name="cap_sc%d" % k) for k in range(PAIRS)]
         bias_row = keep.tile([P, HALF], BF16, name="bias_row")
@@ -84,33 +85,24 @@ def tile_siglip_negative_caption_gradient_s13_kernel(
                 return matrix[: P * TURNED, :].rearrange("(p t) d -> p t d", t=TURNED)[:, t, :]
             return matrix[P * TURNED :, :].rearrange("(p i) d -> p i d", i=2)[:, t - TURNED, :]
 
-        def load_scale(h):
-            nc.sync.dma_start(
-                out=scale_cols[h][:], in_=audio_scale[0, CHUNK * h : CHUNK * (h + 1)].rearrange("(n m) -> n m", m=4)
-            )
-
         def load_cap(t):
             nc.sync.dma_start(out=cap_rows[t][:], in_=tile_rows(captions, t))
 
         def load_first_half(a):
-            nc.sync.dma_start(out=raw_first[a][:], in_=aud_view[0][:, 2 * a * FEATS : 2 * (a + 1) * FEATS])
+            nc.sync.dma_start(out=raw_first[a][:], in_=aud_view[a // 2][:, 2 * (a % 2) * FEATS : 2 * (a % 2 + 1) * FEATS])
 
         def load_chunk(g):
-            nc.sync.dma_start(out=raw_later[g - 1][:], in_=aud_view[g])
+            nc.sync.dma_start(out=raw_later[g - 2][:], in_=aud_view[g])
 
-        for h in range(PASSES):
-            load_scale(h)
-        load_cap(0)
-        load_first_half(0)
-        for t in (1, 2):
-            load_cap(t)
-        load_first_half(1)
-        for t in range(3, TURNED):
-            load_cap(t)
+        nc.sync.dma_start(out=scale_cols[:], in_=audio_scale[0, :].rearrange("(h p m) -> p h m", p=P, m=4))
+        for i in range(4):
+            load_first_half(i)
+            if i == 0:
+                load_cap(0)
+            else:
+                for t in ((1, 2, 3), (4, 5), (6, 7))[i - 1]:
+                    load_cap(t)
         nc.sync.dma_start(out=bias_cols[:], in_=bias[: P * TURNED].rearrange("(p t) -> p t", t=TURNED))
-        load_cap(TURNED)
-        load_chunk(1)
-        load_cap(TURNED + 1)
         nc.sync.dma_start(out=bias_cols_last[:], in_=bias[P * TURNED :].rearrange("(p i) -> p i", i=2))
         for g in range(2, CHUNKS):
             load_chunk(g)
@@ -131,39 +123,14 @@ def tile_siglip_negative_caption_gradient_s13_kernel(
 
         grouped = {}
 
-        def spread_scale(h):
-            xt = psum.tile([P, 4, P], F32, tag="bank", name="spread")
-            for m in range(4):
-                nc.tensor.transpose(xt[:, m, :], scale_cols[h][:, m : m + 1].to_broadcast([P, P]), ident[:])
-            pieces = 2 if h == 0 else 1
-            width = P // pieces
-            for c in range(pieces):
-                first = CHUNK * h + 4 * width * c
-                nc.scalar.copy(
-                    out=scale_all[:, first : first + 4 * width].rearrange("p (n m) -> p n m", m=4),
-                    in_=xt[:, :, width * c : width * (c + 1)].rearrange("p m n -> p n m"),
-                )
-
-        def cap_sort(t):
-            in_order = grouped_tile("cap_in_order")
-            nc.scalar.copy(
-                out=in_order[:].bitcast(F32).rearrange("p (h u n) -> p h u n", h=PASSES, u=2),
-                in_=cap_rows[t][:].bitcast(F32).rearrange("p (h n u) -> p h u n", h=PASSES, u=2),
-            )
-            grouped["sorted", t] = in_order
-
         def cap_turn(t):
             xt = psum.tile([P, PASSES, 2, P], F32, tag="bank", name="cap_xt")
             for h in range(PASSES):
                 for u in range(2):
-                    if ("sorted", t) in grouped:
-                        run = grouped["sorted", t][:].bitcast(F32)[:, HALF * h + P * u : HALF * h + P * (u + 1)]
-                    else:
-                        run = cap_rows[t][:].bitcast(F32)[:, HALF * h + u : HALF * (h + 1) : 2]
-                    nc.tensor.transpose(xt[:, h, u, :], run, ident[:])
+                    nc.tensor.transpose(xt[:, h, u, :], cap_rows[t][:].bitcast(F32)[:, HALF * h + u : HALF * (h + 1) : 2], ident[:])
             if t % 2 == 0:
                 grouped["cap", t // 2] = work.tile(
-                    [P, PASSES, 2, CHUNK], BF16, align_bytes=64, tag="cap_grouped", name="cap_grouped", bufs=PAIRS
+                    [P, PASSES, 2, CHUNK], BF16, align_bytes=64, tag="cap_grouped", name="cap_grouped", bufs=3
                 )
             nc.scalar.copy(
                 out=grouped["cap", t // 2][:, :, t % 2, :].bitcast(F32).rearrange("p h (j u) -> p h j u", u=2),
@@ -177,63 +144,84 @@ def tile_siglip_negative_caption_gradient_s13_kernel(
                 in_=grouped["cap", k][:].rearrange("p h i c -> p (h i c)"),
             )
 
-        audio = {}
+        cast_rows = {}
+        aud_banks = {}
 
-        def widen(g, a, first=0, end=FEATS):
-            for e in range(2):
-                s = 2 * a + e
-                if first == 0:
-                    audio[g, s] = work.tile([P, FEATS], BF16, align_bytes=64, tag="audio", name="audio", bufs=AUDIO_BUFS)
-                if g == 0:
-                    raw = raw_first[a][:, e * FEATS : (e + 1) * FEATS]
-                else:
-                    raw = raw_later[g - 1][:, s * FEATS : (s + 1) * FEATS]
-                nc.vector.tensor_tensor(
-                    out=audio[g, s][:, first:end], in0=raw[:, first:end].bitcast(FP8), in1=scale_all[:, first:end], op=MULT
-                )
+        def ring_tile(slot, shape, name):
+            return work.tile(shape, BF16, align_bytes=64, tag="ring%d" % (slot % RING), name=name, bufs=1)
 
-        def aud_turn(g, a, h):
-            xt = psum.tile([P, 2, 2, P], F32, tag="bank", name="aud_xt")
-            for e in range(2):
-                words = audio[g, 2 * a + e][:].bitcast(F32)
-                for u in range(2):
-                    nc.tensor.transpose(xt[:, e, u, :], words[:, HALF * h + u : HALF * (h + 1) : 2], ident[:])
-            grouped["aud", g, a, h] = grouped_tile("aud_grouped")
-            nc.scalar.copy(
-                out=grouped["aud", g, a, h][:].bitcast(F32).rearrange("p (e q u) -> p e q u", e=2, u=2),
-                in_=xt[:].rearrange("p e u q -> p e q u"),
-            )
+        def cast(i, e, engine, first=0, end=FEATS, slot=None):
+            if first == 0 and engine == "gpsimd":
+                cast_rows[i, e] = ring_tile(slot, [P, FEATS], "cast_pool")
+            elif first == 0:
+                cast_rows[i, e] = work.tile([P, FEATS], BF16, align_bytes=64, tag="cast", name="cast", bufs=CAST_BUFS)
+            if i < 4:
+                raw = raw_first[i][:, e * FEATS : (e + 1) * FEATS]
+            else:
+                s = 2 * (i % 2) + e
+                raw = raw_later[i // 2 - 2][:, s * FEATS : (s + 1) * FEATS]
+            dst = cast_rows[i, e][:].rearrange("p (u n c) -> p u n c", u=2, c=2)[:, :, first // 4 : end // 4, :]
+            src = raw[:, first:end].bitcast(FP8).rearrange("p (n u c) -> p n u c", u=2, c=2)
+            if engine == "scalar" and end - first == FEATS:
+                nc.scalar.copy(out=dst, in_=src.rearrange("p n u c -> p u n c"))
+            elif engine == "scalar":
+                nc.scalar.copy(out=dst.rearrange("p u n c -> p n u c"), in_=src)
+            else:
+                copier = nc.gpsimd if engine == "gpsimd" else nc.vector
+                copier.tensor_copy(out=dst.rearrange("p u n c -> p n u c"), in_=src)
 
-        def aud_quant(g, a):
-            cols = slice(HALF * a, HALF * (a + 1))
+        def aud_turn(i):
             for h in range(PASSES):
-                nc.vector.quantize_mx(
-                    out=aud_codes[g][:, h, cols].bitcast(FP8X4), scales=aud_sc[g][:, h, cols], in_=grouped["aud", g, a, h][:]
+                xt = psum.tile([P, 2, 2, P], F32, tag="bank", name="aud_xt")
+                for e in range(2):
+                    words = cast_rows[i, e][:].bitcast(F32)
+                    for u in range(2):
+                        nc.tensor.transpose(xt[:, u, e, :], words[:, HALF * u + P * h : HALF * u + P * (h + 1)], ident[:])
+                aud_banks[i, h] = xt
+
+        def aud_scale(i, passes=(0, 1)):
+            for h in passes:
+                if h == 0:
+                    grouped["aud", i] = ring_tile(i, [P, PASSES, WIDE], "aud_grouped")
+                scales = scale_cols[:, h, :].rearrange("p (u c) -> p u c", u=2).unsqueeze(1)
+                nc.vector.tensor_tensor(
+                    out=grouped["aud", i][:, h, :].rearrange("p (j u c) -> p j u c", u=2, c=2),
+                    in0=aud_banks[i, h][:].rearrange("p u e q -> p (u e q)").bitcast(BF16).rearrange("p (u j c) -> p j u c", u=2, c=2),
+                    in1=scales.to_broadcast([P, HALF, 2, 2]),
+                    op=MULT,
                 )
+
+        def aud_quant(i):
+            nc.vector.quantize_mx(
+                out=aud_codes[i][:].rearrange("p h j -> p (h j)").bitcast(FP8X4),
+                scales=aud_sc[i][:].rearrange("p h j -> p (h j)"),
+                in_=grouped["aud", i][:].rearrange("p h c -> p (h c)"),
+            )
 
         sigs = {}
         resids = {}
         r_operand = {}
 
-        def probs(tiles, g, first=0, end=CHUNK):
+        def probs(tiles, g, halves=(0, 1)):
             for t in tiles:
                 cols = slice(P * (t % 2), P * (t % 2 + 1))
-                acc = psum.tile([P, end - first], F32, tag="bank", name="logit_sum")
-                for h in range(PASSES):
-                    nc.tensor.matmul_mx(
-                        out=acc[:],
-                        lhsT=cap_codes[t // 2][:, h, cols].bitcast(FP8X4),
-                        lhsT_scale=cap_sc[t // 2][:, h, cols],
-                        rhs=aud_codes[g][:, h, first:end].bitcast(FP8X4),
-                        rhs_scale=aud_sc[g][:, h, first:end],
-                        start=(h == 0),
-                        stop=(h == PASSES - 1),
-                    )
+                acc = psum.tile([P, len(halves), HALF], F32, tag="bank", name="logit_sum")
+                for n, a in enumerate(halves):
+                    for h in range(PASSES):
+                        nc.tensor.matmul_mx(
+                            out=acc[:, n, :],
+                            lhsT=cap_codes[t // 2][:, h, cols].bitcast(FP8X4),
+                            lhsT_scale=cap_sc[t // 2][:, h, cols],
+                            rhs=aud_codes[2 * g + a][:, h, :].bitcast(FP8X4),
+                            rhs_scale=aud_sc[2 * g + a][:, h, :],
+                            start=(h == 0),
+                            stop=(h == PASSES - 1),
+                        )
                 if (t, g // 2) not in sigs:
                     sigs[t, g // 2] = work.tile([P, 2, CHUNK], F32, tag="sig", name="sig", bufs=SIG_BUFS)
                 nc.scalar.activation(
-                    out=sigs[t, g // 2][:, g % 2, first:end].rearrange("p (a q e) -> p a q e", q=P, e=2),
-                    in_=acc[:].rearrange("p (a e q) -> p a q e", q=P, e=2),
+                    out=sigs[t, g // 2][:, g % 2, HALF * halves[0] : HALF * (halves[-1] + 1)].rearrange("p (a q e) -> p a q e", q=P, e=2),
+                    in_=acc[:].rearrange("p a (e q) -> p a q e", e=2),
                     func=SIGMOID,
                     bias=bias_cols[:, t : t + 1] if t < TURNED else bias_cols_last[:, t - TURNED : t - TURNED + 1],
                 )
@@ -276,12 +264,12 @@ def tile_siglip_negative_caption_gradient_s13_kernel(
             for a in range(2):
                 acc = psum.tile([P, 2, HALF], F32, tag="bank", name="direct_sum")
                 for e in range(2):
-                    cols = slice(HALF * a + P * e, HALF * a + P * (e + 1))
+                    cols = slice(P * e, P * (e + 1))
                     for h in range(PASSES):
                         nc.tensor.matmul_mx(
                             out=acc[:, e, :],
-                            lhsT=aud_codes[g][:, h, cols].bitcast(FP8X4),
-                            lhsT_scale=aud_sc[g][:, h, cols],
+                            lhsT=aud_codes[2 * g + a][:, h, cols].bitcast(FP8X4),
+                            lhsT_scale=aud_sc[2 * g + a][:, h, cols],
                             rhs=cap_codes[LAST_PAIR][:, h, :].bitcast(FP8X4),
                             rhs_scale=cap_sc[LAST_PAIR][:, h, :],
                             start=(h == 0),
@@ -349,10 +337,6 @@ def tile_siglip_negative_caption_gradient_s13_kernel(
             grad(t, 0, CHUNK)
             grad(t, CHUNK, FEATS)
 
-        def turn_half(g, a):
-            for h in range(PASSES):
-                aud_turn(g, a, h)
-
         def turn_pair(k):
             for t in (2 * k, 2 * k + 1):
                 for c2 in range(2):
@@ -364,72 +348,83 @@ def tile_siglip_negative_caption_gradient_s13_kernel(
 
         turned = range(TURNED)
         last_pair = (TURNED, TURNED + 1)
-        some = TURNED // 2
 
-        for h in range(PASSES):
-            spread_scale(h)
+        cast(0, 0, "vector")
+        cast(0, 1, "scalar", 0, CHUNK)
+        cast(0, 1, "vector", CHUNK, FEATS)
+        aud_turn(0)
+        cast(1, 1, "gpsimd", slot=2)
+        cast(1, 0, "scalar")
+        aud_scale(0)
         cap_turn(0)
-        for first, end in ((0, HALF), (HALF, CHUNK), (CHUNK, FEATS)):
-            widen(0, 0, first, end)
-        for h in range(PASSES):
-            cap_turn(1 + h)
-            aud_turn(0, 0, h)
-        for h in range(PASSES):
-            widen(0, 1, CHUNK * h, CHUNK * (h + 1))
+        cap_turn(1)
+        aud_turn(1)
+        cast(2, 1, "gpsimd", slot=3)
+        cast(2, 0, "scalar")
+        aud_scale(1)
+        cap_turn(2)
         cap_turn(3)
-        for h in range(PASSES):
-            cap_turn(4 + h)
-            aud_turn(0, 1, h)
-        cap_turn(TURNED)
-        cap_sort(TURNED + 1)
-        aud_quant(0, 0)
-        for k in range(LAST_PAIR):
-            cap_quant(k)
-
-        probs(turned, 0, 0, HALF)
-        widen(1, 0)
-        aud_quant(0, 1)
-        cap_turn(TURNED + 1)
-        turn_half(1, 0)
-        probs(turned, 0, HALF, CHUNK)
-
-        widen(1, 1)
-        aud_quant(1, 0)
-        turn_half(1, 1)
-        probs(turned, 1, 0, HALF)
-
-        widen(2, 0)
-        aud_quant(1, 1)
-        cap_quant(LAST_PAIR)
-        turn_half(2, 0)
-        probs(turned, 1, HALF, CHUNK)
-
-        widen(2, 1)
-        aud_quant(2, 0)
-        probs(last_pair[:1], 0)
-        turn_half(2, 1)
-        probs(last_pair[1:], 0)
-        probs(last_pair, 1)
-
-        for a in range(2):
-            widen(LAST, a)
-            aud_quant(LAST - 1 + a, 1 - a)
-            turn_half(LAST, a)
-            probs(range(some * a, some * (a + 1)), LAST - 1)
-
+        cast(3, 0, "scalar")
+        cap_quant(0)
+        aud_quant(0)
+        cap_turn(4)
+        cap_turn(5)
+        aud_turn(2)
+        cap_quant(1)
+        aud_quant(1)
+        cast(3, 1, "gpsimd", slot=1)
+        cap_turn(6)
+        cap_turn(7)
+        cast(4, 0, "scalar")
+        aud_scale(2)
+        probs(range(2), 0)
+        cap_quant(2)
+        aud_quant(2)
+        cast(4, 1, "gpsimd", slot=2)
+        aud_turn(3)
+        cast(5, 0, "scalar")
+        aud_scale(3)
+        probs((2, 3, 4, 5), 0)
+        cast(5, 1, "scalar")
+        cap_quant(3)
+        aud_quant(3)
+        cast(6, 1, "gpsimd", slot=3)
+        aud_turn(4)
+        aud_scale(4)
+        probs((6, 7), 0)
+        cast(6, 0, "scalar")
+        probs((0,), 1)
+        aud_turn(5)
+        aud_scale(5, (0,))
+        aud_quant(4)
+        cast(7, 1, "gpsimd", slot=0)
+        aud_scale(5, (1,))
+        probs((1, 2), 1)
+        cast(7, 0, "scalar")
+        probs((3, 4), 1)
+        aud_turn(6)
+        aud_scale(6, (0,))
+        aud_quant(5)
+        aud_scale(6, (1,))
+        probs((5, 6, 7), 1)
+        aud_turn(7)
+        aud_scale(7, (0,))
+        aud_quant(6)
+        aud_scale(7, (1,))
+        probs(turned, 2)
+        direct_logits(FIRST_DIRECT)
         weigh(0, 0)
-        aud_quant(LAST, 1)
+        aud_quant(7)
         weigh(1, 0)
-        weigh(2, 0)
         probs(turned, LAST)
+        weigh(2, 0)
         weigh(0, 1)
         weigh(1, 1)
-        direct_logits(FIRST_DIRECT)
         turn_pair(0)
         direct_logits(LAST)
         weigh(2, 1)
-        weigh(3, 0)
         quant_tile(0)
+        weigh(3, 0)
         weigh(3, 1)
         quant_tile(1)
         grads(0)

from contextlib import ExitStack

import concourse.mybir as mybir
from concourse.masks import make_identity

F32 = mybir.dt.float32
BF16 = mybir.dt.bfloat16
U32 = mybir.dt.uint32
I32 = mybir.dt.int32
U8 = mybir.dt.uint8
FP8 = mybir.dt.float8_e4m3fn
FP8X4 = mybir.dt.float8_e4m3fn_x4
FP4X4 = mybir.dt.float4_e2m1fn_x4
MULT = mybir.AluOpType.mult
ADD = mybir.AluOpType.add
SIGMOID = mybir.ActivationFunctionType.Sigmoid

CLIPS, CAPS, FEATS = 2048, 1024, 1024
P = 128
CHUNK = 512
HALF = CHUNK // 2
CHUNKS = CLIPS // CHUNK
HALVES = 2 * CHUNKS
LAST = CHUNKS - 1
PASSES = FEATS // CHUNK
TILES = CAPS // P
PAIRS = TILES // 2
LAST_PAIR = PAIRS - 1
TURNED = 2 * LAST_PAIR
FIRST_DIRECT = CHUNKS - 2
WIDE = 4 * HALF

ROW_BUFS = TILES + 1
GROUPED_BUFS = 6
CAST_BUFS = 4
RING = 4
SIG_BUFS = 2 * TURNED + 2
RES_BUFS = 5

FLOPS = 2 * 2 * CLIPS * CAPS * FEATS


def tile_siglip_negative_caption_gradient_s13_kernel(
    tc, audio_bytes, audio_scale, captions, bias, clip_weight, bank_words, bank_scales, out
):
    nc = tc.nc
    with ExitStack() as ctx:
        keep = ctx.enter_context(tc.tile_pool(name="keep", bufs=1))
        work = ctx.enter_context(tc.tile_pool(name="work", bufs=3))
        psum = ctx.enter_context(tc.psum_pool(name="psum", bufs=8))

        scale_cols = keep.tile([P, PASSES, 4], F32, name="scale_cols")
        raw_first = [keep.tile([P, 2 * FEATS], U8, name="raw_first%d" % a) for a in range(4)]
        raw_later = [keep.tile([P, 4 * FEATS], U8, name="raw_later%d" % g) for g in range(2, CHUNKS)]
        cap_rows = [
            work.tile([P, FEATS], BF16, align_bytes=64, tag="rows", name="cap_rows%d" % t, bufs=ROW_BUFS)
            for t in range(TILES)
        ]
        weight_all = keep.tile([P, CLIPS], BF16, name="weight_all")
        bias_cols = keep.tile([P, TURNED], BF16, name="bias_cols")
        bias_cols_last = keep.tile([P, 2], BF16, name="bias_cols_last")
        bank = keep.tile([P, CHUNKS, 2 * FEATS], U8, align_bytes=64, name="bank")
        bank_sc = keep.tile([P, CHUNKS, FEATS], U8, align_bytes=64, name="bank_sc")
        ident = keep.tile([P, P], F32, name="ident")
        aud_codes = [keep.tile([P, PASSES, HALF], U32, align_bytes=64, name="aud_codes%d" % i) for i in range(HALVES)]
        aud_sc = [keep.tile([P, PASSES, HALF], U8, align_bytes=64, name="aud_sc%d" % i) for i in range(HALVES)]
        cap_codes = [keep.tile([P, PASSES, 2 * P], U32, align_bytes=64, name="cap_codes%d" % k) for k in range(PAIRS)]
        cap_sc = [keep.tile([P, PASSES, 2 * P], U8, align_bytes=64, name="cap_sc%d" % k) for k in range(PAIRS)]
        bias_row = keep.tile([P, HALF], BF16, name="bias_row")
        weight_cols = keep.tile([P, CHUNKS - FIRST_DIRECT, 4], BF16, name="weight_cols")

        ctx.enter_context(tc.manual_schedule())

        table = keep.tile([P, 1], F32, name="table")
        nc.vector.memset(table[:], 0.0)
        nc.scalar.activation(out=table[:], in_=table[:], func=SIGMOID)

        make_identity(nc, ident[:])
        nc.gpsimd.memset(bank_sc[:].rearrange("p g d -> p (g d)").bitcast(U32), 0)

        aud_view = audio_bytes.rearrange("(g q s) d -> g q (s d)", q=P, s=4)

        def tile_rows(matrix, t):
            if t < TURNED:
                return matrix[: P * TURNED, :].rearrange("(p t) d -> p t d", t=TURNED)[:, t, :]
            return matrix[P * TURNED :, :].rearrange("(p i) d -> p i d", i=2)[:, t - TURNED, :]

        def load_cap(t):
            nc.sync.dma_start(out=cap_rows[t][:], in_=tile_rows(captions, t))

        def load_first_half(a):
            nc.sync.dma_start(out=raw_first[a][:], in_=aud_view[a // 2][:, 2 * (a % 2) * FEATS : 2 * (a % 2 + 1) * FEATS])

        def load_chunk(g):
            nc.sync.dma_start(out=raw_later[g - 2][:], in_=aud_view[g])

        nc.sync.dma_start(out=scale_cols[:], in_=audio_scale[0, :].rearrange("(h p m) -> p h m", p=P, m=4))
        for i in range(4):
            load_first_half(i)
            if i == 0:
                load_cap(0)
            else:
                for t in ((1, 2, 3), (4, 5), (6, 7))[i - 1]:
                    load_cap(t)
        nc.sync.dma_start(out=bias_cols[:], in_=bias[: P * TURNED].rearrange("(p t) -> p t", t=TURNED))
        nc.sync.dma_start(out=bias_cols_last[:], in_=bias[P * TURNED :].rearrange("(p i) -> p i", i=2))
        for g in range(2, CHUNKS):
            load_chunk(g)
        nc.sync.dma_start(out=weight_all[:], in_=clip_weight.partition_broadcast(P))
        nc.sync.dma_start(out=bias_row[:], in_=bias[P * TURNED :].partition_broadcast(P))
        nc.sync.dma_start(out=bank[:], in_=bank_words.rearrange("g p n -> p g n"))
        for n in range(4):
            nc.sync.dma_start(
                out=bank_sc[32 * n : 32 * n + 4, :, :].bitcast(I32),
                in_=bank_scales[:, 4 * n : 4 * n + 4, :].rearrange("g b d -> b g d").bitcast(I32),
            )
        nc.sync.dma_start(
            out=weight_cols[:], in_=clip_weight[CHUNK * FIRST_DIRECT :].rearrange("(g q s) -> q g s", q=P, s=4)
        )

        def grouped_tile(name):
            return work.tile([P, WIDE], BF16, align_bytes=64, tag="grouped", name=name, bufs=GROUPED_BUFS)

        grouped = {}

        def cap_turn(t):
            xt = psum.tile([P, PASSES, 2, P], F32, tag="bank", name="cap_xt")
            for h in range(PASSES):
                for u in range(2):
                    nc.tensor.transpose(xt[:, h, u, :], cap_rows[t][:].bitcast(F32)[:, HALF * h + u : HALF * (h + 1) : 2], ident[:])
            if t % 2 == 0:
                grouped["cap", t // 2] = work.tile(
                    [P, PASSES, 2, CHUNK], BF16, align_bytes=64, tag="cap_grouped", name="cap_grouped", bufs=3
                )
            nc.scalar.copy(
                out=grouped["cap", t // 2][:, :, t % 2, :].bitcast(F32).rearrange("p h (j u) -> p h j u", u=2),
                in_=xt[:].rearrange("p h u j -> p h j u"),
            )

        def cap_quant(k):
            nc.vector.quantize_mx(
                out=cap_codes[k][:].rearrange("p h j -> p (h j)").bitcast(FP8X4),
                scales=cap_sc[k][:].rearrange("p h j -> p (h j)"),
                in_=grouped["cap", k][:].rearrange("p h i c -> p (h i c)"),
            )

        cast_rows = {}
        aud_banks = {}

        def ring_tile(slot, shape, name):
            return work.tile(shape, BF16, align_bytes=64, tag="ring%d" % (slot % RING), name=name, bufs=1)

        def cast(i, e, engine, first=0, end=FEATS, slot=None):
            if first == 0 and engine == "gpsimd":
                cast_rows[i, e] = ring_tile(slot, [P, FEATS], "cast_pool")
            elif first == 0:
                cast_rows[i, e] = work.tile([P, FEATS], BF16, align_bytes=64, tag="cast", name="cast", bufs=CAST_BUFS)
            if i < 4:
                raw = raw_first[i][:, e * FEATS : (e + 1) * FEATS]
            else:
                s = 2 * (i % 2) + e
                raw = raw_later[i // 2 - 2][:, s * FEATS : (s + 1) * FEATS]
            dst = cast_rows[i, e][:].rearrange("p (u n c) -> p u n c", u=2, c=2)[:, :, first // 4 : end // 4, :]
            src = raw[:, first:end].bitcast(FP8).rearrange("p (n u c) -> p n u c", u=2, c=2)
            if engine == "scalar" and end - first == FEATS:
                nc.scalar.copy(out=dst, in_=src.rearrange("p n u c -> p u n c"))
            elif engine == "scalar":
                nc.scalar.copy(out=dst.rearrange("p u n c -> p n u c"), in_=src)
            else:
                copier = nc.gpsimd if engine == "gpsimd" else nc.vector
                copier.tensor_copy(out=dst.rearrange("p u n c -> p n u c"), in_=src)

        def aud_turn(i):
            for h in range(PASSES):
                xt = psum.tile([P, 2, 2, P], F32, tag="bank", name="aud_xt")
                for e in range(2):
                    words = cast_rows[i, e][:].bitcast(F32)
                    for u in range(2):
                        nc.tensor.transpose(xt[:, u, e, :], words[:, HALF * u + P * h : HALF * u + P * (h + 1)], ident[:])
                aud_banks[i, h] = xt

        def aud_scale(i, passes=(0, 1)):
            for h in passes:
                if h == 0:
                    grouped["aud", i] = ring_tile(i, [P, PASSES, WIDE], "aud_grouped")
                scales = scale_cols[:, h, :].rearrange("p (u c) -> p u c", u=2).unsqueeze(1)
                nc.vector.tensor_tensor(
                    out=grouped["aud", i][:, h, :].rearrange("p (j u c) -> p j u c", u=2, c=2),
                    in0=aud_banks[i, h][:].rearrange("p u e q -> p (u e q)").bitcast(BF16).rearrange("p (u j c) -> p j u c", u=2, c=2),
                    in1=scales.to_broadcast([P, HALF, 2, 2]),
                    op=MULT,
                )

        def aud_quant(i):
            nc.vector.quantize_mx(
                out=aud_codes[i][:].rearrange("p h j -> p (h j)").bitcast(FP8X4),
                scales=aud_sc[i][:].rearrange("p h j -> p (h j)"),
                in_=grouped["aud", i][:].rearrange("p h c -> p (h c)"),
            )

        sigs = {}
        resids = {}
        r_operand = {}

        def probs(tiles, g, halves=(0, 1)):
            for t in tiles:
                cols = slice(P * (t % 2), P * (t % 2 + 1))
                acc = psum.tile([P, len(halves), HALF], F32, tag="bank", name="logit_sum")
                for n, a in enumerate(halves):
                    for h in range(PASSES):
                        nc.tensor.matmul_mx(
                            out=acc[:, n, :],
                            lhsT=cap_codes[t // 2][:, h, cols].bitcast(FP8X4),
                            lhsT_scale=cap_sc[t // 2][:, h, cols],
                            rhs=aud_codes[2 * g + a][:, h, :].bitcast(FP8X4),
                            rhs_scale=aud_sc[2 * g + a][:, h, :],
                            start=(h == 0),
                            stop=(h == PASSES - 1),
                        )
                if (t, g // 2) not in sigs:
                    sigs[t, g // 2] = work.tile([P, 2, CHUNK], F32, tag="sig", name="sig", bufs=SIG_BUFS)
                nc.scalar.activation(
                    out=sigs[t, g // 2][:, g % 2, HALF * halves[0] : HALF * (halves[-1] + 1)].rearrange("p (a q e) -> p a q e", q=P, e=2),
                    in_=acc[:].rearrange("p a (e q) -> p a q e", e=2),
                    func=SIGMOID,
                    bias=bias_cols[:, t : t + 1] if t < TURNED else bias_cols_last[:, t - TURNED : t - TURNED + 1],
                )

        def weigh(t, c2):
            resids[t, c2] = work.tile([P, 2 * CHUNK], BF16, align_bytes=64, tag="rows", name="resid", bufs=ROW_BUFS)
            weights = weight_all[:, 2 * CHUNK * c2 : 2 * CHUNK * (c2 + 1)]
            nc.vector.tensor_tensor(
                out=resids[t, c2][:].rearrange("p (a c q e) -> p a c q e", a=2, c=2, e=2),
                in0=sigs[t, c2][:].rearrange("p c (a q e) -> p a c q e", a=2, e=2),
                in1=weights.rearrange("p (c q a e) -> p a c q e", c=2, a=2, e=2),
                op=MULT,
            )

        def resid_turn(t, c2):
            xt = psum.tile([P, 2, 2, P], F32, tag="bank", name="r_xt")
            words = resids[t, c2][:].bitcast(F32)
            for a in range(2):
                for c in range(2):
                    nc.tensor.transpose(xt[:, c, a, :], words[:, HALF * a + P * c : HALF * a + P * (c + 1)], ident[:])
            grouped["r", t, c2] = grouped_tile("r_grouped")
            nc.scalar.copy(
                out=grouped["r", t, c2][:].bitcast(F32).rearrange("p (c j a) -> p c j a", c=2, a=2),
                in_=xt[:].rearrange("p c a j -> p c j a"),
            )

        def quantise_resid(name, src, owners):
            codes = keep.tile([P, 2 * P], U32, align_bytes=64, name="r_codes_" + name)
            scales = keep.tile([P, 2 * P], U8, align_bytes=64, name="r_sc_" + name)
            nc.vector.quantize_mx(out=codes[:].bitcast(FP8X4), scales=scales[:], in_=src)
            for n, owner in enumerate(owners):
                r_operand[owner] = (codes[:, P * n : P * (n + 1)], scales[:, P * n : P * (n + 1)])

        def resid_quant(t, c2):
            quantise_resid("%d_%d" % (t, c2), grouped["r", t, c2][:], [(t, 2 * c2), (t, 2 * c2 + 1)])

        direct = {}

        def direct_logits(g):
            for a in range(2):
                acc = psum.tile([P, 2, HALF], F32, tag="bank", name="direct_sum")
                for e in range(2):
                    cols = slice(P * e, P * (e + 1))
                    for h in range(PASSES):
                        nc.tensor.matmul_mx(
                            out=acc[:, e, :],
                            lhsT=aud_codes[2 * g + a][:, h, cols].bitcast(FP8X4),
                            lhsT_scale=aud_sc[2 * g + a][:, h, cols],
                            rhs=cap_codes[LAST_PAIR][:, h, :].bitcast(FP8X4),
                            rhs_scale=cap_sc[LAST_PAIR][:, h, :],
                            start=(h == 0),
                            stop=(h == PASSES - 1),
                        )
                direct["sum", g, a] = acc

        def direct_bias(g):
            for a in range(2):
                biased = work.tile([P, 2, HALF], F32, tag="biased", name="biased", bufs=2 * (CHUNKS - FIRST_DIRECT))
                row = bias_row[:].rearrange("q (p i) -> q i p", i=2).unsqueeze(1)
                nc.vector.tensor_tensor(
                    out=biased[:].rearrange("q e (i p) -> q e i p", i=2),
                    in0=direct["sum", g, a][:].rearrange("q e (i p) -> q e i p", i=2),
                    in1=row.to_broadcast([P, 2, 2, P]),
                    op=ADD,
                )
                direct["biased", g, a] = biased

        def direct_sigmoid(g):
            direct["prob", g] = work.tile([P, 2, HALF, 2], F32, tag="prob", name="prob", bufs=CHUNKS - FIRST_DIRECT)
            for a in range(2):
                nc.scalar.activation(
                    out=direct["prob", g][:, a, :, :],
                    in_=direct["biased", g, a][:].rearrange("p e j -> p j e"),
                    func=SIGMOID,
                )

        def direct_weigh(g):
            grouped["direct", g] = grouped_tile("d_grouped")
            weights = weight_cols[:, g - FIRST_DIRECT, :].rearrange("p (a e) -> p a e", a=2).unsqueeze(1)
            nc.vector.tensor_tensor(
                out=grouped["direct", g][:].rearrange("p (j a e) -> p j a e", a=2, e=2),
                in0=direct["prob", g][:].rearrange("p a j e -> p j a e"),
                in1=weights.to_broadcast([P, HALF, 2, 2]),
                op=MULT,
            )

        def direct_quant(g):
            quantise_resid("direct_%d" % g, grouped["direct", g][:], [(TURNED, g), (TURNED + 1, g)])

        def grad(t, first, end, on_vector=False):
            acc = psum.tile([P, end - first], F32, tag="bank", name="grad_sum")
            for g in range(CHUNKS):
                nc.tensor.matmul_mx(
                    out=acc[:],
                    lhsT=r_operand[t, g][0].bitcast(FP8X4),
                    lhsT_scale=r_operand[t, g][1],
                    rhs=bank[:, g, 2 * first : 2 * end].bitcast(FP4X4),
                    rhs_scale=bank_sc[:, g, first:end],
                    start=(g == 0),
                    stop=(g == LAST),
                )
            if end - first == CHUNK:
                res = work.tile([P, CHUNK], F32, tag="res", name="res", bufs=RES_BUFS)
            else:
                res = work.tile([P, end - first], F32, align_bytes=64, tag="rows", name="res_part", bufs=ROW_BUFS)
            if on_vector:
                nc.vector.tensor_copy(out=res[:], in_=acc[:])
            else:
                nc.scalar.copy(out=res[:], in_=acc[:])
            nc.sync.dma_start(out=tile_rows(out, t)[:, first:end], in_=res[:])

        def grads(t):
            grad(t, 0, CHUNK)
            grad(t, CHUNK, FEATS)

        def turn_pair(k):
            for t in (2 * k, 2 * k + 1):
                for c2 in range(2):
                    resid_turn(t, c2)

        def quant_tile(t):
            for c2 in range(2):
                resid_quant(t, c2)

        turned = range(TURNED)
        last_pair = (TURNED, TURNED + 1)

        cast(0, 0, "vector")
        cast(0, 1, "scalar", 0, CHUNK)
        cast(0, 1, "vector", CHUNK, FEATS)
        aud_turn(0)
        cast(1, 1, "gpsimd", slot=2)
        cast(1, 0, "scalar")
        aud_scale(0)
        cap_turn(0)
        cap_turn(1)
        aud_turn(1)
        cast(2, 1, "gpsimd", slot=3)
        cast(2, 0, "scalar")
        aud_scale(1)
        cap_turn(2)
        cap_turn(3)
        cast(3, 0, "scalar")
        cap_quant(0)
        aud_quant(0)
        cap_turn(4)
        cap_turn(5)
        aud_turn(2)
        cap_quant(1)
        aud_quant(1)
        cast(3, 1, "gpsimd", slot=1)
        cap_turn(6)
        cap_turn(7)
        cast(4, 0, "scalar")
        aud_scale(2)
        probs(range(2), 0)
        cap_quant(2)
        aud_quant(2)
        cast(4, 1, "gpsimd", slot=2)
        aud_turn(3)
        cast(5, 0, "scalar")
        aud_scale(3)
        probs((2, 3, 4, 5), 0)
        cast(5, 1, "scalar")
        cap_quant(3)
        aud_quant(3)
        cast(6, 1, "gpsimd", slot=3)
        aud_turn(4)
        aud_scale(4)
        probs((6, 7), 0)
        cast(6, 0, "scalar")
        probs((0,), 1)
        aud_turn(5)
        aud_scale(5, (0,))
        aud_quant(4)
        cast(7, 1, "gpsimd", slot=0)
        aud_scale(5, (1,))
        probs((1, 2), 1)
        cast(7, 0, "scalar")
        probs((3, 4), 1)
        aud_turn(6)
        aud_scale(6, (0,))
        aud_quant(5)
        aud_scale(6, (1,))
        probs((5, 6, 7), 1)
        aud_turn(7)
        aud_scale(7, (0,))
        aud_quant(6)
        aud_scale(7, (1,))
        probs(turned, 2)
        direct_logits(FIRST_DIRECT)
        weigh(0, 0)
        aud_quant(7)
        weigh(1, 0)
        probs(turned, LAST)
        weigh(2, 0)
        weigh(0, 1)
        weigh(1, 1)
        turn_pair(0)
        direct_logits(LAST)
        weigh(2, 1)
        quant_tile(0)
        weigh(3, 0)
        weigh(3, 1)
        quant_tile(1)
        grads(0)

        direct_bias(FIRST_DIRECT)
        turn_pair(1)
        direct_sigmoid(FIRST_DIRECT)
        weigh(4, 0)
        grads(1)
        quant_tile(2)
        weigh(4, 1)
        for c2 in range(2):
            weigh(5, c2)
        grads(2)
        quant_tile(3)

        direct_bias(LAST)
        turn_pair(2)
        direct_sigmoid(LAST)
        grads(3)
        quant_tile(4)
        for t in last_pair:
            weigh(t, 0)
        grads(4)
        quant_tile(5)

        for t in last_pair:
            resid_turn(t, 0)
        for g in range(FIRST_DIRECT, CHUNKS):
            direct_weigh(g)
        resid_quant(last_pair[0], 0)
        for g in range(FIRST_DIRECT, CHUNKS):
            direct_quant(g)
        resid_quant(last_pair[1], 0)
        grads(TURNED - 1)
        grads(TURNED)

        edges = (0, HALF, CHUNK, CHUNK + HALF, FEATS - P, FEATS)
        for n in range(len(edges) - 1):
            grad(TILES - 1, edges[n], edges[n + 1], on_vector=(n % 2 == 1))
